import numpy as np
import ml_dtypes


def mxq(x, axis, fmt="e4m3"):
    dtype, down = {"e4m3": (ml_dtypes.float8_e4m3fn, 7), "e5m2": (ml_dtypes.float8_e5m2, 14)}[fmt]
    v = np.moveaxis(np.asarray(x, np.float32).astype(ml_dtypes.bfloat16).astype(np.float64), axis, -1)
    blocks = v.reshape(v.shape[:-1] + (-1, 32))
    amax = np.abs(blocks).max(-1, keepdims=True)
    byte = np.maximum(np.where(amax > 0, np.frexp(amax)[1] - 1 + 127, 0) - down, 1)
    scale = np.exp2(byte - 127.0)
    codes = (blocks / scale).astype(np.float32).astype(dtype).astype(np.float64)
    return np.moveaxis((codes * scale).reshape(v.shape), -1, axis)


WIDE = False


def mx_kscale(k):
    if not WIDE:
        return np.ones(k)
    levels = np.array([18, -18])
    if k % 512:
        return np.exp2(np.random.permutation(np.resize(levels, k // 32))).repeat(32)
    a = np.empty((k // 512, 16))
    for p in range(k // 512):
        a[p, :8] = np.random.permutation(np.resize(levels, 8))
        for g in range(8):
            far = levels[np.abs(levels - a[p, g]) >= 10]
            a[p, g + 8] = far[np.random.randint(len(far))]
    return np.exp2(a.ravel()).repeat(32)


def f64(x):
    return np.asarray(x).astype(np.float64)


def striped(idx):
    return np.tile(np.asarray(idx).reshape(-1, 16).T, (8, 1)).astype(np.uint16)


def unstriped(offs):
    return offs[:16].T.reshape(-1).astype(np.int64)


B, N, T, D, R = 1, 512, 2048, 512, 1024


def setup_inputs():
    n = np.random.standard_normal
    idx = np.random.permutation(T)[:B * N]
    s = mx_kscale(D)[:, None]
    u = np.ones(T)
    u[idx] = mx_kscale(B * N)
    r = np.random.uniform(0.5, 2.0, T) * u
    x = n((B, D, R))
    return {
        "xT": (x * s).astype(np.float32),
        "wT": (n((D, T)) * (1.00 / np.sqrt(D)) / s / r).astype(np.float32),
        "y": (2 * np.random.randint(0, 2, (B, R, N)) - 1).astype(np.float32),
        "wt": (np.random.uniform(0.5, 1.5, (B, R, 1)) * 1.0 / np.sqrt(R)).astype(np.float32),
        "ts": np.tile(r, (128, 1)).astype(np.float32),
        "offs": striped(idx),
    }


def reference(xT, wT, y, wt, ts, offs):
    idx = unstriped(offs)
    pick = lambda x: x[:, idx].reshape(x.shape[0], B, N).transpose(1, 0, 2)
    w = pick(f64(wT))
    a = mxq(f64(xT), 1, "e4m3").transpose(0, 2, 1) @ mxq(w, 1, "e4m3")
    ts_ = pick(f64(ts))[:, :1, :]
    a = a * ts_
    g = -f64(wt) * f64(y) * np.maximum(1.0 - f64(y) * a, 0.0)
    g = g * ts_
    gx = mxq(g, 2, "e5m2") @ mxq(w, 2, "e4m3").transpose(0, 2, 1)
    return gx

@@ -1,0 +1,233 @@
+from contextlib import ExitStack
+
+import concourse.mybir as mybir
+from concourse.masks import make_identity
+
+D, T, N, R = 512, 2048, 512, 1024
+P = 128
+PACK = 4
+BLOCKS = R // P
+X_CHUNKS = [(0, 256), (256, 512), (512, 1024)]
+Y_ROWS = 256
+
+FLOPS = 2 * 2 * R * N * D
+BYTES = 4 * (D * R + D * T + R * N + R + T + R * D) + 2 * P * (N // 16)
+
+F32 = mybir.dt.float32
+BF16 = mybir.dt.bfloat16
+U32 = mybir.dt.uint32
+U16 = mybir.dt.uint16
+U8 = mybir.dt.uint8
+E4M3 = mybir.dt.float8_e4m3fn_x4
+E5M2 = mybir.dt.float8_e5m2_x4
+MULT = mybir.AluOpType.mult
+ACT = mybir.ActivationFunctionType
+
+
+def tile_attend_gsqh_x_ts_kernel(tc, xT, wT, y, wt, ts, offs, out):
+    nc = tc.nc
+    with ExitStack() as ctx:
+        keep = ctx.enter_context(tc.tile_pool(name="keep", bufs=1))
+        work = ctx.enter_context(tc.tile_pool(name="work", bufs=BLOCKS))
+        psum = ctx.enter_context(tc.psum_pool(name="psum", bufs=1))
+
+        offsets = keep.tile([P, N // 16], U16, name="offsets")
+        nc.sync.dma_start(offsets[:], offs)
+
+        wt_rows = keep.tile([P, P], F32, name="wt_rows")
+        nc.sync.dma_start(wt_rows[P - BLOCKS : P, :], wt[0].rearrange("(b p) o -> b (p o)", p=P))
+        ts_window = keep.tile([P, T], F32, name="ts_window")
+        nc.sync.dma_start(ts_window[P - 1 : P, :], ts[0:1, :])
+        nc.vector.memset(wt_rows[0 : P - BLOCKS, :], 0.0)
+        nc.vector.memset(ts_window[0 : P - 1, :], 0.0)
+
+        w_rows = wT.rearrange("(p t) c -> p t c", t=PACK)
+        w_planes = []
+        for t in range(PACK):
+            plane = keep.tile([P, T], F32, name="w_plane%d" % t)
+            nc.sync.dma_start(plane[:], w_rows[:, t, :])
+            w_planes.append(plane)
+
+        x_rows = xT[0].rearrange("(p t) r -> p t r", t=PACK)
+        y_rows = y[0].rearrange("(k j p) i -> k p j i", p=P, j=Y_ROWS // P)
+        x_raw = {}
+        y_raw = {}
+
+        def load_x(k):
+            lo, hi = X_CHUNKS[k]
+            raw = keep.tile([P, PACK, hi - lo], F32, name="x_raw%d" % k)
+            nc.sync.dma_start(raw[:], x_rows[:, :, lo:hi])
+            for b in range(lo // P, hi // P):
+                x_raw[b] = raw[:, :, b * P - lo : (b + 1) * P - lo]
+
+        def load_y(k):
+            raw = keep.tile([P, Y_ROWS // P, N], F32, name="y_raw%d" % k)
+            nc.sync.dma_start(raw[:], y_rows[k])
+            for j in range(Y_ROWS // P):
+                y_raw[k * (Y_ROWS // P) + j] = raw[:, j, :]
+
+        load_x(0)
+        load_y(0)
+        load_x(1)
+        load_y(1)
+        load_x(2)
+        load_y(2)
+        load_y(3)
+
+        ident_f32 = keep.tile([P, P], F32, name="ident_f32")
+        make_identity(nc, ident_f32[:])
+        ident_bf16 = keep.tile([P, P], BF16, name="ident_bf16")
+        make_identity(nc, ident_bf16[:])
+
+        wt_turned = psum.tile([P, P], F32, name="wt_turned", tag="turn", bufs=2)
+        nc.tensor.transpose(wt_turned[:], wt_rows[:], ident_f32[:])
+        neg_wt = keep.tile([P, BLOCKS], F32, name="neg_wt")
+        nc.scalar.activation(neg_wt[:], wt_turned[:, P - BLOCKS : P], ACT.Copy, scale=-1.0)
+
+        ts_listed = keep.tile([P, N], F32, name="ts_listed")
+        nc.vector.tensor_copy(ts_listed[:], ts_window[:].indirect(offsets[:]))
+        ts_turned = psum.tile([P, PACK, P], F32, name="ts_turned", tag="turn", bufs=2)
+        for q in range(PACK):
+            nc.tensor.transpose(ts_turned[:, q, :], ts_listed[:, q * P : (q + 1) * P], ident_f32[:])
+        ts_cols = keep.tile([P, PACK], F32, name="ts_cols")
+        nc.scalar.copy(ts_cols[:], ts_turned[:, :, P - 1])
+        ts_spread = psum.tile([P, N], F32, name="ts_spread")
+        for q in range(PACK):
+            nc.tensor.transpose(
+                ts_spread[:, q * P : (q + 1) * P],
+                ts_cols[:, q : q + 1].to_broadcast([P, P]),
+                ident_f32[:],
+            )
+
+        w_by_d = keep.tile([P, N, PACK], BF16, name="w_by_d", align_bytes=64)
+        w_by_slot = keep.tile([P, PACK, P, PACK], BF16, name="w_by_slot", align_bytes=64)
+        w_quads = w_by_d[:].rearrange("p (s j) t -> p j t s", j=PACK)
+        for t in range(PACK):
+            nc.vector.tensor_copy(w_by_d[:, :, t], w_planes[t][:].indirect(offsets[:]))
+            w_turned = psum.tile([P, PACK, P], BF16, name="w_turned", tag="result", bufs=3)
+            for j in range(PACK):
+                nc.tensor.transpose(w_turned[:, j, :], w_quads[:, j, t, :], ident_bf16[:])
+            nc.scalar.copy(w_by_slot[:, t, :, :], w_turned[:].rearrange("s j p -> s p j"))
+
+        w1_codes = keep.tile([P, N], U32, name="w1_codes", align_bytes=64)
+        w1_scales = keep.tile([P, N], U8, name="w1_scales", align_bytes=64)
+        nc.vector.quantize_mx(
+            out=w1_codes[:].bitcast(E4M3),
+            scales=w1_scales[:],
+            in_=w_by_d[:].rearrange("p i t -> p (i t)"),
+        )
+
+        x_grouped = keep.tile([P, R, PACK], BF16, name="x_grouped", align_bytes=64)
+        x_codes = keep.tile([P, R], U32, name="x_codes", align_bytes=64)
+        x_scales = keep.tile([P, R], U8, name="x_scales", align_bytes=64)
+        w2_codes = keep.tile([P, D], U32, name="w2_codes", align_bytes=64)
+        w2_scales = keep.tile([P, D], U8, name="w2_scales", align_bytes=64)
+
+        def group_x(b):
+            rows = slice(b * P, (b + 1) * P)
+            nc.scalar.copy(
+                x_grouped[:, rows, :].rearrange("p (c i) t -> p c t i", i=PACK),
+                x_raw[b].rearrange("p t (c i) -> p c t i", i=PACK),
+            )
+
+        def quantize_x(b, count):
+            rows = slice(b * P, (b + count) * P)
+            nc.vector.quantize_mx(
+                out=x_codes[:, rows].bitcast(E4M3),
+                scales=x_scales[:, rows],
+                in_=x_grouped[:, rows, :].rearrange("p r t -> p (r t)"),
+            )
+
+        signed = {}
+        sums = {}
+        slack = {}
+        h_grouped = {}
+
+        def sign_scales(b):
+            signed[b] = work.tile([P, N], F32, name="signed")
+            nc.vector.tensor_tensor(signed[b][:], ts_spread[:], y_raw[b], MULT)
+
+        def margins(b):
+            rows = slice(b * P, (b + 1) * P)
+            raw_a = psum.tile([P, N], F32, name="raw_a", bufs=2)
+            nc.tensor.matmul_mx(
+                out=raw_a[:],
+                lhsT=x_codes[:, rows].bitcast(E4M3),
+                lhsT_scale=x_scales[:, rows],
+                rhs=w1_codes[:].bitcast(E4M3),
+                rhs_scale=w1_scales[:],
+                start=True,
+                stop=True,
+            )
+            margin = work.tile([P, N], F32, name="margin")
+            nc.vector.tensor_tensor(margin[:], raw_a[:], signed[b][:], MULT)
+            slack[b] = work.tile([P, N], F32, name="slack")
+            nc.scalar.activation(slack[b][:], margin[:], ACT.Relu, bias=1.0, scale=-1.0)
+
+        def gradient(b):
+            h = work.tile([P, N], BF16, name="h")
+            nc.vector.scalar_tensor_tensor(
+                h[:], slack[b][:], neg_wt[:, b : b + 1], signed[b][:], MULT, MULT
+            )
+            h_words = h[:].bitcast(F32)
+            h_turned = psum.tile([P, 2, P], F32, name="h_turned", tag="turn", bufs=2)
+            for u in range(2):
+                nc.tensor.transpose(h_turned[:, u, :], h_words[:, u : N // 2 : 2], ident_f32[:])
+            h_grouped[b] = work.tile([P, N], BF16, name="h_grouped", align_bytes=64)
+            nc.scalar.copy(
+                h_grouped[b][:].bitcast(F32).rearrange("s (r u) -> s r u", u=2),
+                h_turned[:].rearrange("s u r -> s r u"),
+            )
+
+        def product(b):
+            h_codes = work.tile([P, P], U32, name="h_codes", align_bytes=64)
+            h_scales = work.tile([P, P], U8, name="h_scales", align_bytes=64)
+            nc.vector.quantize_mx(
+                out=h_codes[:].bitcast(E5M2), scales=h_scales[:], in_=h_grouped[b][:]
+            )
+            sums[b] = psum.tile([P, D], F32, name="sums", tag="result", bufs=3)
+            nc.tensor.matmul_mx(
+                out=sums[b][:],
+                lhsT=h_codes[:].bitcast(E5M2),
+                lhsT_scale=h_scales[:],
+                rhs=w2_codes[:].bitcast(E4M3),
+                rhs_scale=w2_scales[:],
+                start=True,
+                stop=True,
+            )
+
+        def store(b):
+            result = work.tile([P, D], F32, name="result")
+            nc.scalar.copy(
+                result[:].rearrange("r (p t) -> r p t", t=PACK),
+                sums[b][:].rearrange("r (t p) -> r p t", t=PACK),
+            )
+            nc.sync.dma_start(out[0, b * P : (b + 1) * P, :], result[:])
+
+        group_x(0)
+        quantize_x(0, 1)
+        sign_scales(0)
+        group_x(1)
+        for step in range(BLOCKS + 3):
+            if 0 <= step - 2 < BLOCKS:
+                product(step - 2)
+            if 0 <= step - 1 < BLOCKS:
+                gradient(step - 1)
+            if step < BLOCKS:
+                margins(step)
+            if step == 0:
+                quantize_x(1, 1)
+                nc.vector.quantize_mx(
+                    out=w2_codes[:].bitcast(E4M3),
+                    scales=w2_scales[:],
+                    in_=w_by_slot[:].rearrange("s t p j -> s (t p j)"),
+                )
+            if step + 1 < BLOCKS:
+                sign_scales(step + 1)
+            if step % 2 == 0 and step + 2 < BLOCKS:
+                group_x(step + 2)
+                group_x(step + 3)
+            if step % 2 == 1 and step + 1 < BLOCKS:
+                quantize_x(step + 1, 2)
+            if 0 <= step - 3 < BLOCKS:
+                store(step - 3)

@@ -7,7 +7,7 @@ D, T, N, R = 512, 2048, 512, 1024
 P = 128
 PACK = 4
 BLOCKS = R // P
-X_CHUNKS = [(0, 256), (256, 512), (512, 1024)]
+X_CHUNKS = [(0, 256), (256, 512), (512, 768), (768, 1024)]
 Y_ROWS = 256
 
 FLOPS = 2 * 2 * R * N * D
@@ -28,7 +28,8 @@ def tile_attend_gsqh_x_ts_kernel(tc, xT, wT, y, wt, ts, offs, out):
     nc = tc.nc
     with ExitStack() as ctx:
         keep = ctx.enter_context(tc.tile_pool(name="keep", bufs=1))
-        work = ctx.enter_context(tc.tile_pool(name="work", bufs=BLOCKS))
+        work = ctx.enter_context(tc.tile_pool(name="work", bufs=1))
+        stage = ctx.enter_context(tc.tile_pool(name="stage", bufs=PACK))
         psum = ctx.enter_context(tc.psum_pool(name="psum", bufs=1))
 
         offsets = keep.tile([P, N // 16], U16, name="offsets")
@@ -44,7 +45,7 @@ def tile_attend_gsqh_x_ts_kernel(tc, xT, wT, y, wt, ts, offs, out):
         w_rows = wT.rearrange("(p t) c -> p t c", t=PACK)
         w_planes = []
         for t in range(PACK):
-            plane = keep.tile([P, T], F32, name="w_plane%d" % t)
+            plane = stage.tile([P, T], F32, name="w_plane%d" % t, tag="loaded")
             nc.sync.dma_start(plane[:], w_rows[:, t, :])
             w_planes.append(plane)
 
@@ -55,24 +56,16 @@ def tile_attend_gsqh_x_ts_kernel(tc, xT, wT, y, wt, ts, offs, out):
 
         def load_x(k):
             lo, hi = X_CHUNKS[k]
-            raw = keep.tile([P, PACK, hi - lo], F32, name="x_raw%d" % k)
+            raw = stage.tile([P, PACK, hi - lo], F32, name="x_raw%d" % k, tag="loaded")
             nc.sync.dma_start(raw[:], x_rows[:, :, lo:hi])
             for b in range(lo // P, hi // P):
-                x_raw[b] = raw[:, :, b * P - lo : (b + 1) * P - lo]
+                x_raw[b] = (raw, b * P - lo)
 
         def load_y(k):
-            raw = keep.tile([P, Y_ROWS // P, N], F32, name="y_raw%d" % k)
+            raw = stage.tile([P, Y_ROWS // P, N], F32, name="y_raw%d" % k, tag="loaded")
             nc.sync.dma_start(raw[:], y_rows[k])
             for j in range(Y_ROWS // P):
-                y_raw[k * (Y_ROWS // P) + j] = raw[:, j, :]
-
-        load_x(0)
-        load_y(0)
-        load_x(1)
-        load_y(1)
-        load_x(2)
-        load_y(2)
-        load_y(3)
+                y_raw[k * (Y_ROWS // P) + j] = (raw, j)
 
         ident_f32 = keep.tile([P, P], F32, name="ident_f32")
         make_identity(nc, ident_f32[:])
@@ -86,28 +79,38 @@ def tile_attend_gsqh_x_ts_kernel(tc, xT, wT, y, wt, ts, offs, out):
 
         ts_listed = keep.tile([P, N], F32, name="ts_listed")
         nc.vector.tensor_copy(ts_listed[:], ts_window[:].indirect(offsets[:]))
+        ts_split = keep.tile([P, 2, P, 2], F32, name="ts_split")
+        nc.scalar.copy(ts_split[:], ts_listed[:].rearrange("p (s u e) -> p u s e", u=2, e=2))
+        ts_flat = ts_split[:].rearrange("p u s e -> p (u s e)")
         ts_turned = psum.tile([P, PACK, P], F32, name="ts_turned", tag="turn", bufs=2)
         for q in range(PACK):
-            nc.tensor.transpose(ts_turned[:, q, :], ts_listed[:, q * P : (q + 1) * P], ident_f32[:])
+            nc.tensor.transpose(ts_turned[:, q, :], ts_flat[:, q * P : (q + 1) * P], ident_f32[:])
         ts_cols = keep.tile([P, PACK], F32, name="ts_cols")
         nc.scalar.copy(ts_cols[:], ts_turned[:, :, P - 1])
-        ts_spread = psum.tile([P, N], F32, name="ts_spread")
+        ts_rows = psum.tile([P, N], F32, name="ts_rows", tag="turn", bufs=2)
         for q in range(PACK):
             nc.tensor.transpose(
-                ts_spread[:, q * P : (q + 1) * P],
+                ts_rows[:, q * P : (q + 1) * P],
                 ts_cols[:, q : q + 1].to_broadcast([P, P]),
                 ident_f32[:],
             )
+        ts_spread = keep.tile([P, N], F32, name="ts_spread")
+        nc.scalar.copy(ts_spread[:], ts_rows[:])
 
         w_by_d = keep.tile([P, N, PACK], BF16, name="w_by_d", align_bytes=64)
         w_by_slot = keep.tile([P, PACK, P, PACK], BF16, name="w_by_slot", align_bytes=64)
         w_quads = w_by_d[:].rearrange("p (s j) t -> p j t s", j=PACK)
         for t in range(PACK):
             nc.vector.tensor_copy(w_by_d[:, :, t], w_planes[t][:].indirect(offsets[:]))
-            w_turned = psum.tile([P, PACK, P], BF16, name="w_turned", tag="result", bufs=3)
+            w_turned = psum.tile([P, PACK, P], BF16, name="w_turned", tag="sums", bufs=3)
             for j in range(PACK):
                 nc.tensor.transpose(w_turned[:, j, :], w_quads[:, j, t, :], ident_bf16[:])
             nc.scalar.copy(w_by_slot[:, t, :, :], w_turned[:].rearrange("s j p -> s p j"))
+
+        load_x(0)
+        load_y(0)
+        load_x(1)
+        load_y(1)
 
         w1_codes = keep.tile([P, N], U32, name="w1_codes", align_bytes=64)
         w1_scales = keep.tile([P, N], U8, name="w1_scales", align_bytes=64)
@@ -122,34 +125,56 @@ def tile_attend_gsqh_x_ts_kernel(tc, xT, wT, y, wt, ts, offs, out):
         x_scales = keep.tile([P, R], U8, name="x_scales", align_bytes=64)
         w2_codes = keep.tile([P, D], U32, name="w2_codes", align_bytes=64)
         w2_scales = keep.tile([P, D], U8, name="w2_scales", align_bytes=64)
+        margin = keep.tile([P, BLOCKS, N], F32, name="margin")
+        slack = keep.tile([P, BLOCKS, N], F32, name="slack")
+        h = keep.tile([P, BLOCKS, N], BF16, name="h")
+        h_grouped = keep.tile([P, R, PACK], BF16, name="h_grouped", align_bytes=64)
+        h_codes = keep.tile([P, R], U32, name="h_codes", align_bytes=64)
+        h_scales = keep.tile([P, R], U8, name="h_scales", align_bytes=64)
+        result = keep.tile([P, BLOCKS, D], F32, name="result")
+        signed = {}
+        sums = {}
 
-        def group_x(b):
-            rows = slice(b * P, (b + 1) * P)
-            nc.scalar.copy(
-                x_grouped[:, rows, :].rearrange("p (c i) t -> p c t i", i=PACK),
-                x_raw[b].rearrange("p t (c i) -> p c t i", i=PACK),
+        def rows_of(b, count):
+            return slice(b * P, (b + count) * P)
+
+        def group_x(b, count, copy):
+            raw, first = x_raw[b]
+            copy(
+                x_grouped[:, rows_of(b, count), :].rearrange("p (c i) t -> p c t i", i=PACK),
+                raw[:, :, first : first + count * P].rearrange("p t (c i) -> p c t i", i=PACK),
             )
 
         def quantize_x(b, count):
-            rows = slice(b * P, (b + count) * P)
+            rows = rows_of(b, count)
             nc.vector.quantize_mx(
                 out=x_codes[:, rows].bitcast(E4M3),
                 scales=x_scales[:, rows],
                 in_=x_grouped[:, rows, :].rearrange("p r t -> p (r t)"),
             )
 
-        signed = {}
-        sums = {}
-        slack = {}
-        h_grouped = {}
+        def quantize_w2():
+            nc.vector.quantize_mx(
+                out=w2_codes[:].bitcast(E4M3),
+                scales=w2_scales[:],
+                in_=w_by_slot[:].rearrange("s t p j -> s (t p j)"),
+            )
 
-        def sign_scales(b):
-            signed[b] = work.tile([P, N], F32, name="signed")
-            nc.vector.tensor_tensor(signed[b][:], ts_spread[:], y_raw[b], MULT)
+        def sign_scales(b, count):
+            raw, first = y_raw[b]
+            both = work.tile([P, 2, count, N // 2], F32, name="signed%d" % b)
+            nc.vector.tensor_tensor(
+                both[:],
+                ts_spread[:].rearrange("p (u k) -> p u k", u=2).unsqueeze(2).to_broadcast([P, 2, count, N // 2]),
+                raw[:, first : first + count, :].rearrange("p j (s u e) -> p u (j s) e", u=2, e=2),
+                MULT,
+            )
+            for j in range(count):
+                signed[b + j] = both[:, :, j, :]
 
         def margins(b):
-            rows = slice(b * P, (b + 1) * P)
-            raw_a = psum.tile([P, N], F32, name="raw_a", bufs=2)
+            rows = rows_of(b, 1)
+            raw_a = psum.tile([P, N], F32, name="raw_a", bufs=3)
             nc.tensor.matmul_mx(
                 out=raw_a[:],
                 lhsT=x_codes[:, rows].bitcast(E4M3),
@@ -159,75 +184,138 @@ def tile_attend_gsqh_x_ts_kernel(tc, xT, wT, y, wt, ts, offs, out):
                 start=True,
                 stop=True,
             )
-            margin = work.tile([P, N], F32, name="margin")
-            nc.vector.tensor_tensor(margin[:], raw_a[:], signed[b][:], MULT)
-            slack[b] = work.tile([P, N], F32, name="slack")
-            nc.scalar.activation(slack[b][:], margin[:], ACT.Relu, bias=1.0, scale=-1.0)
+            nc.vector.tensor_tensor(
+                margin[:, b, :].rearrange("p (u s e) -> p u s e", u=2, e=2),
+                raw_a[:].rearrange("p (s u e) -> p u s e", u=2, e=2),
+                signed[b].rearrange("p u (s e) -> p u s e", e=2),
+                MULT,
+            )
+
+        def hinge(b, count):
+            nc.scalar.activation(
+                slack[:, b : b + count, :], margin[:, b : b + count, :], ACT.Relu, bias=1.0, scale=-1.0
+            )
 
         def gradient(b):
-            h = work.tile([P, N], BF16, name="h")
             nc.vector.scalar_tensor_tensor(
-                h[:], slack[b][:], neg_wt[:, b : b + 1], signed[b][:], MULT, MULT
-            )
-            h_words = h[:].bitcast(F32)
-            h_turned = psum.tile([P, 2, P], F32, name="h_turned", tag="turn", bufs=2)
-            for u in range(2):
-                nc.tensor.transpose(h_turned[:, u, :], h_words[:, u : N // 2 : 2], ident_f32[:])
-            h_grouped[b] = work.tile([P, N], BF16, name="h_grouped", align_bytes=64)
-            nc.scalar.copy(
-                h_grouped[b][:].bitcast(F32).rearrange("s (r u) -> s r u", u=2),
-                h_turned[:].rearrange("s u r -> s r u"),
+                h[:, b, :].rearrange("p (u k) -> p u k", u=2),
+                slack[:, b, :].rearrange("p (u k) -> p u k", u=2),
+                neg_wt[:, b : b + 1],
+                signed[b],
+                MULT,
+                MULT,
             )
 
-        def product(b):
-            h_codes = work.tile([P, P], U32, name="h_codes", align_bytes=64)
-            h_scales = work.tile([P, P], U8, name="h_scales", align_bytes=64)
+        def turn_h(b, count, copy):
+            h_turned = psum.tile([P, count, 2, P], F32, name="h_turned", tag="turn", bufs=2)
+            for j in range(count):
+                h_words = h[:, b + j, :].bitcast(F32)
+                for u in range(2):
+                    nc.tensor.transpose(h_turned[:, j, u, :], h_words[:, u * P : (u + 1) * P], ident_f32[:])
+            copy(
+                h_grouped[:, rows_of(b, count), :]
+                .rearrange("s r t -> s (r t)")
+                .bitcast(F32)
+                .rearrange("s (j r u) -> s j r u", j=count, u=2),
+                h_turned[:].rearrange("s j u r -> s j r u"),
+            )
+
+        def product(b, count):
+            rows = rows_of(b, count)
             nc.vector.quantize_mx(
-                out=h_codes[:].bitcast(E5M2), scales=h_scales[:], in_=h_grouped[b][:]
+                out=h_codes[:, rows].bitcast(E5M2),
+                scales=h_scales[:, rows],
+                in_=h_grouped[:, rows, :].rearrange("s r t -> s (r t)"),
             )
-            sums[b] = psum.tile([P, D], F32, name="sums", tag="result", bufs=3)
-            nc.tensor.matmul_mx(
-                out=sums[b][:],
-                lhsT=h_codes[:].bitcast(E5M2),
-                lhsT_scale=h_scales[:],
-                rhs=w2_codes[:].bitcast(E4M3),
-                rhs_scale=w2_scales[:],
-                start=True,
-                stop=True,
-            )
-
-        def store(b):
-            result = work.tile([P, D], F32, name="result")
-            nc.scalar.copy(
-                result[:].rearrange("r (p t) -> r p t", t=PACK),
-                sums[b][:].rearrange("r (t p) -> r p t", t=PACK),
-            )
-            nc.sync.dma_start(out[0, b * P : (b + 1) * P, :], result[:])
-
-        group_x(0)
-        quantize_x(0, 1)
-        sign_scales(0)
-        group_x(1)
-        for step in range(BLOCKS + 3):
-            if 0 <= step - 2 < BLOCKS:
-                product(step - 2)
-            if 0 <= step - 1 < BLOCKS:
-                gradient(step - 1)
-            if step < BLOCKS:
-                margins(step)
-            if step == 0:
-                quantize_x(1, 1)
-                nc.vector.quantize_mx(
-                    out=w2_codes[:].bitcast(E4M3),
-                    scales=w2_scales[:],
-                    in_=w_by_slot[:].rearrange("s t p j -> s (t p j)"),
+            for k in range(b, b + count):
+                sums[k] = psum.tile([P, D], F32, name="sums", tag="sums", bufs=3)
+                nc.tensor.matmul_mx(
+                    out=sums[k][:],
+                    lhsT=h_codes[:, rows_of(k, 1)].bitcast(E5M2),
+                    lhsT_scale=h_scales[:, rows_of(k, 1)],
+                    rhs=w2_codes[:].bitcast(E4M3),
+                    rhs_scale=w2_scales[:],
+                    start=True,
+                    stop=True,
                 )
-            if step + 1 < BLOCKS:
-                sign_scales(step + 1)
-            if step % 2 == 0 and step + 2 < BLOCKS:
-                group_x(step + 2)
-                group_x(step + 3)
-            if step % 2 == 1 and step + 1 < BLOCKS:
-                quantize_x(step + 1, 2)
-            if 0 <= step - 3 < BLOCKS:
-                store(step - 3)
+
+        def store(b, on_vector, pieces):
+            width = P // pieces
+            for first in range(0, P, width):
+                cols = slice(first * PACK, (first + width) * PACK)
+                ordered = result[:, b, cols].rearrange("r (p t) -> r p t", t=PACK)
+                turned = sums[b][:].rearrange("r (t p) -> r p t", t=PACK)[:, first : first + width, :]
+                if on_vector:
+                    nc.vector.tensor_copy(ordered, turned)
+                else:
+                    nc.scalar.copy(ordered, turned)
+                nc.sync.dma_start(out[0, rows_of(b, 1), cols], result[:, b, cols])
+
+        group_x(0, 1, nc.scalar.copy)
+        quantize_x(0, 1)
+        sign_scales(0, 1)
+        margins(0)
+        group_x(1, 1, nc.scalar.copy)
+        quantize_x(1, 1)
+        sign_scales(1, 1)
+        quantize_w2()
+        margins(1)
+        group_x(2, 2, nc.scalar.copy)
+        quantize_x(2, 2)
+        sign_scales(2, 2)
+        hinge(0, 1)
+        margins(2)
+        hinge(1, 1)
+        gradient(0)
+        margins(3)
+        turn_h(0, 1, nc.scalar.copy)
+        load_x(2)
+        load_y(2)
+        group_x(4, 2, nc.scalar.copy)
+        quantize_x(4, 2)
+        sign_scales(4, 2)
+        hinge(2, 1)
+        gradient(1)
+        margins(4)
+        turn_h(1, 1, nc.scalar.copy)
+        product(0, 1)
+        hinge(3, 1)
+        gradient(2)
+        margins(5)
+        turn_h(2, 1, nc.scalar.copy)
+        product(1, 1)
+        load_x(3)
+        load_y(3)
+        group_x(6, 2, nc.scalar.copy)
+        quantize_x(6, 2)
+        sign_scales(6, 2)
+        hinge(4, 1)
+        gradient(3)
+        store(0, False, 1)
+        margins(6)
+        turn_h(3, 1, nc.scalar.copy)
+        product(2, 1)
+        hinge(5, 1)
+        gradient(4)
+        store(1, False, 1)
+        margins(7)
+        turn_h(4, 1, nc.scalar.copy)
+        product(3, 1)
+        hinge(6, 1)
+        gradient(5)
+        store(2, False, 1)
+        turn_h(5, 1, nc.scalar.copy)
+        product(4, 1)
+        hinge(7, 1)
+        gradient(6)
+        store(3, False, 1)
+        turn_h(6, 1, nc.scalar.copy)
+        product(5, 1)
+        gradient(7)
+        store(4, False, 1)
+        turn_h(7, 1, nc.scalar.copy)
+        product(6, 1)
+        store(5, False, 1)
+        product(7, 1)
+        store(6, False, 1)
+        store(7, True, 2)

@@ -252,67 +252,76 @@ def tile_attend_gsqh_x_ts_kernel(tc, xT, wT, y, wt, ts, offs, out):
                 nc.sync.dma_start(out[0, rows_of(b, 1), cols], result[:, b, cols])
 
         group_x(0, 1, nc.scalar.copy)
+        group_x(1, 1, nc.scalar.copy)
+        group_x(2, 1, nc.scalar.copy)
         quantize_x(0, 1)
         sign_scales(0, 1)
-        margins(0)
-        group_x(1, 1, nc.scalar.copy)
+        group_x(3, 1, nc.scalar.copy)
         quantize_x(1, 1)
         sign_scales(1, 1)
-        quantize_w2()
-        margins(1)
-        group_x(2, 2, nc.scalar.copy)
-        quantize_x(2, 2)
-        sign_scales(2, 2)
+        margins(0)
         hinge(0, 1)
-        margins(2)
-        hinge(1, 1)
-        gradient(0)
-        margins(3)
-        turn_h(0, 1, nc.scalar.copy)
         load_x(2)
         load_y(2)
-        group_x(4, 2, nc.scalar.copy)
-        quantize_x(4, 2)
-        sign_scales(4, 2)
+        group_x(4, 1, nc.scalar.copy)
+        quantize_x(2, 1)
+        sign_scales(2, 1)
+        margins(1)
+        quantize_w2()
+        hinge(1, 1)
+        group_x(5, 1, nc.scalar.copy)
+        quantize_x(3, 1)
+        sign_scales(3, 1)
+        margins(2)
         hinge(2, 1)
-        gradient(1)
-        margins(4)
-        turn_h(1, 1, nc.scalar.copy)
-        product(0, 1)
-        hinge(3, 1)
-        gradient(2)
-        margins(5)
-        turn_h(2, 1, nc.scalar.copy)
-        product(1, 1)
+        gradient(0)
         load_x(3)
         load_y(3)
-        group_x(6, 2, nc.scalar.copy)
-        quantize_x(6, 2)
-        sign_scales(6, 2)
+        group_x(6, 1, nc.scalar.copy)
+        quantize_x(4, 1)
+        sign_scales(4, 1)
+        margins(3)
+        hinge(3, 1)
+        gradient(1)
+        turn_h(0, 1, nc.scalar.copy)
+        group_x(7, 1, nc.scalar.copy)
+        quantize_x(5, 1)
+        sign_scales(5, 1)
+        margins(4)
         hinge(4, 1)
+        gradient(2)
+        turn_h(1, 1, nc.scalar.copy)
+        product(0, 1)
+        quantize_x(6, 1)
+        sign_scales(6, 1)
+        margins(5)
+        hinge(5, 1)
         gradient(3)
-        store(0, False, 1)
+        turn_h(2, 1, nc.scalar.copy)
+        product(1, 1)
+        quantize_x(7, 1)
+        sign_scales(7, 1)
         margins(6)
+        store(0, False, 1)
+        hinge(6, 1)
+        gradient(4)
         turn_h(3, 1, nc.scalar.copy)
         product(2, 1)
-        hinge(5, 1)
-        gradient(4)
-        store(1, False, 1)
         margins(7)
+        store(1, False, 1)
+        hinge(7, 1)
+        gradient(5)
         turn_h(4, 1, nc.scalar.copy)
         product(3, 1)
-        hinge(6, 1)
-        gradient(5)
         store(2, False, 1)
+        gradient(6)
         turn_h(5, 1, nc.scalar.copy)
         product(4, 1)
-        hinge(7, 1)
-        gradient(6)
         store(3, False, 1)
+        gradient(7)
         turn_h(6, 1, nc.scalar.copy)
         product(5, 1)
-        gradient(7)
-        store(4, False, 1)
+        store(4, True, 1)
         turn_h(7, 1, nc.scalar.copy)
         product(6, 1)
         store(5, False, 1)

@@ -9,6 +9,8 @@ PACK = 4
 BLOCKS = R // P
 X_CHUNKS = [(0, 256), (256, 512), (512, 768), (768, 1024)]
 Y_ROWS = 256
+GPSIMD_BLOCKS = 5
+CHUNK = 1024
 
 FLOPS = 2 * 2 * R * N * D
 BYTES = 4 * (D * R + D * T + R * N + R + T + R * D) + 2 * P * (N // 16)
@@ -28,14 +30,13 @@ def tile_attend_gsqh_x_ts_kernel(tc, xT, wT, y, wt, ts, offs, out):
     nc = tc.nc
     with ExitStack() as ctx:
         keep = ctx.enter_context(tc.tile_pool(name="keep", bufs=1))
-        work = ctx.enter_context(tc.tile_pool(name="work", bufs=1))
-        stage = ctx.enter_context(tc.tile_pool(name="stage", bufs=PACK))
+        stage = ctx.enter_context(tc.tile_pool(name="stage", bufs=1))
         psum = ctx.enter_context(tc.psum_pool(name="psum", bufs=1))
 
         offsets = keep.tile([P, N // 16], U16, name="offsets")
         nc.sync.dma_start(offsets[:], offs)
 
-        wt_rows = keep.tile([P, P], F32, name="wt_rows")
+        wt_rows = stage.tile([P, P], F32, name="wt_rows", tag="slot3", align_bytes=64)
         nc.sync.dma_start(wt_rows[P - BLOCKS : P, :], wt[0].rearrange("(b p) o -> b (p o)", p=P))
         ts_window = keep.tile([P, T], F32, name="ts_window")
         nc.sync.dma_start(ts_window[P - 1 : P, :], ts[0:1, :])
@@ -44,26 +45,30 @@ def tile_attend_gsqh_x_ts_kernel(tc, xT, wT, y, wt, ts, offs, out):
 
         w_rows = wT.rearrange("(p t) c -> p t c", t=PACK)
         w_planes = []
-        for t in range(PACK):
-            plane = stage.tile([P, T], F32, name="w_plane%d" % t, tag="loaded")
+
+        def load_plane(t):
+            plane = stage.tile([P, T], F32, name="w_plane%d" % t, tag="slot%d" % t, align_bytes=64)
             nc.sync.dma_start(plane[:], w_rows[:, t, :])
             w_planes.append(plane)
+
+        for t in range(PACK - 1):
+            load_plane(t)
 
         x_rows = xT[0].rearrange("(p t) r -> p t r", t=PACK)
         y_rows = y[0].rearrange("(k j p) i -> k p j i", p=P, j=Y_ROWS // P)
         x_raw = {}
         y_raw = {}
 
-        def load_x(k):
+        def load_x(k, space):
             lo, hi = X_CHUNKS[k]
-            raw = stage.tile([P, PACK, hi - lo], F32, name="x_raw%d" % k, tag="loaded")
-            nc.sync.dma_start(raw[:], x_rows[:, :, lo:hi])
+            raw = space.rearrange("p (t r) -> p t r", t=PACK)
+            nc.sync.dma_start(raw, x_rows[:, :, lo:hi])
             for b in range(lo // P, hi // P):
                 x_raw[b] = (raw, b * P - lo)
 
-        def load_y(k):
-            raw = stage.tile([P, Y_ROWS // P, N], F32, name="y_raw%d" % k, tag="loaded")
-            nc.sync.dma_start(raw[:], y_rows[k])
+        def load_y(k, space):
+            raw = space.rearrange("p (j i) -> p j i", i=N)
+            nc.sync.dma_start(raw, y_rows[k])
             for j in range(Y_ROWS // P):
                 y_raw[k * (Y_ROWS // P) + j] = (raw, j)
 
@@ -74,43 +79,69 @@ def tile_attend_gsqh_x_ts_kernel(tc, xT, wT, y, wt, ts, offs, out):
 
         wt_turned = psum.tile([P, P], F32, name="wt_turned", tag="turn", bufs=2)
         nc.tensor.transpose(wt_turned[:], wt_rows[:], ident_f32[:])
-        neg_wt = keep.tile([P, BLOCKS], F32, name="neg_wt")
-        nc.scalar.activation(neg_wt[:], wt_turned[:, P - BLOCKS : P], ACT.Copy, scale=-1.0)
+        load_plane(PACK - 1)
+        wt_cols = keep.tile([P, BLOCKS], F32, name="wt_cols")
+        wt_size = keep.tile([P, BLOCKS], F32, name="wt_size")
+        wt_flip = keep.tile([P, BLOCKS], F32, name="wt_flip")
+        nc.scalar.copy(wt_cols[:], wt_turned[:, P - BLOCKS : P])
+        nc.scalar.activation(wt_size[:], wt_turned[:, P - BLOCKS : P], ACT.Abs)
+        nc.scalar.activation(wt_flip[:], wt_turned[:, P - BLOCKS : P], ACT.Sign, scale=-1.0)
 
         ts_listed = keep.tile([P, N], F32, name="ts_listed")
         nc.vector.tensor_copy(ts_listed[:], ts_window[:].indirect(offsets[:]))
-        ts_split = keep.tile([P, 2, P, 2], F32, name="ts_split")
-        nc.scalar.copy(ts_split[:], ts_listed[:].rearrange("p (s u e) -> p u s e", u=2, e=2))
-        ts_flat = ts_split[:].rearrange("p u s e -> p (u s e)")
         ts_turned = psum.tile([P, PACK, P], F32, name="ts_turned", tag="turn", bufs=2)
         for q in range(PACK):
-            nc.tensor.transpose(ts_turned[:, q, :], ts_flat[:, q * P : (q + 1) * P], ident_f32[:])
+            nc.tensor.transpose(ts_turned[:, q, :], ts_listed[:, q * P : (q + 1) * P], ident_f32[:])
         ts_cols = keep.tile([P, PACK], F32, name="ts_cols")
         nc.scalar.copy(ts_cols[:], ts_turned[:, :, P - 1])
-        ts_rows = psum.tile([P, N], F32, name="ts_rows", tag="turn", bufs=2)
+        ts_rows = psum.tile([P, N], F32, name="ts_rows")
         for q in range(PACK):
             nc.tensor.transpose(
                 ts_rows[:, q * P : (q + 1) * P],
                 ts_cols[:, q : q + 1].to_broadcast([P, P]),
                 ident_f32[:],
             )
-        ts_spread = keep.tile([P, N], F32, name="ts_spread")
-        nc.scalar.copy(ts_spread[:], ts_rows[:])
 
         w_by_d = keep.tile([P, N, PACK], BF16, name="w_by_d", align_bytes=64)
-        w_by_slot = keep.tile([P, PACK, P, PACK], BF16, name="w_by_slot", align_bytes=64)
         w_quads = w_by_d[:].rearrange("p (s j) t -> p j t s", j=PACK)
-        for t in range(PACK):
-            nc.vector.tensor_copy(w_by_d[:, :, t], w_planes[t][:].indirect(offsets[:]))
-            w_turned = psum.tile([P, PACK, P], BF16, name="w_turned", tag="sums", bufs=3)
-            for j in range(PACK):
-                nc.tensor.transpose(w_turned[:, j, :], w_quads[:, j, t, :], ident_bf16[:])
-            nc.scalar.copy(w_by_slot[:, t, :, :], w_turned[:].rearrange("s j p -> s p j"))
+        w2_codes = keep.tile([P, D], U32, name="w2_codes", align_bytes=64)
+        w2_scales = keep.tile([P, D], U8, name="w2_scales", align_bytes=64)
+        w_turned = {}
 
-        load_x(0)
-        load_y(0)
-        load_x(1)
-        load_y(1)
+        def gather_w(t):
+            nc.vector.tensor_copy(w_by_d[:, :, t], w_planes[t][:].indirect(offsets[:]))
+            w_turned[t] = psum.tile([P, PACK, P], BF16, name="w_turned", tag="sums", bufs=3)
+            for j in range(PACK):
+                nc.tensor.transpose(w_turned[t][:, j, :], w_quads[:, j, t, :], ident_bf16[:])
+
+        def quantize_w2(half, w_by_slot):
+            for e in range(2):
+                nc.scalar.copy(w_by_slot[:, e, :, :], w_turned[2 * half + e][:].rearrange("s j p -> s p j"))
+            cols = slice(half * 2 * P, (half + 1) * 2 * P)
+            nc.vector.quantize_mx(
+                out=w2_codes[:, cols].bitcast(E4M3),
+                scales=w2_scales[:, cols],
+                in_=w_by_slot[:].rearrange("s e p j -> s (e p j)"),
+            )
+
+        gather_w(0)
+        gather_w(1)
+        gather_w(2)
+        w_first_half = keep.tile([P, 2, P, PACK], BF16, name="w_first_half", align_bytes=64)
+        quantize_w2(0, w_first_half)
+        gather_w(3)
+
+        x_first = stage.tile([P, CHUNK], F32, name="x_first", tag="slot0", align_bytes=64)
+        y_first = stage.tile([P, CHUNK], F32, name="y_first", tag="slot1", align_bytes=64)
+        x_second = stage.tile([P, CHUNK], F32, name="x_second", tag="slot2", align_bytes=64)
+        later = stage.tile([P, 5 * CHUNK], F32, name="later", tag="slot3", align_bytes=64)
+        load_x(0, x_first[:])
+        load_y(0, y_first[:])
+        load_x(1, x_second[:])
+        load_y(1, later[:, 0:CHUNK])
+        for k in range(2, 4):
+            load_x(k, later[:, (2 * k - 3) * CHUNK : (2 * k - 2) * CHUNK])
+            load_y(k, later[:, (2 * k - 2) * CHUNK : (2 * k - 1) * CHUNK])
 
         w1_codes = keep.tile([P, N], U32, name="w1_codes", align_bytes=64)
         w1_scales = keep.tile([P, N], U8, name="w1_scales", align_bytes=64)
@@ -120,211 +151,187 @@ def tile_attend_gsqh_x_ts_kernel(tc, xT, wT, y, wt, ts, offs, out):
             in_=w_by_d[:].rearrange("p i t -> p (i t)"),
         )
 
-        x_grouped = keep.tile([P, R, PACK], BF16, name="x_grouped", align_bytes=64)
-        x_codes = keep.tile([P, R], U32, name="x_codes", align_bytes=64)
+        def shared(shape, dtype, name, tag):
+            return stage.tile(shape, dtype, name=name, tag=tag, align_bytes=64)
+
         x_scales = keep.tile([P, R], U8, name="x_scales", align_bytes=64)
-        w2_codes = keep.tile([P, D], U32, name="w2_codes", align_bytes=64)
-        w2_scales = keep.tile([P, D], U8, name="w2_scales", align_bytes=64)
-        margin = keep.tile([P, BLOCKS, N], F32, name="margin")
-        slack = keep.tile([P, BLOCKS, N], F32, name="slack")
-        h = keep.tile([P, BLOCKS, N], BF16, name="h")
-        h_grouped = keep.tile([P, R, PACK], BF16, name="h_grouped", align_bytes=64)
-        h_codes = keep.tile([P, R], U32, name="h_codes", align_bytes=64)
         h_scales = keep.tile([P, R], U8, name="h_scales", align_bytes=64)
-        result = keep.tile([P, BLOCKS, D], F32, name="result")
+        h_grouped = [
+            keep.tile([P, P * PACK], BF16, name="h_grouped%d" % b, align_bytes=64) for b in range(BLOCKS)
+        ]
+        result = [keep.tile([P, D], F32, name="result%d" % b) for b in range(BLOCKS)]
+        x_grouped = {}
+        x_codes = {}
+        h_codes = {}
         signed = {}
+        margin = {}
+        slack = {}
+        h = {}
         sums = {}
+        raw_a = {}
+        h_turned = {}
+
+        pair_tag = ["pair0", "pair1", "slot0", "signed0"]
+        h_tag = {0: "pair1", 2: "signed0", GPSIMD_BLOCKS: "slack%d" % (GPSIMD_BLOCKS - 1)}
 
         def rows_of(b, count):
             return slice(b * P, (b + count) * P)
 
-        def group_x(b, count, copy):
+        def group_x(b):
             raw, first = x_raw[b]
-            copy(
-                x_grouped[:, rows_of(b, count), :].rearrange("p (c i) t -> p c t i", i=PACK),
-                raw[:, :, first : first + count * P].rearrange("p t (c i) -> p c t i", i=PACK),
+            if b % 2 == 0:
+                x_grouped[b // 2] = shared([P, 2 * P, PACK], BF16, "x_grouped%d" % b, pair_tag[b // 2])
+            nc.scalar.copy(
+                x_grouped[b // 2][:, rows_of(b % 2, 1), :].rearrange("p (c i) t -> p c t i", i=PACK),
+                raw[:, :, first : first + P].rearrange("p t (c i) -> p c t i", i=PACK),
             )
+
+        def code_space(codes, name, first, count, tag):
+            space = shared([P, count * P], U32, name, tag)
+            for k in range(count):
+                codes[first + k] = (space, k)
+
+        def words(codes, b, count):
+            space, k = codes[b]
+            return space[:, rows_of(k, count)]
 
         def quantize_x(b, count):
-            rows = rows_of(b, count)
             nc.vector.quantize_mx(
-                out=x_codes[:, rows].bitcast(E4M3),
-                scales=x_scales[:, rows],
-                in_=x_grouped[:, rows, :].rearrange("p r t -> p (r t)"),
+                out=words(x_codes, b, count).bitcast(E4M3),
+                scales=x_scales[:, rows_of(b, count)],
+                in_=x_grouped[b // 2][:, rows_of(b % 2, count), :].rearrange("p r t -> p (r t)"),
             )
 
-        def quantize_w2():
-            nc.vector.quantize_mx(
-                out=w2_codes[:].bitcast(E4M3),
-                scales=w2_scales[:],
-                in_=w_by_slot[:].rearrange("s t p j -> s (t p j)"),
-            )
-
-        def sign_scales(b, count):
+        def sign_scales(b):
             raw, first = y_raw[b]
-            both = work.tile([P, 2, count, N // 2], F32, name="signed%d" % b)
-            nc.vector.tensor_tensor(
-                both[:],
-                ts_spread[:].rearrange("p (u k) -> p u k", u=2).unsqueeze(2).to_broadcast([P, 2, count, N // 2]),
-                raw[:, first : first + count, :].rearrange("p j (s u e) -> p u (j s) e", u=2, e=2),
-                MULT,
+            tag = "margin%d" % (b - 3) if b >= 3 else "signed%d" % b
+            signed[b] = shared([P, N], F32, "signed%d" % b, tag)
+            nc.vector.scalar_tensor_tensor(
+                signed[b][:], raw[:, first, :], wt_flip[:, b : b + 1], ts_rows[:], MULT, MULT
             )
-            for j in range(count):
-                signed[b + j] = both[:, :, j, :]
 
-        def margins(b):
-            rows = rows_of(b, 1)
-            raw_a = psum.tile([P, N], F32, name="raw_a", bufs=3)
+        def scores(b):
+            raw_a[b] = psum.tile([P, N], F32, name="raw_a", bufs=2)
             nc.tensor.matmul_mx(
-                out=raw_a[:],
-                lhsT=x_codes[:, rows].bitcast(E4M3),
-                lhsT_scale=x_scales[:, rows],
+                out=raw_a[b][:],
+                lhsT=words(x_codes, b, 1).bitcast(E4M3),
+                lhsT_scale=x_scales[:, rows_of(b, 1)],
                 rhs=w1_codes[:].bitcast(E4M3),
                 rhs_scale=w1_scales[:],
                 start=True,
                 stop=True,
             )
-            nc.vector.tensor_tensor(
-                margin[:, b, :].rearrange("p (u s e) -> p u s e", u=2, e=2),
-                raw_a[:].rearrange("p (s u e) -> p u s e", u=2, e=2),
-                signed[b].rearrange("p u (s e) -> p u s e", e=2),
-                MULT,
-            )
 
-        def hinge(b, count):
+        def margins(b):
+            margin[b] = shared([P, N], F32, "margin%d" % b, "margin%d" % b)
+            nc.vector.tensor_tensor(margin[b][:], raw_a[b][:], signed[b][:], MULT)
+            slack[b] = shared([P, N], F32, "slack%d" % b, "slack%d" % b)
             nc.scalar.activation(
-                slack[:, b : b + count, :], margin[:, b : b + count, :], ACT.Relu, bias=1.0, scale=-1.0
+                slack[b][:], margin[b][:], ACT.Relu, bias=wt_size[:, b : b + 1], scale=wt_cols[:, b : b + 1]
             )
 
         def gradient(b):
-            nc.vector.scalar_tensor_tensor(
-                h[:, b, :].rearrange("p (u k) -> p u k", u=2),
-                slack[:, b, :].rearrange("p (u k) -> p u k", u=2),
-                neg_wt[:, b : b + 1],
-                signed[b],
-                MULT,
-                MULT,
-            )
+            engine = nc.gpsimd if b < GPSIMD_BLOCKS else nc.vector
+            h[b] = shared([P, N], BF16, "h%d" % b, h_tag.get(b, "h%d" % b))
+            engine.tensor_tensor(h[b][:], slack[b][:], signed[b][:], MULT)
 
-        def turn_h(b, count, copy):
-            h_turned = psum.tile([P, count, 2, P], F32, name="h_turned", tag="turn", bufs=2)
-            for j in range(count):
-                h_words = h[:, b + j, :].bitcast(F32)
-                for u in range(2):
-                    nc.tensor.transpose(h_turned[:, j, u, :], h_words[:, u * P : (u + 1) * P], ident_f32[:])
+        def turn_h(b, copy):
+            h_turned[b] = psum.tile([P, 2, P], F32, name="h_turned", tag="turn", bufs=2)
+            h_words = h[b][:].bitcast(F32)
+            for u in range(2):
+                nc.tensor.transpose(h_turned[b][:, u, :], h_words[:, u : 2 * P : 2], ident_f32[:])
             copy(
-                h_grouped[:, rows_of(b, count), :]
-                .rearrange("s r t -> s (r t)")
-                .bitcast(F32)
-                .rearrange("s (j r u) -> s j r u", j=count, u=2),
-                h_turned[:].rearrange("s j u r -> s j r u"),
+                h_grouped[b][:].bitcast(F32).rearrange("s (r u) -> s r u", u=2),
+                h_turned[b][:].rearrange("s u r -> s r u"),
             )
 
-        def product(b, count):
-            rows = rows_of(b, count)
+        def product(b):
             nc.vector.quantize_mx(
-                out=h_codes[:, rows].bitcast(E5M2),
-                scales=h_scales[:, rows],
-                in_=h_grouped[:, rows, :].rearrange("s r t -> s (r t)"),
+                out=words(h_codes, b, 1).bitcast(E5M2), scales=h_scales[:, rows_of(b, 1)], in_=h_grouped[b][:]
             )
-            for k in range(b, b + count):
-                sums[k] = psum.tile([P, D], F32, name="sums", tag="sums", bufs=3)
-                nc.tensor.matmul_mx(
-                    out=sums[k][:],
-                    lhsT=h_codes[:, rows_of(k, 1)].bitcast(E5M2),
-                    lhsT_scale=h_scales[:, rows_of(k, 1)],
-                    rhs=w2_codes[:].bitcast(E4M3),
-                    rhs_scale=w2_scales[:],
-                    start=True,
-                    stop=True,
-                )
+            sums[b] = psum.tile([P, D], F32, name="sums", tag="sums", bufs=3)
+            nc.tensor.matmul_mx(
+                out=sums[b][:],
+                lhsT=words(h_codes, b, 1).bitcast(E5M2),
+                lhsT_scale=h_scales[:, rows_of(b, 1)],
+                rhs=w2_codes[:].bitcast(E4M3),
+                rhs_scale=w2_scales[:],
+                start=True,
+                stop=True,
+            )
 
-        def store(b, on_vector, pieces):
+        def store(b, copy, pieces):
             width = P // pieces
             for first in range(0, P, width):
                 cols = slice(first * PACK, (first + width) * PACK)
-                ordered = result[:, b, cols].rearrange("r (p t) -> r p t", t=PACK)
+                ordered = result[b][:, cols].rearrange("r (p t) -> r p t", t=PACK)
                 turned = sums[b][:].rearrange("r (t p) -> r p t", t=PACK)[:, first : first + width, :]
-                if on_vector:
-                    nc.vector.tensor_copy(ordered, turned)
-                else:
-                    nc.scalar.copy(ordered, turned)
-                nc.sync.dma_start(out[0, rows_of(b, 1), cols], result[:, b, cols])
+                copy(ordered, turned)
+                nc.sync.dma_start(out[0, rows_of(b, 1), cols], result[b][:, cols])
 
-        group_x(0, 1, nc.scalar.copy)
-        group_x(1, 1, nc.scalar.copy)
-        group_x(2, 1, nc.scalar.copy)
+        on_scalar = nc.scalar.copy
+        on_vector = nc.vector.tensor_copy
+        code_space(x_codes, "x_codes_early", 0, 4, "x_codes_early")
+        group_x(0)
+        group_x(1)
         quantize_x(0, 1)
-        sign_scales(0, 1)
-        group_x(3, 1, nc.scalar.copy)
+        sign_scales(0)
         quantize_x(1, 1)
-        sign_scales(1, 1)
+        scores(0)
         margins(0)
-        hinge(0, 1)
-        load_x(2)
-        load_y(2)
-        group_x(4, 1, nc.scalar.copy)
-        quantize_x(2, 1)
-        sign_scales(2, 1)
-        margins(1)
-        quantize_w2()
-        hinge(1, 1)
-        group_x(5, 1, nc.scalar.copy)
-        quantize_x(3, 1)
-        sign_scales(3, 1)
-        margins(2)
-        hinge(2, 1)
+        sign_scales(1)
+        scores(1)
+        group_x(2)
+        group_x(3)
+        quantize_w2(1, shared([P, 2, P, PACK], BF16, "w_second_half", "slot0"))
+        quantize_x(2, 2)
         gradient(0)
-        load_x(3)
-        load_y(3)
-        group_x(6, 1, nc.scalar.copy)
-        quantize_x(4, 1)
-        sign_scales(4, 1)
-        margins(3)
-        hinge(3, 1)
+        margins(1)
         gradient(1)
-        turn_h(0, 1, nc.scalar.copy)
-        group_x(7, 1, nc.scalar.copy)
-        quantize_x(5, 1)
-        sign_scales(5, 1)
-        margins(4)
-        hinge(4, 1)
+        group_x(4)
+        group_x(5)
+        for b in (2, 3):
+            scores(b)
+            sign_scales(b)
+            margins(b)
+        group_x(6)
+        group_x(7)
+        sign_scales(4)
+        turn_h(0, on_scalar)
+        code_space(h_codes, "h_codes_first", 0, 1, "signed1")
+        product(0)
+        code_space(x_codes, "x_codes_late", 4, 4, "slack1")
+        quantize_x(4, 2)
+        quantize_x(6, 2)
         gradient(2)
-        turn_h(1, 1, nc.scalar.copy)
-        product(0, 1)
-        quantize_x(6, 1)
-        sign_scales(6, 1)
-        margins(5)
-        hinge(5, 1)
         gradient(3)
-        turn_h(2, 1, nc.scalar.copy)
-        product(1, 1)
-        quantize_x(7, 1)
-        sign_scales(7, 1)
-        margins(6)
-        store(0, False, 1)
-        hinge(6, 1)
-        gradient(4)
-        turn_h(3, 1, nc.scalar.copy)
-        product(2, 1)
-        margins(7)
-        store(1, False, 1)
-        hinge(7, 1)
-        gradient(5)
-        turn_h(4, 1, nc.scalar.copy)
-        product(3, 1)
-        store(2, False, 1)
-        gradient(6)
-        turn_h(5, 1, nc.scalar.copy)
-        product(4, 1)
-        store(3, False, 1)
-        gradient(7)
-        turn_h(6, 1, nc.scalar.copy)
-        product(5, 1)
-        store(4, True, 1)
-        turn_h(7, 1, nc.scalar.copy)
-        product(6, 1)
-        store(5, False, 1)
-        product(7, 1)
-        store(6, False, 1)
-        store(7, True, 2)
+        turn_h(1, on_scalar)
+        store(0, on_scalar, 1)
+        for b in range(4, BLOCKS):
+            scores(b)
+            if b + 1 < BLOCKS:
+                sign_scales(b + 1)
+            margins(b)
+            if b < GPSIMD_BLOCKS:
+                gradient(b)
+            if b in (5, 6):
+                turn_h(b - 3, on_scalar)
+        code_space(h_codes, "h_codes_rest", 1, BLOCKS - 1, "margin1")
+        for b in range(1, 4):
+            product(b)
+            gradient(b + 4)
+        turn_h(4, on_scalar)
+        store(1, on_scalar, 1)
+        product(4)
+        turn_h(5, on_vector)
+        store(2, on_scalar, 1)
+        turn_h(6, on_vector)
+        product(5)
+        store(3, on_scalar, 1)
+        turn_h(7, on_vector)
+        product(6)
+        store(4, on_scalar, 1)
+        product(7)
+        store(5, on_scalar, 1)
+        store(6, on_scalar, 1)
+        store(7, on_vector, 2)

@@ -9,7 +9,7 @@ PACK = 4
 BLOCKS = R // P
 X_CHUNKS = [(0, 256), (256, 512), (512, 768), (768, 1024)]
 Y_ROWS = 256
-GPSIMD_BLOCKS = 5
+GPSIMD_BLOCKS = 4
 CHUNK = 1024
 
 FLOPS = 2 * 2 * R * N * D
@@ -80,12 +80,12 @@ def tile_attend_gsqh_x_ts_kernel(tc, xT, wT, y, wt, ts, offs, out):
         wt_turned = psum.tile([P, P], F32, name="wt_turned", tag="turn", bufs=2)
         nc.tensor.transpose(wt_turned[:], wt_rows[:], ident_f32[:])
         load_plane(PACK - 1)
-        wt_cols = keep.tile([P, BLOCKS], F32, name="wt_cols")
+        wt_minus = keep.tile([P, BLOCKS], F32, name="wt_minus")
         wt_size = keep.tile([P, BLOCKS], F32, name="wt_size")
         wt_flip = keep.tile([P, BLOCKS], F32, name="wt_flip")
-        nc.scalar.copy(wt_cols[:], wt_turned[:, P - BLOCKS : P])
         nc.scalar.activation(wt_size[:], wt_turned[:, P - BLOCKS : P], ACT.Abs)
         nc.scalar.activation(wt_flip[:], wt_turned[:, P - BLOCKS : P], ACT.Sign, scale=-1.0)
+        nc.scalar.activation(wt_minus[:], wt_size[:], ACT.Copy, scale=-1.0)
 
         ts_listed = keep.tile([P, N], F32, name="ts_listed")
         nc.vector.tensor_copy(ts_listed[:], ts_window[:].indirect(offsets[:]))
@@ -156,9 +156,7 @@ def tile_attend_gsqh_x_ts_kernel(tc, xT, wT, y, wt, ts, offs, out):
 
         x_scales = keep.tile([P, R], U8, name="x_scales", align_bytes=64)
         h_scales = keep.tile([P, R], U8, name="h_scales", align_bytes=64)
-        h_grouped = [
-            keep.tile([P, P * PACK], BF16, name="h_grouped%d" % b, align_bytes=64) for b in range(BLOCKS)
-        ]
+        h_grouped = {}
         result = [keep.tile([P, D], F32, name="result%d" % b) for b in range(BLOCKS)]
         x_grouped = {}
         x_codes = {}
@@ -172,10 +170,16 @@ def tile_attend_gsqh_x_ts_kernel(tc, xT, wT, y, wt, ts, offs, out):
         h_turned = {}
 
         pair_tag = ["pair0", "pair1", "slot0", "signed0"]
-        h_tag = {0: "pair1", 2: "signed0", GPSIMD_BLOCKS: "slack%d" % (GPSIMD_BLOCKS - 1)}
+        h_tag = {0: "pair1", 2: "signed0", 4: "margin0"}
 
         def rows_of(b, count):
             return slice(b * P, (b + count) * P)
+
+        def split(slots):
+            return slots.rearrange("p (s u e) -> p u s e", u=2, e=2)
+
+        def in_order(slots):
+            return slots.rearrange("p (u s e) -> p u s e", u=2, e=2)
 
         def group_x(b):
             raw, first = x_raw[b]
@@ -206,12 +210,10 @@ def tile_attend_gsqh_x_ts_kernel(tc, xT, wT, y, wt, ts, offs, out):
             raw, first = y_raw[b]
             tag = "margin%d" % (b - 3) if b >= 3 else "signed%d" % b
             signed[b] = shared([P, N], F32, "signed%d" % b, tag)
-            nc.vector.scalar_tensor_tensor(
-                signed[b][:], raw[:, first, :], wt_flip[:, b : b + 1], ts_rows[:], MULT, MULT
-            )
+            nc.vector.tensor_tensor(in_order(signed[b][:]), split(raw[:, first, :]), split(ts_rows[:]), MULT)
 
         def scores(b):
-            raw_a[b] = psum.tile([P, N], F32, name="raw_a", bufs=2)
+            raw_a[b] = psum.tile([P, N], F32, name="raw_a", tag="raw_a", bufs=2)
             nc.tensor.matmul_mx(
                 out=raw_a[b][:],
                 lhsT=words(x_codes, b, 1).bitcast(E4M3),
@@ -224,10 +226,10 @@ def tile_attend_gsqh_x_ts_kernel(tc, xT, wT, y, wt, ts, offs, out):
 
         def margins(b):
             margin[b] = shared([P, N], F32, "margin%d" % b, "margin%d" % b)
-            nc.vector.tensor_tensor(margin[b][:], raw_a[b][:], signed[b][:], MULT)
+            nc.vector.tensor_tensor(in_order(margin[b][:]), in_order(signed[b][:]), split(raw_a[b][:]), MULT)
             slack[b] = shared([P, N], F32, "slack%d" % b, "slack%d" % b)
             nc.scalar.activation(
-                slack[b][:], margin[b][:], ACT.Relu, bias=wt_size[:, b : b + 1], scale=wt_cols[:, b : b + 1]
+                slack[b][:], margin[b][:], ACT.Relu, bias=wt_size[:, b : b + 1], scale=wt_minus[:, b : b + 1]
             )
 
         def gradient(b):
@@ -239,7 +241,8 @@ def tile_attend_gsqh_x_ts_kernel(tc, xT, wT, y, wt, ts, offs, out):
             h_turned[b] = psum.tile([P, 2, P], F32, name="h_turned", tag="turn", bufs=2)
             h_words = h[b][:].bitcast(F32)
             for u in range(2):
-                nc.tensor.transpose(h_turned[b][:, u, :], h_words[:, u : 2 * P : 2], ident_f32[:])
+                nc.tensor.transpose(h_turned[b][:, u, :], h_words[:, u * P : (u + 1) * P], ident_f32[:])
+            h_grouped[b] = shared([P, P * PACK], BF16, "h_grouped%d" % b, "h_grouped%d" % b)
             copy(
                 h_grouped[b][:].bitcast(F32).rearrange("s (r u) -> s r u", u=2),
                 h_turned[b][:].rearrange("s u r -> s r u"),
@@ -249,7 +252,10 @@ def tile_attend_gsqh_x_ts_kernel(tc, xT, wT, y, wt, ts, offs, out):
             nc.vector.quantize_mx(
                 out=words(h_codes, b, 1).bitcast(E5M2), scales=h_scales[:, rows_of(b, 1)], in_=h_grouped[b][:]
             )
-            sums[b] = psum.tile([P, D], F32, name="sums", tag="sums", bufs=3)
+            if b in (4, 5):
+                sums[b] = psum.tile([P, D], F32, name="sums_late", tag="raw_a", bufs=2)
+            else:
+                sums[b] = psum.tile([P, D], F32, name="sums", tag="sums", bufs=3)
             nc.tensor.matmul_mx(
                 out=sums[b][:],
                 lhsT=words(h_codes, b, 1).bitcast(E5M2),
@@ -260,13 +266,16 @@ def tile_attend_gsqh_x_ts_kernel(tc, xT, wT, y, wt, ts, offs, out):
                 stop=True,
             )
 
-        def store(b, copy, pieces):
+        def store(b, by_vector, pieces):
             width = P // pieces
             for first in range(0, P, width):
                 cols = slice(first * PACK, (first + width) * PACK)
                 ordered = result[b][:, cols].rearrange("r (p t) -> r p t", t=PACK)
                 turned = sums[b][:].rearrange("r (t p) -> r p t", t=PACK)[:, first : first + width, :]
-                copy(ordered, turned)
+                if by_vector:
+                    nc.vector.tensor_scalar(ordered, turned, wt_flip[:, b : b + 1], None, MULT)
+                else:
+                    nc.scalar.activation(ordered, turned, ACT.Copy, scale=wt_flip[:, b : b + 1])
                 nc.sync.dma_start(out[0, rows_of(b, 1), cols], result[b][:, cols])
 
         on_scalar = nc.scalar.copy
@@ -306,32 +315,35 @@ def tile_attend_gsqh_x_ts_kernel(tc, xT, wT, y, wt, ts, offs, out):
         gradient(2)
         gradient(3)
         turn_h(1, on_scalar)
-        store(0, on_scalar, 1)
+        store(0, False, 1)
         for b in range(4, BLOCKS):
             scores(b)
             if b + 1 < BLOCKS:
                 sign_scales(b + 1)
             margins(b)
-            if b < GPSIMD_BLOCKS:
-                gradient(b)
-            if b in (5, 6):
-                turn_h(b - 3, on_scalar)
-        code_space(h_codes, "h_codes_rest", 1, BLOCKS - 1, "margin1")
-        for b in range(1, 4):
-            product(b)
-            gradient(b + 4)
+            if b == 5:
+                turn_h(2, on_scalar)
+        code_space(h_codes, "h_codes_rest", 1, BLOCKS - 1, "slack3")
+        product(1)
+        product(2)
+        gradient(4)
+        turn_h(3, on_scalar)
+        store(1, False, 1)
+        gradient(5)
         turn_h(4, on_scalar)
-        store(1, on_scalar, 1)
+        product(3)
+        store(2, False, 1)
+        gradient(6)
+        gradient(7)
+        turn_h(5, on_scalar)
         product(4)
-        turn_h(5, on_vector)
-        store(2, on_scalar, 1)
+        store(3, False, 1)
         turn_h(6, on_vector)
         product(5)
-        store(3, on_scalar, 1)
+        store(4, False, 1)
         turn_h(7, on_vector)
         product(6)
-        store(4, on_scalar, 1)
+        store(5, False, 1)
         product(7)
-        store(5, on_scalar, 1)
-        store(6, on_scalar, 1)
-        store(7, on_vector, 2)
+        store(6, False, 1)
+        store(7, True, 2)

@@ -36,7 +36,7 @@ def tile_attend_gsqh_x_ts_kernel(tc, xT, wT, y, wt, ts, offs, out):
         offsets = keep.tile([P, N // 16], U16, name="offsets")
         nc.sync.dma_start(offsets[:], offs)
 
-        wt_rows = stage.tile([P, P], F32, name="wt_rows", tag="slot3", align_bytes=64)
+        wt_rows = keep.tile([P, P], F32, name="wt_rows")
         nc.sync.dma_start(wt_rows[P - BLOCKS : P, :], wt[0].rearrange("(b p) o -> b (p o)", p=P))
         ts_window = keep.tile([P, T], F32, name="ts_window")
         nc.sync.dma_start(ts_window[P - 1 : P, :], ts[0:1, :])
@@ -51,7 +51,7 @@ def tile_attend_gsqh_x_ts_kernel(tc, xT, wT, y, wt, ts, offs, out):
             nc.sync.dma_start(plane[:], w_rows[:, t, :])
             w_planes.append(plane)
 
-        for t in range(PACK - 1):
+        for t in range(PACK):
             load_plane(t)
 
         x_rows = xT[0].rearrange("(p t) r -> p t r", t=PACK)
@@ -77,9 +77,8 @@ def tile_attend_gsqh_x_ts_kernel(tc, xT, wT, y, wt, ts, offs, out):
         ident_bf16 = keep.tile([P, P], BF16, name="ident_bf16")
         make_identity(nc, ident_bf16[:])
 
-        wt_turned = psum.tile([P, P], F32, name="wt_turned", tag="turn", bufs=2)
+        wt_turned = psum.tile([P, P], F32, name="wt_turned", tag="bank1")
         nc.tensor.transpose(wt_turned[:], wt_rows[:], ident_f32[:])
-        load_plane(PACK - 1)
         wt_minus = keep.tile([P, BLOCKS], F32, name="wt_minus")
         wt_size = keep.tile([P, BLOCKS], F32, name="wt_size")
         wt_flip = keep.tile([P, BLOCKS], F32, name="wt_flip")
@@ -89,12 +88,12 @@ def tile_attend_gsqh_x_ts_kernel(tc, xT, wT, y, wt, ts, offs, out):
 
         ts_listed = keep.tile([P, N], F32, name="ts_listed")
         nc.vector.tensor_copy(ts_listed[:], ts_window[:].indirect(offsets[:]))
-        ts_turned = psum.tile([P, PACK, P], F32, name="ts_turned", tag="turn", bufs=2)
+        ts_turned = psum.tile([P, PACK, P], F32, name="ts_turned", tag="bank2")
         for q in range(PACK):
             nc.tensor.transpose(ts_turned[:, q, :], ts_listed[:, q * P : (q + 1) * P], ident_f32[:])
         ts_cols = keep.tile([P, PACK], F32, name="ts_cols")
         nc.scalar.copy(ts_cols[:], ts_turned[:, :, P - 1])
-        ts_rows = psum.tile([P, N], F32, name="ts_rows")
+        ts_rows = psum.tile([P, N], F32, name="ts_rows", tag="bank0")
         for q in range(PACK):
             nc.tensor.transpose(
                 ts_rows[:, q * P : (q + 1) * P],
@@ -104,32 +103,19 @@ def tile_attend_gsqh_x_ts_kernel(tc, xT, wT, y, wt, ts, offs, out):
 
         w_by_d = keep.tile([P, N, PACK], BF16, name="w_by_d", align_bytes=64)
         w_quads = w_by_d[:].rearrange("p (s j) t -> p j t s", j=PACK)
-        w2_codes = keep.tile([P, D], U32, name="w2_codes", align_bytes=64)
+        w_by_slot = keep.tile([P, PACK, P, PACK], BF16, name="w_by_slot", align_bytes=64)
         w2_scales = keep.tile([P, D], U8, name="w2_scales", align_bytes=64)
-        w_turned = {}
 
-        def gather_w(t):
-            nc.vector.tensor_copy(w_by_d[:, :, t], w_planes[t][:].indirect(offsets[:]))
-            w_turned[t] = psum.tile([P, PACK, P], BF16, name="w_turned", tag="sums", bufs=3)
+        def turn_w(t, bank):
+            w_turned = psum.tile([P, PACK, P], BF16, name="w_turned%d" % t, tag=bank)
             for j in range(PACK):
-                nc.tensor.transpose(w_turned[t][:, j, :], w_quads[:, j, t, :], ident_bf16[:])
+                nc.tensor.transpose(w_turned[:, j, :], w_quads[:, j, t, :], ident_bf16[:])
+            nc.scalar.copy(w_by_slot[:, t, :, :], w_turned[:].rearrange("s j p -> s p j"))
 
-        def quantize_w2(half, w_by_slot):
-            for e in range(2):
-                nc.scalar.copy(w_by_slot[:, e, :, :], w_turned[2 * half + e][:].rearrange("s j p -> s p j"))
-            cols = slice(half * 2 * P, (half + 1) * 2 * P)
-            nc.vector.quantize_mx(
-                out=w2_codes[:, cols].bitcast(E4M3),
-                scales=w2_scales[:, cols],
-                in_=w_by_slot[:].rearrange("s e p j -> s (e p j)"),
-            )
-
-        gather_w(0)
-        gather_w(1)
-        gather_w(2)
-        w_first_half = keep.tile([P, 2, P, PACK], BF16, name="w_first_half", align_bytes=64)
-        quantize_w2(0, w_first_half)
-        gather_w(3)
+        for t in range(PACK):
+            nc.vector.tensor_copy(w_by_d[:, :, t], w_planes[t][:].indirect(offsets[:]))
+            if t < PACK - 1:
+                turn_w(t, "bank%d" % (t + 1))
 
         x_first = stage.tile([P, CHUNK], F32, name="x_first", tag="slot0", align_bytes=64)
         y_first = stage.tile([P, CHUNK], F32, name="y_first", tag="slot1", align_bytes=64)
@@ -160,6 +146,7 @@ def tile_attend_gsqh_x_ts_kernel(tc, xT, wT, y, wt, ts, offs, out):
         result = [keep.tile([P, D], F32, name="result%d" % b) for b in range(BLOCKS)]
         x_grouped = {}
         x_codes = {}
+        late_codes = {}
         h_codes = {}
         signed = {}
         margin = {}
@@ -169,8 +156,10 @@ def tile_attend_gsqh_x_ts_kernel(tc, xT, wT, y, wt, ts, offs, out):
         raw_a = {}
         h_turned = {}
 
-        pair_tag = ["pair0", "pair1", "slot0", "signed0"]
-        h_tag = {0: "pair1", 2: "signed0", 4: "margin0"}
+        pair_tag = ["pair0", "pair1", "margin0", "signed0"]
+        raw_bank = ["bank1", "bank2", "bank3", "bank2", "bank3", "bank2", "bank3", "bank2"]
+        sums_bank = ["bank1", "bank6", "bank7", "bank1", "bank3", "bank2", "bank6", "bank7"]
+        h_tag = {0: "pair1", 2: "signed0", 4: "signed3"}
 
         def rows_of(b, count):
             return slice(b * P, (b + count) * P)
@@ -208,12 +197,12 @@ def tile_attend_gsqh_x_ts_kernel(tc, xT, wT, y, wt, ts, offs, out):
 
         def sign_scales(b):
             raw, first = y_raw[b]
-            tag = "margin%d" % (b - 3) if b >= 3 else "signed%d" % b
+            tag = "margin%d" % (b - 3) if b >= 4 else "signed%d" % b
             signed[b] = shared([P, N], F32, "signed%d" % b, tag)
             nc.vector.tensor_tensor(in_order(signed[b][:]), split(raw[:, first, :]), split(ts_rows[:]), MULT)
 
         def scores(b):
-            raw_a[b] = psum.tile([P, N], F32, name="raw_a", tag="raw_a", bufs=2)
+            raw_a[b] = psum.tile([P, N], F32, name="raw_a%d" % b, tag=raw_bank[b])
             nc.tensor.matmul_mx(
                 out=raw_a[b][:],
                 lhsT=words(x_codes, b, 1).bitcast(E4M3),
@@ -252,15 +241,12 @@ def tile_attend_gsqh_x_ts_kernel(tc, xT, wT, y, wt, ts, offs, out):
             nc.vector.quantize_mx(
                 out=words(h_codes, b, 1).bitcast(E5M2), scales=h_scales[:, rows_of(b, 1)], in_=h_grouped[b][:]
             )
-            if b in (4, 5):
-                sums[b] = psum.tile([P, D], F32, name="sums_late", tag="raw_a", bufs=2)
-            else:
-                sums[b] = psum.tile([P, D], F32, name="sums", tag="sums", bufs=3)
+            sums[b] = psum.tile([P, D], F32, name="sums%d" % b, tag=sums_bank[b])
             nc.tensor.matmul_mx(
                 out=sums[b][:],
                 lhsT=words(h_codes, b, 1).bitcast(E5M2),
                 lhsT_scale=h_scales[:, rows_of(b, 1)],
-                rhs=w2_codes[:].bitcast(E4M3),
+                rhs=words(late_codes, 4, 4).bitcast(E4M3),
                 rhs_scale=w2_scales[:],
                 start=True,
                 stop=True,
@@ -290,9 +276,9 @@ def tile_attend_gsqh_x_ts_kernel(tc, xT, wT, y, wt, ts, offs, out):
         margins(0)
         sign_scales(1)
         scores(1)
+        turn_w(PACK - 1, "bank1")
         group_x(2)
         group_x(3)
-        quantize_w2(1, shared([P, 2, P, PACK], BF16, "w_second_half", "slot0"))
         quantize_x(2, 2)
         gradient(0)
         margins(1)
@@ -307,9 +293,16 @@ def tile_attend_gsqh_x_ts_kernel(tc, xT, wT, y, wt, ts, offs, out):
         group_x(7)
         sign_scales(4)
         turn_h(0, on_scalar)
+        code_space(late_codes, "late_codes", 0, 8, "slack1")
+        for k in range(4):
+            x_codes[4 + k] = late_codes[k]
+        nc.vector.quantize_mx(
+            out=words(late_codes, 4, 4).bitcast(E4M3),
+            scales=w2_scales[:],
+            in_=w_by_slot[:].rearrange("s t p j -> s (t p j)"),
+        )
         code_space(h_codes, "h_codes_first", 0, 1, "signed1")
         product(0)
-        code_space(x_codes, "x_codes_late", 4, 4, "slack1")
         quantize_x(4, 2)
         quantize_x(6, 2)
         gradient(2)

@@ -9,7 +9,7 @@ PACK = 4
 BLOCKS = R // P
 X_CHUNKS = [(0, 256), (256, 512), (512, 768), (768, 1024)]
 Y_ROWS = 256
-GPSIMD_BLOCKS = 4
+GPSIMD_BLOCKS = 5
 CHUNK = 1024
 
 FLOPS = 2 * 2 * R * N * D
@@ -143,7 +143,7 @@ def tile_attend_gsqh_x_ts_kernel(tc, xT, wT, y, wt, ts, offs, out):
         x_scales = keep.tile([P, R], U8, name="x_scales", align_bytes=64)
         h_scales = keep.tile([P, R], U8, name="h_scales", align_bytes=64)
         h_grouped = {}
-        result = [keep.tile([P, D], F32, name="result%d" % b) for b in range(BLOCKS)]
+        result = {}
         x_grouped = {}
         x_codes = {}
         late_codes = {}
@@ -159,7 +159,7 @@ def tile_attend_gsqh_x_ts_kernel(tc, xT, wT, y, wt, ts, offs, out):
         pair_tag = ["pair0", "pair1", "margin0", "signed0"]
         raw_bank = ["bank1", "bank2", "bank3", "bank2", "bank3", "bank2", "bank3", "bank2"]
         sums_bank = ["bank1", "bank6", "bank7", "bank1", "bank3", "bank2", "bank6", "bank7"]
-        h_tag = {0: "pair1", 2: "signed0", 4: "signed3"}
+        h_tag = {0: "pair1", 3: "signed0", 5: "margin1"}
 
         def rows_of(b, count):
             return slice(b * P, (b + count) * P)
@@ -197,7 +197,7 @@ def tile_attend_gsqh_x_ts_kernel(tc, xT, wT, y, wt, ts, offs, out):
 
         def sign_scales(b):
             raw, first = y_raw[b]
-            tag = "margin%d" % (b - 3) if b >= 4 else "signed%d" % b
+            tag = "margin%d" % (b - 3) if 4 <= b <= 6 else "signed%d" % b
             signed[b] = shared([P, N], F32, "signed%d" % b, tag)
             nc.vector.tensor_tensor(in_order(signed[b][:]), split(raw[:, first, :]), split(ts_rows[:]), MULT)
 
@@ -254,6 +254,7 @@ def tile_attend_gsqh_x_ts_kernel(tc, xT, wT, y, wt, ts, offs, out):
 
         def store(b, by_vector, pieces):
             width = P // pieces
+            result[b] = shared([P, D], F32, "result%d" % b, "margin%d" % (b + 4) if b < 2 else "result%d" % b)
             for first in range(0, P, width):
                 cols = slice(first * PACK, (first + width) * PACK)
                 ordered = result[b][:, cols].rearrange("r (p t) -> r p t", t=PACK)
@@ -289,42 +290,47 @@ def tile_attend_gsqh_x_ts_kernel(tc, xT, wT, y, wt, ts, offs, out):
             scores(b)
             sign_scales(b)
             margins(b)
+        gradient(2)
         group_x(6)
         group_x(7)
         sign_scales(4)
+        sign_scales(5)
         turn_h(0, on_scalar)
-        code_space(late_codes, "late_codes", 0, 8, "slack1")
+        turn_h(1, on_scalar)
+        code_space(late_codes, "late_codes", 0, 8, "slack2")
         for k in range(4):
             x_codes[4 + k] = late_codes[k]
+        quantize_x(4, 2)
+        scores(4)
+        scores(5)
         nc.vector.quantize_mx(
             out=words(late_codes, 4, 4).bitcast(E4M3),
             scales=w2_scales[:],
             in_=w_by_slot[:].rearrange("s t p j -> s (t p j)"),
         )
-        code_space(h_codes, "h_codes_first", 0, 1, "signed1")
+        code_space(h_codes, "h_codes_first", 0, 2, "signed2")
         product(0)
-        quantize_x(4, 2)
-        quantize_x(6, 2)
-        gradient(2)
-        gradient(3)
-        turn_h(1, on_scalar)
-        store(0, False, 1)
-        for b in range(4, BLOCKS):
-            scores(b)
-            if b + 1 < BLOCKS:
-                sign_scales(b + 1)
-            margins(b)
-            if b == 5:
-                turn_h(2, on_scalar)
-        code_space(h_codes, "h_codes_rest", 1, BLOCKS - 1, "slack3")
         product(1)
-        product(2)
+        quantize_x(6, 2)
+        gradient(3)
+        margins(4)
         gradient(4)
-        turn_h(3, on_scalar)
+        sign_scales(6)
+        margins(5)
+        store(0, False, 1)
+        turn_h(2, on_scalar)
+        scores(6)
+        sign_scales(7)
+        margins(6)
         store(1, False, 1)
+        scores(7)
+        margins(7)
+        turn_h(3, on_vector)
+        code_space(h_codes, "h_codes_rest", 2, BLOCKS - 2, "slack4")
+        product(2)
+        product(3)
         gradient(5)
         turn_h(4, on_scalar)
-        product(3)
         store(2, False, 1)
         gradient(6)
         gradient(7)

@@ -6,11 +6,10 @@ from concourse.masks import make_identity
 D, T, N, R = 512, 2048, 512, 1024
 P = 128
 PACK = 4
+RUN = 8
 BLOCKS = R // P
-X_CHUNKS = [(0, 256), (256, 512), (512, 768), (768, 1024)]
-Y_ROWS = 256
-GPSIMD_BLOCKS = 5
-CHUNK = 1024
+CHUNK_ROWS = 256
+CHUNK_BLOCKS = CHUNK_ROWS // P
 
 FLOPS = 2 * 2 * R * N * D
 BYTES = 4 * (D * R + D * T + R * N + R + T + R * D) + 2 * P * (N // 16)
@@ -23,6 +22,7 @@ U8 = mybir.dt.uint8
 E4M3 = mybir.dt.float8_e4m3fn_x4
 E5M2 = mybir.dt.float8_e5m2_x4
 MULT = mybir.AluOpType.mult
+ADD = mybir.AluOpType.add
 ACT = mybir.ActivationFunctionType
 
 
@@ -30,319 +30,306 @@ def tile_attend_gsqh_x_ts_kernel(tc, xT, wT, y, wt, ts, offs, out):
     nc = tc.nc
     with ExitStack() as ctx:
         keep = ctx.enter_context(tc.tile_pool(name="keep", bufs=1))
-        stage = ctx.enter_context(tc.tile_pool(name="stage", bufs=1))
         psum = ctx.enter_context(tc.psum_pool(name="psum", bufs=1))
+
+        def sbuf(shape, dtype, name, tag=None):
+            return keep.tile(shape, dtype, name=name, tag=tag or name, align_bytes=64)
+
+        def bank(shape, dtype, name, index):
+            return psum.tile(shape, dtype, name=name, tag="bank%d" % index)
 
         offsets = keep.tile([P, N // 16], U16, name="offsets")
         nc.sync.dma_start(offsets[:], offs)
 
-        wt_rows = keep.tile([P, P], F32, name="wt_rows")
+        wt_rows = sbuf([P, P], F32, "wt_rows")
         nc.sync.dma_start(wt_rows[P - BLOCKS : P, :], wt[0].rearrange("(b p) o -> b (p o)", p=P))
-        ts_window = keep.tile([P, T], F32, name="ts_window")
+        ts_window = sbuf([P, T], F32, "ts_window")
         nc.sync.dma_start(ts_window[P - 1 : P, :], ts[0:1, :])
         nc.vector.memset(wt_rows[0 : P - BLOCKS, :], 0.0)
         nc.vector.memset(ts_window[0 : P - 1, :], 0.0)
 
-        w_rows = wT.rearrange("(p t) c -> p t c", t=PACK)
+        w_rows = wT.rearrange("(p f) c -> p f c", f=PACK)
         w_planes = []
-
-        def load_plane(t):
-            plane = stage.tile([P, T], F32, name="w_plane%d" % t, tag="slot%d" % t, align_bytes=64)
-            nc.sync.dma_start(plane[:], w_rows[:, t, :])
+        for f in range(PACK):
+            plane = sbuf([P, T], F32, "w_plane%d" % f)
+            nc.sync.dma_start(plane[:], w_rows[:, f, :])
             w_planes.append(plane)
 
-        for t in range(PACK):
-            load_plane(t)
-
-        x_rows = xT[0].rearrange("(p t) r -> p t r", t=PACK)
-        y_rows = y[0].rearrange("(k j p) i -> k p j i", p=P, j=Y_ROWS // P)
+        x_rows = xT[0].rearrange("(p f) r -> p f r", f=PACK)
+        y_rows = y[0].rearrange("(k j p) i -> k p j i", p=P, j=CHUNK_BLOCKS)
         x_raw = {}
         y_raw = {}
 
-        def load_x(k, space):
-            lo, hi = X_CHUNKS[k]
-            raw = space.rearrange("p (t r) -> p t r", t=PACK)
-            nc.sync.dma_start(raw, x_rows[:, :, lo:hi])
-            for b in range(lo // P, hi // P):
-                x_raw[b] = (raw, b * P - lo)
+        def load_x(k):
+            x_raw[k] = sbuf([P, PACK, CHUNK_ROWS], F32, "x_raw%d" % k)
+            nc.sync.dma_start(x_raw[k][:], x_rows[:, :, k * CHUNK_ROWS : (k + 1) * CHUNK_ROWS])
 
-        def load_y(k, space):
-            raw = space.rearrange("p (j i) -> p j i", i=N)
-            nc.sync.dma_start(raw, y_rows[k])
-            for j in range(Y_ROWS // P):
-                y_raw[k * (Y_ROWS // P) + j] = (raw, j)
+        def load_y(k):
+            y_raw[k] = sbuf([P, CHUNK_BLOCKS, N], F32, "y_raw%d" % k)
+            nc.sync.dma_start(y_raw[k][:], y_rows[k])
 
-        ident_f32 = keep.tile([P, P], F32, name="ident_f32")
+        load_x(0)
+        for k in range(1, R // CHUNK_ROWS):
+            load_x(k)
+            load_y(k - 1)
+        load_y(R // CHUNK_ROWS - 1)
+
+        ident_f32 = sbuf([P, P], F32, "ident_f32")
         make_identity(nc, ident_f32[:])
-        ident_bf16 = keep.tile([P, P], BF16, name="ident_bf16")
+        ident_bf16 = sbuf([P, P], BF16, "ident_bf16")
         make_identity(nc, ident_bf16[:])
 
-        wt_turned = psum.tile([P, P], F32, name="wt_turned", tag="bank1")
-        nc.tensor.transpose(wt_turned[:], wt_rows[:], ident_f32[:])
-        wt_minus = keep.tile([P, BLOCKS], F32, name="wt_minus")
-        wt_size = keep.tile([P, BLOCKS], F32, name="wt_size")
-        wt_flip = keep.tile([P, BLOCKS], F32, name="wt_flip")
-        nc.scalar.activation(wt_size[:], wt_turned[:, P - BLOCKS : P], ACT.Abs)
-        nc.scalar.activation(wt_flip[:], wt_turned[:, P - BLOCKS : P], ACT.Sign, scale=-1.0)
-        nc.scalar.activation(wt_minus[:], wt_size[:], ACT.Copy, scale=-1.0)
+        def dealt(slots):
+            return slots.rearrange("p (g t j) -> p t g j", t=PACK, j=RUN)
 
-        ts_listed = keep.tile([P, N], F32, name="ts_listed")
+        def as_dealt(slots):
+            return slots.rearrange("p (t g j) -> p t g j", t=PACK, j=RUN)
+
+        wt_turned = bank([P, P], F32, "wt_turned", 4)
+        nc.tensor.transpose(wt_turned[:], wt_rows[:], ident_f32[:])
+        wt_minus = sbuf([P, BLOCKS], F32, "wt_minus")
+        nc.scalar.activation(wt_minus[:], wt_turned[:, P - BLOCKS : P], ACT.Copy, scale=-1.0)
+
+        ts_listed = sbuf([P, N], F32, "ts_listed")
         nc.vector.tensor_copy(ts_listed[:], ts_window[:].indirect(offsets[:]))
-        ts_turned = psum.tile([P, PACK, P], F32, name="ts_turned", tag="bank2")
-        for q in range(PACK):
-            nc.tensor.transpose(ts_turned[:, q, :], ts_listed[:, q * P : (q + 1) * P], ident_f32[:])
-        ts_cols = keep.tile([P, PACK], F32, name="ts_cols")
-        nc.scalar.copy(ts_cols[:], ts_turned[:, :, P - 1])
-        ts_rows = psum.tile([P, N], F32, name="ts_rows", tag="bank0")
-        for q in range(PACK):
-            nc.tensor.transpose(
-                ts_rows[:, q * P : (q + 1) * P],
-                ts_cols[:, q : q + 1].to_broadcast([P, P]),
-                ident_f32[:],
+        ts_dealt = sbuf([P, N], F32, "ts_dealt")
+        nc.scalar.copy(as_dealt(ts_dealt[:]), dealt(ts_listed[:]))
+        ts_turned = bank([P, PACK, P], F32, "ts_turned", 5)
+        for t in range(PACK):
+            nc.tensor.transpose(ts_turned[:, t, :], ts_dealt[:, t * P : (t + 1) * P], ident_f32[:])
+        ts_size = sbuf([P, PACK], F32, "ts_size")
+        ts_sign = sbuf([P, PACK], F32, "ts_sign")
+        ts_minus = sbuf([P, PACK], F32, "ts_minus")
+        ts_slope = sbuf([P, PACK], F32, "ts_slope")
+        nc.scalar.activation(ts_sign[:], ts_turned[:, :, P - 1], ACT.Sign)
+        nc.scalar.activation(ts_size[:], ts_turned[:, :, P - 1], ACT.Abs)
+        nc.scalar.activation(ts_minus[:], ts_turned[:, :, P - 1], ACT.Copy, scale=-1.0)
+        nc.gpsimd.tensor_tensor(ts_slope[:], ts_minus[:], ts_size[:], MULT)
+
+        w_by_d = sbuf([P, N, PACK], BF16, "w_by_d")
+        w_listed = w_by_d[:].rearrange("p (t g j) f -> p f g t j", t=PACK, j=RUN)
+        w_by_slot = sbuf([P, PACK, P, PACK], BF16, "w_by_slot")
+        w_turned = {}
+
+        def turn_w(f, index):
+            w_turned[f] = bank([P, PACK, P], BF16, "w_turned%d" % f, index)
+            for t in range(PACK):
+                nc.tensor.transpose(w_turned[f][:, t, :], w_by_d[:, t * P : (t + 1) * P, f], ident_bf16[:])
+
+        def sign_w_scalar(f):
+            for t in range(PACK):
+                nc.scalar.activation(
+                    w_by_slot[:, f, :, t], w_turned[f][:, t, :], ACT.Copy, scale=ts_sign[:, t : t + 1]
+                )
+
+        def sign_w_vector(f):
+            nc.vector.tensor_tensor(
+                w_by_slot[:, f, :, :],
+                ts_sign[:].unsqueeze(1).to_broadcast([P, P, PACK]),
+                w_turned[f][:].rearrange("s t p -> s p t"),
+                MULT,
             )
 
-        w_by_d = keep.tile([P, N, PACK], BF16, name="w_by_d", align_bytes=64)
-        w_quads = w_by_d[:].rearrange("p (s j) t -> p j t s", j=PACK)
-        w_by_slot = keep.tile([P, PACK, P, PACK], BF16, name="w_by_slot", align_bytes=64)
-        w2_scales = keep.tile([P, D], U8, name="w2_scales", align_bytes=64)
+        for f in range(PACK):
+            nc.vector.tensor_copy(w_listed[:, f], w_planes[f][:].indirect(offsets[:]))
+            if f < PACK - 1:
+                turn_w(f, (2, 3, 7)[f])
+                sign_w_scalar(f)
 
-        def turn_w(t, bank):
-            w_turned = psum.tile([P, PACK, P], BF16, name="w_turned%d" % t, tag=bank)
-            for j in range(PACK):
-                nc.tensor.transpose(w_turned[:, j, :], w_quads[:, j, t, :], ident_bf16[:])
-            nc.scalar.copy(w_by_slot[:, t, :, :], w_turned[:].rearrange("s j p -> s p j"))
-
-        for t in range(PACK):
-            nc.vector.tensor_copy(w_by_d[:, :, t], w_planes[t][:].indirect(offsets[:]))
-            if t < PACK - 1:
-                turn_w(t, "bank%d" % (t + 1))
-
-        x_first = stage.tile([P, CHUNK], F32, name="x_first", tag="slot0", align_bytes=64)
-        y_first = stage.tile([P, CHUNK], F32, name="y_first", tag="slot1", align_bytes=64)
-        x_second = stage.tile([P, CHUNK], F32, name="x_second", tag="slot2", align_bytes=64)
-        later = stage.tile([P, 5 * CHUNK], F32, name="later", tag="slot3", align_bytes=64)
-        load_x(0, x_first[:])
-        load_y(0, y_first[:])
-        load_x(1, x_second[:])
-        load_y(1, later[:, 0:CHUNK])
-        for k in range(2, 4):
-            load_x(k, later[:, (2 * k - 3) * CHUNK : (2 * k - 2) * CHUNK])
-            load_y(k, later[:, (2 * k - 2) * CHUNK : (2 * k - 1) * CHUNK])
-
-        w1_codes = keep.tile([P, N], U32, name="w1_codes", align_bytes=64)
-        w1_scales = keep.tile([P, N], U8, name="w1_scales", align_bytes=64)
+        w1_codes = sbuf([P, N], U32, "w1_codes")
+        w1_scales = sbuf([P, N], U8, "w1_scales")
         nc.vector.quantize_mx(
             out=w1_codes[:].bitcast(E4M3),
             scales=w1_scales[:],
-            in_=w_by_d[:].rearrange("p i t -> p (i t)"),
+            in_=w_by_d[:].rearrange("p i f -> p (i f)"),
         )
+        w2_codes = sbuf([P, D], U32, "w2_codes")
+        w2_scales = sbuf([P, D], U8, "w2_scales")
 
-        def shared(shape, dtype, name, tag):
-            return stage.tile(shape, dtype, name=name, tag=tag, align_bytes=64)
+        def quantize_w2():
+            nc.vector.quantize_mx(
+                out=w2_codes[:].bitcast(E4M3),
+                scales=w2_scales[:],
+                in_=w_by_slot[:].rearrange("s f p t -> s (f p t)"),
+            )
 
-        x_scales = keep.tile([P, R], U8, name="x_scales", align_bytes=64)
-        h_scales = keep.tile([P, R], U8, name="h_scales", align_bytes=64)
-        h_grouped = {}
-        result = {}
+        x_codes = sbuf([P, R], U32, "x_codes")
+        x_scales = sbuf([P, R], U8, "x_scales")
+        h_codes = sbuf([P, R], U32, "h_codes")
+        h_scales = sbuf([P, R], U8, "h_scales")
         x_grouped = {}
-        x_codes = {}
-        late_codes = {}
-        h_codes = {}
-        signed = {}
-        margin = {}
+        raw = {}
+        flipped = {}
+        flipped_turned = {}
+        weighted = {}
+        weighted_turned = {}
         slack = {}
-        h = {}
+        h_grouped = {}
         sums = {}
-        raw_a = {}
-        h_turned = {}
 
-        pair_tag = ["pair0", "pair1", "margin0", "signed0"]
-        raw_bank = ["bank1", "bank2", "bank3", "bank2", "bank3", "bank2", "bank3", "bank2"]
-        sums_bank = ["bank1", "bank6", "bank7", "bank1", "bank3", "bank2", "bank6", "bank7"]
-        h_tag = {0: "pair1", 3: "signed0", 5: "margin1"}
-
-        def rows_of(b, count):
+        def rows_of(b, count=1):
             return slice(b * P, (b + count) * P)
 
-        def split(slots):
-            return slots.rearrange("p (s u e) -> p u s e", u=2, e=2)
-
-        def in_order(slots):
-            return slots.rearrange("p (u s e) -> p u s e", u=2, e=2)
-
         def group_x(b):
-            raw, first = x_raw[b]
-            if b % 2 == 0:
-                x_grouped[b // 2] = shared([P, 2 * P, PACK], BF16, "x_grouped%d" % b, pair_tag[b // 2])
+            k, j = divmod(b, CHUNK_BLOCKS)
+            if j == 0:
+                x_grouped[k] = sbuf([P, CHUNK_ROWS, PACK], BF16, "x_grouped%d" % k)
             nc.scalar.copy(
-                x_grouped[b // 2][:, rows_of(b % 2, 1), :].rearrange("p (c i) t -> p c t i", i=PACK),
-                raw[:, :, first : first + P].rearrange("p t (c i) -> p c t i", i=PACK),
+                x_grouped[k][:, rows_of(j), :].rearrange("p (c i) f -> p c f i", i=PACK),
+                x_raw[k][:, :, rows_of(j)].rearrange("p f (c i) -> p c f i", i=PACK),
             )
-
-        def code_space(codes, name, first, count, tag):
-            space = shared([P, count * P], U32, name, tag)
-            for k in range(count):
-                codes[first + k] = (space, k)
-
-        def words(codes, b, count):
-            space, k = codes[b]
-            return space[:, rows_of(k, count)]
 
         def quantize_x(b, count):
+            k, j = divmod(b, CHUNK_BLOCKS)
             nc.vector.quantize_mx(
-                out=words(x_codes, b, count).bitcast(E4M3),
+                out=x_codes[:, rows_of(b, count)].bitcast(E4M3),
                 scales=x_scales[:, rows_of(b, count)],
-                in_=x_grouped[b // 2][:, rows_of(b % 2, count), :].rearrange("p r t -> p (r t)"),
+                in_=x_grouped[k][:, rows_of(j, count), :].rearrange("p r f -> p (r f)"),
             )
 
-        def sign_scales(b):
-            raw, first = y_raw[b]
-            tag = "margin%d" % (b - 3) if 4 <= b <= 6 else "signed%d" % b
-            signed[b] = shared([P, N], F32, "signed%d" % b, tag)
-            nc.vector.tensor_tensor(in_order(signed[b][:]), split(raw[:, first, :]), split(ts_rows[:]), MULT)
-
         def scores(b):
-            raw_a[b] = psum.tile([P, N], F32, name="raw_a%d" % b, tag=raw_bank[b])
+            raw[b] = bank([P, N], F32, "raw%d" % b, b % 2)
             nc.tensor.matmul_mx(
-                out=raw_a[b][:],
-                lhsT=words(x_codes, b, 1).bitcast(E4M3),
-                lhsT_scale=x_scales[:, rows_of(b, 1)],
+                out=raw[b][:],
+                lhsT=x_codes[:, rows_of(b)].bitcast(E4M3),
+                lhsT_scale=x_scales[:, rows_of(b)],
                 rhs=w1_codes[:].bitcast(E4M3),
                 rhs_scale=w1_scales[:],
                 start=True,
                 stop=True,
             )
 
-        def margins(b):
-            margin[b] = shared([P, N], F32, "margin%d" % b, "margin%d" % b)
-            nc.vector.tensor_tensor(in_order(margin[b][:]), in_order(signed[b][:]), split(raw_a[b][:]), MULT)
-            slack[b] = shared([P, N], F32, "slack%d" % b, "slack%d" % b)
-            nc.scalar.activation(
-                slack[b][:], margin[b][:], ACT.Relu, bias=wt_size[:, b : b + 1], scale=wt_minus[:, b : b + 1]
-            )
+        def labels(b):
+            k, j = divmod(b, CHUNK_BLOCKS)
+            return dealt(y_raw[k][:, j, :])
+
+        def turn(name, source, index):
+            turned = bank([P, PACK, P], F32, name, index)
+            for t in range(PACK):
+                nc.tensor.transpose(turned[:, t, :], source[:, t * P : (t + 1) * P], ident_f32[:])
+            return turned
+
+        def flip(b):
+            flipped[b] = sbuf([P, N], F32, "flipped%d" % b)
+            nc.vector.tensor_tensor(as_dealt(flipped[b][:]), labels(b), as_dealt(raw[b][:]), MULT)
+
+        def turn_flipped(b):
+            flipped_turned[b] = turn("flipped_turned%d" % b, flipped[b], 2 + b % 2)
+
+        def hinge(b):
+            slack[b] = sbuf([P, PACK, P], F32, "slack%d" % b)
+            for t in range(PACK):
+                nc.scalar.activation(
+                    slack[b][:, t, :],
+                    flipped_turned[b][:, t, :],
+                    ACT.Relu,
+                    bias=ts_size[:, t : t + 1],
+                    scale=ts_slope[:, t : t + 1],
+                )
+
+        weighted_tags = ["weighted0", "x_grouped1", "w_by_slot", "x_grouped2"]
+        weighted_tags.extend("h_grouped%d" % b for b in range(BLOCKS - len(weighted_tags)))
+
+        def weigh(b):
+            weighted[b] = sbuf([P, N], F32, "weighted%d" % b, weighted_tags[b])
+            nc.gpsimd.tensor_scalar(as_dealt(weighted[b][:]), labels(b), wt_minus[:, b : b + 1], 0.0, MULT, ADD)
+
+        def turn_weighted(b):
+            weighted_turned[b] = turn("weighted_turned%d" % b, weighted[b], 4 + b % 2)
 
         def gradient(b):
-            engine = nc.gpsimd if b < GPSIMD_BLOCKS else nc.vector
-            h[b] = shared([P, N], BF16, "h%d" % b, h_tag.get(b, "h%d" % b))
-            engine.tensor_tensor(h[b][:], slack[b][:], signed[b][:], MULT)
+            h_grouped[b] = sbuf([P, P, PACK], BF16, "h_grouped%d" % b)
+            nc.vector.tensor_tensor(
+                h_grouped[b][:].rearrange("s (c i) t -> s c t i", i=PACK),
+                slack[b][:].rearrange("s t (c i) -> s c t i", i=PACK),
+                weighted_turned[b][:].rearrange("s t (c i) -> s c t i", i=PACK),
+                MULT,
+            )
 
-        def turn_h(b, copy):
-            h_turned[b] = psum.tile([P, 2, P], F32, name="h_turned", tag="turn", bufs=2)
-            h_words = h[b][:].bitcast(F32)
-            for u in range(2):
-                nc.tensor.transpose(h_turned[b][:, u, :], h_words[:, u * P : (u + 1) * P], ident_f32[:])
-            h_grouped[b] = shared([P, P * PACK], BF16, "h_grouped%d" % b, "h_grouped%d" % b)
-            copy(
-                h_grouped[b][:].bitcast(F32).rearrange("s (r u) -> s r u", u=2),
-                h_turned[b][:].rearrange("s u r -> s r u"),
+        def quantize_h(b):
+            nc.vector.quantize_mx(
+                out=h_codes[:, rows_of(b)].bitcast(E5M2),
+                scales=h_scales[:, rows_of(b)],
+                in_=h_grouped[b][:].rearrange("s r t -> s (r t)"),
             )
 
         def product(b):
-            nc.vector.quantize_mx(
-                out=words(h_codes, b, 1).bitcast(E5M2), scales=h_scales[:, rows_of(b, 1)], in_=h_grouped[b][:]
-            )
-            sums[b] = psum.tile([P, D], F32, name="sums%d" % b, tag=sums_bank[b])
+            sums[b] = bank([P, D], F32, "sums%d" % b, 6 + b % 2)
             nc.tensor.matmul_mx(
                 out=sums[b][:],
-                lhsT=words(h_codes, b, 1).bitcast(E5M2),
-                lhsT_scale=h_scales[:, rows_of(b, 1)],
-                rhs=words(late_codes, 4, 4).bitcast(E4M3),
+                lhsT=h_codes[:, rows_of(b)].bitcast(E5M2),
+                lhsT_scale=h_scales[:, rows_of(b)],
+                rhs=w2_codes[:].bitcast(E4M3),
                 rhs_scale=w2_scales[:],
                 start=True,
                 stop=True,
             )
 
-        def store(b, by_vector, pieces):
+        def store(b, copy, pieces=1):
             width = P // pieces
-            result[b] = shared([P, D], F32, "result%d" % b, "margin%d" % (b + 4) if b < 2 else "result%d" % b)
+            result = sbuf([P, D], F32, "result%d" % b)
             for first in range(0, P, width):
                 cols = slice(first * PACK, (first + width) * PACK)
-                ordered = result[b][:, cols].rearrange("r (p t) -> r p t", t=PACK)
-                turned = sums[b][:].rearrange("r (t p) -> r p t", t=PACK)[:, first : first + width, :]
-                if by_vector:
-                    nc.vector.tensor_scalar(ordered, turned, wt_flip[:, b : b + 1], None, MULT)
-                else:
-                    nc.scalar.activation(ordered, turned, ACT.Copy, scale=wt_flip[:, b : b + 1])
-                nc.sync.dma_start(out[0, rows_of(b, 1), cols], result[b][:, cols])
+                copy(
+                    result[:, cols].rearrange("r (p f) -> r p f", f=PACK),
+                    sums[b][:].rearrange("r (f p) -> r p f", f=PACK)[:, first : first + width, :],
+                )
+                nc.sync.dma_start(out[0, rows_of(b), cols], result[:, cols])
 
-        on_scalar = nc.scalar.copy
-        on_vector = nc.vector.tensor_copy
-        code_space(x_codes, "x_codes_early", 0, 4, "x_codes_early")
-        group_x(0)
-        group_x(1)
+        turn_w(PACK - 1, 6)
+        for b in range(4):
+            group_x(b)
         quantize_x(0, 1)
-        sign_scales(0)
         quantize_x(1, 1)
         scores(0)
-        margins(0)
-        sign_scales(1)
         scores(1)
-        turn_w(PACK - 1, "bank1")
-        group_x(2)
-        group_x(3)
+        sign_w_vector(PACK - 1)
+        flip(0)
+        weigh(0)
         quantize_x(2, 2)
-        gradient(0)
-        margins(1)
-        gradient(1)
+        turn_flipped(0)
+        scores(2)
+        turn_weighted(0)
+        flip(1)
+        weigh(1)
+        quantize_w2()
         group_x(4)
         group_x(5)
-        for b in (2, 3):
-            scores(b)
-            sign_scales(b)
-            margins(b)
-        gradient(2)
+        turn_flipped(1)
+        scores(3)
+        turn_weighted(1)
+        hinge(0)
+        hinge(1)
+        flip(2)
+        weigh(2)
+        quantize_x(4, 2)
+        turn_flipped(2)
+        scores(4)
+        flip(3)
+        weigh(3)
+        turn_flipped(3)
+        scores(5)
         group_x(6)
         group_x(7)
-        sign_scales(4)
-        sign_scales(5)
-        turn_h(0, on_scalar)
-        turn_h(1, on_scalar)
-        code_space(late_codes, "late_codes", 0, 8, "slack2")
-        for k in range(4):
-            x_codes[4 + k] = late_codes[k]
-        quantize_x(4, 2)
-        scores(4)
-        scores(5)
-        nc.vector.quantize_mx(
-            out=words(late_codes, 4, 4).bitcast(E4M3),
-            scales=w2_scales[:],
-            in_=w_by_slot[:].rearrange("s t p j -> s (t p j)"),
-        )
-        code_space(h_codes, "h_codes_first", 0, 2, "signed2")
-        product(0)
-        product(1)
-        quantize_x(6, 2)
-        gradient(3)
-        margins(4)
-        gradient(4)
-        sign_scales(6)
-        margins(5)
-        store(0, False, 1)
-        turn_h(2, on_scalar)
-        scores(6)
-        sign_scales(7)
-        margins(6)
-        store(1, False, 1)
-        scores(7)
-        margins(7)
-        turn_h(3, on_vector)
-        code_space(h_codes, "h_codes_rest", 2, BLOCKS - 2, "slack4")
-        product(2)
-        product(3)
-        gradient(5)
-        turn_h(4, on_scalar)
-        store(2, False, 1)
-        gradient(6)
-        gradient(7)
-        turn_h(5, on_scalar)
-        product(4)
-        store(3, False, 1)
-        turn_h(6, on_vector)
-        product(5)
-        store(4, False, 1)
-        turn_h(7, on_vector)
-        product(6)
-        store(5, False, 1)
-        product(7)
-        store(6, False, 1)
-        store(7, True, 2)
+        hinge(2)
+        for b in range(BLOCKS):
+            gradient(b)
+            if b + 4 < BLOCKS:
+                flip(b + 4)
+            quantize_h(b)
+            if b == 0:
+                quantize_x(6, 2)
+            if b + 4 < BLOCKS:
+                weigh(b + 4)
+                turn_flipped(b + 4)
+            if b + 2 < BLOCKS:
+                turn_weighted(b + 2)
+            product(b)
+            if b + 6 < BLOCKS:
+                scores(b + 6)
+            if b + 3 < BLOCKS:
+                hinge(b + 3)
+            if b == BLOCKS - 1:
+                store(b, nc.vector.tensor_copy, 2)
+            else:
+                store(b, nc.scalar.copy)

@@ -7,6 +7,7 @@ D, T, N, R = 512, 2048, 512, 1024
 P = 128
 PACK = 4
 RUN = 8
+BANKS = 8
 BLOCKS = R // P
 CHUNK_ROWS = 256
 CHUNK_BLOCKS = CHUNK_ROWS // P
@@ -35,8 +36,15 @@ def tile_attend_gsqh_x_ts_kernel(tc, xT, wT, y, wt, ts, offs, out):
         def sbuf(shape, dtype, name, tag=None):
             return keep.tile(shape, dtype, name=name, tag=tag or name, align_bytes=64)
 
-        def bank(shape, dtype, name, index):
-            return psum.tile(shape, dtype, name=name, tag="bank%d" % index)
+        free_banks = list(range(BANKS))
+        bank_of = {}
+
+        def bank(shape, dtype, name):
+            bank_of[name] = free_banks.pop(0)
+            return psum.tile(shape, dtype, name=name, tag="bank%d" % bank_of[name])
+
+        def release(name):
+            free_banks.append(bank_of.pop(name))
 
         offsets = keep.tile([P, N // 16], U16, name="offsets")
         nc.sync.dma_start(offsets[:], offs)
@@ -85,16 +93,17 @@ def tile_attend_gsqh_x_ts_kernel(tc, xT, wT, y, wt, ts, offs, out):
         def as_dealt(slots):
             return slots.rearrange("p (t g j) -> p t g j", t=PACK, j=RUN)
 
-        wt_turned = bank([P, P], F32, "wt_turned", 4)
+        wt_turned = bank([P, P], F32, "wt_turned")
         nc.tensor.transpose(wt_turned[:], wt_rows[:], ident_f32[:])
         wt_minus = sbuf([P, BLOCKS], F32, "wt_minus")
         nc.scalar.activation(wt_minus[:], wt_turned[:, P - BLOCKS : P], ACT.Copy, scale=-1.0)
+        release("wt_turned")
 
         ts_listed = sbuf([P, N], F32, "ts_listed")
         nc.vector.tensor_copy(ts_listed[:], ts_window[:].indirect(offsets[:]))
         ts_dealt = sbuf([P, N], F32, "ts_dealt")
         nc.scalar.copy(as_dealt(ts_dealt[:]), dealt(ts_listed[:]))
-        ts_turned = bank([P, PACK, P], F32, "ts_turned", 5)
+        ts_turned = bank([P, PACK, P], F32, "ts_turned")
         for t in range(PACK):
             nc.tensor.transpose(ts_turned[:, t, :], ts_dealt[:, t * P : (t + 1) * P], ident_f32[:])
         ts_size = sbuf([P, PACK], F32, "ts_size")
@@ -104,15 +113,17 @@ def tile_attend_gsqh_x_ts_kernel(tc, xT, wT, y, wt, ts, offs, out):
         nc.scalar.activation(ts_sign[:], ts_turned[:, :, P - 1], ACT.Sign)
         nc.scalar.activation(ts_size[:], ts_turned[:, :, P - 1], ACT.Abs)
         nc.scalar.activation(ts_minus[:], ts_turned[:, :, P - 1], ACT.Copy, scale=-1.0)
+        release("ts_turned")
         nc.gpsimd.tensor_tensor(ts_slope[:], ts_minus[:], ts_size[:], MULT)
 
         w_by_d = sbuf([P, N, PACK], BF16, "w_by_d")
         w_listed = w_by_d[:].rearrange("p (t g j) f -> p f g t j", t=PACK, j=RUN)
-        w_by_slot = sbuf([P, PACK, P, PACK], BF16, "w_by_slot")
+        w_by_slot = sbuf([P, PACK - 1, P, PACK], BF16, "w_by_slot")
         w_turned = {}
+        w_last = []
 
-        def turn_w(f, index):
-            w_turned[f] = bank([P, PACK, P], BF16, "w_turned%d" % f, index)
+        def turn_w(f):
+            w_turned[f] = bank([P, PACK, P], BF16, "w_turned%d" % f)
             for t in range(PACK):
                 nc.tensor.transpose(w_turned[f][:, t, :], w_by_d[:, t * P : (t + 1) * P, f], ident_bf16[:])
 
@@ -121,19 +132,22 @@ def tile_attend_gsqh_x_ts_kernel(tc, xT, wT, y, wt, ts, offs, out):
                 nc.scalar.activation(
                     w_by_slot[:, f, :, t], w_turned[f][:, t, :], ACT.Copy, scale=ts_sign[:, t : t + 1]
                 )
+            release("w_turned%d" % f)
 
         def sign_w_vector(f):
+            w_last.append(sbuf([P, P, PACK], BF16, "w_last", "x_raw0"))
             nc.vector.tensor_tensor(
-                w_by_slot[:, f, :, :],
+                w_last[0][:],
                 ts_sign[:].unsqueeze(1).to_broadcast([P, P, PACK]),
                 w_turned[f][:].rearrange("s t p -> s p t"),
                 MULT,
             )
+            release("w_turned%d" % f)
 
         for f in range(PACK):
             nc.vector.tensor_copy(w_listed[:, f], w_planes[f][:].indirect(offsets[:]))
             if f < PACK - 1:
-                turn_w(f, (2, 3, 7)[f])
+                turn_w(f)
                 sign_w_scalar(f)
 
         w1_codes = sbuf([P, N], U32, "w1_codes")
@@ -143,19 +157,26 @@ def tile_attend_gsqh_x_ts_kernel(tc, xT, wT, y, wt, ts, offs, out):
             scales=w1_scales[:],
             in_=w_by_d[:].rearrange("p i f -> p (i f)"),
         )
-        w2_codes = sbuf([P, D], U32, "w2_codes")
+        w2_codes = []
         w2_scales = sbuf([P, D], U8, "w2_scales")
 
         def quantize_w2():
-            nc.vector.quantize_mx(
-                out=w2_codes[:].bitcast(E4M3),
-                scales=w2_scales[:],
-                in_=w_by_slot[:].rearrange("s f p t -> s (f p t)"),
-            )
+            w2_codes.append(sbuf([P, D], U32, "w2_codes", "x_grouped0"))
+            parts = [
+                (0, 2, w_by_slot[:, 0:2].rearrange("s f p t -> s (f p t)")),
+                (2, 3, w_by_slot[:, 2].rearrange("s p t -> s (p t)")),
+                (3, 4, w_last[0][:].rearrange("s p t -> s (p t)")),
+            ]
+            for first, last, values in parts:
+                nc.vector.quantize_mx(
+                    out=w2_codes[0][:, first * P : last * P].bitcast(E4M3),
+                    scales=w2_scales[:, first * P : last * P],
+                    in_=values,
+                )
 
         x_codes = sbuf([P, R], U32, "x_codes")
         x_scales = sbuf([P, R], U8, "x_scales")
-        h_codes = sbuf([P, R], U32, "h_codes")
+        h_codes = {}
         h_scales = sbuf([P, R], U8, "h_scales")
         x_grouped = {}
         raw = {}
@@ -188,7 +209,7 @@ def tile_attend_gsqh_x_ts_kernel(tc, xT, wT, y, wt, ts, offs, out):
             )
 
         def scores(b):
-            raw[b] = bank([P, N], F32, "raw%d" % b, b % 2)
+            raw[b] = bank([P, N], F32, "raw%d" % b)
             nc.tensor.matmul_mx(
                 out=raw[b][:],
                 lhsT=x_codes[:, rows_of(b)].bitcast(E4M3),
@@ -203,8 +224,8 @@ def tile_attend_gsqh_x_ts_kernel(tc, xT, wT, y, wt, ts, offs, out):
             k, j = divmod(b, CHUNK_BLOCKS)
             return dealt(y_raw[k][:, j, :])
 
-        def turn(name, source, index):
-            turned = bank([P, PACK, P], F32, name, index)
+        def turn(name, source):
+            turned = bank([P, PACK, P], F32, name)
             for t in range(PACK):
                 nc.tensor.transpose(turned[:, t, :], source[:, t * P : (t + 1) * P], ident_f32[:])
             return turned
@@ -212,9 +233,10 @@ def tile_attend_gsqh_x_ts_kernel(tc, xT, wT, y, wt, ts, offs, out):
         def flip(b):
             flipped[b] = sbuf([P, N], F32, "flipped%d" % b)
             nc.vector.tensor_tensor(as_dealt(flipped[b][:]), labels(b), as_dealt(raw[b][:]), MULT)
+            release("raw%d" % b)
 
         def turn_flipped(b):
-            flipped_turned[b] = turn("flipped_turned%d" % b, flipped[b], 2 + b % 2)
+            flipped_turned[b] = turn("flipped_turned%d" % b, flipped[b])
 
         def hinge(b):
             slack[b] = sbuf([P, PACK, P], F32, "slack%d" % b)
@@ -226,16 +248,24 @@ def tile_attend_gsqh_x_ts_kernel(tc, xT, wT, y, wt, ts, offs, out):
                     bias=ts_size[:, t : t + 1],
                     scale=ts_slope[:, t : t + 1],
                 )
+            release("flipped_turned%d" % b)
 
-        weighted_tags = ["weighted0", "x_grouped1", "w_by_slot", "x_grouped2"]
-        weighted_tags.extend("h_grouped%d" % b for b in range(BLOCKS - len(weighted_tags)))
+        def weigh_scalar(b):
+            weighted[b] = sbuf([P, N], F32, "weighted%d" % b)
+            nc.scalar.activation(as_dealt(weighted[b][:]), labels(b), ACT.Copy, scale=wt_minus[:, b : b + 1])
+
+        pair_tags = {1: "x_grouped1", 2: "h_grouped0", 3: "h_grouped1"}
+        pairs = {}
 
         def weigh(b):
-            weighted[b] = sbuf([P, N], F32, "weighted%d" % b, weighted_tags[b])
-            nc.gpsimd.tensor_scalar(as_dealt(weighted[b][:]), labels(b), wt_minus[:, b : b + 1], 0.0, MULT, ADD)
+            k, j = divmod(b, CHUNK_BLOCKS)
+            if j == 0:
+                pairs[k] = sbuf([P, CHUNK_BLOCKS, N], F32, "weighted_pair%d" % k, pair_tags[k])
+            weighted[b] = pairs[k][:, j, :]
+            nc.gpsimd.tensor_scalar(as_dealt(weighted[b]), labels(b), wt_minus[:, b : b + 1], 0.0, MULT, ADD)
 
         def turn_weighted(b):
-            weighted_turned[b] = turn("weighted_turned%d" % b, weighted[b], 4 + b % 2)
+            weighted_turned[b] = turn("weighted_turned%d" % b, weighted[b])
 
         def gradient(b):
             h_grouped[b] = sbuf([P, P, PACK], BF16, "h_grouped%d" % b)
@@ -245,21 +275,23 @@ def tile_attend_gsqh_x_ts_kernel(tc, xT, wT, y, wt, ts, offs, out):
                 weighted_turned[b][:].rearrange("s t (c i) -> s c t i", i=PACK),
                 MULT,
             )
+            release("weighted_turned%d" % b)
 
         def quantize_h(b):
+            h_codes[b] = sbuf([P, P], U32, "h_codes%d" % b, "y_raw3" if b == 2 else None)
             nc.vector.quantize_mx(
-                out=h_codes[:, rows_of(b)].bitcast(E5M2),
+                out=h_codes[b][:].bitcast(E5M2),
                 scales=h_scales[:, rows_of(b)],
                 in_=h_grouped[b][:].rearrange("s r t -> s (r t)"),
             )
 
         def product(b):
-            sums[b] = bank([P, D], F32, "sums%d" % b, 6 + b % 2)
+            sums[b] = bank([P, D], F32, "sums%d" % b)
             nc.tensor.matmul_mx(
                 out=sums[b][:],
-                lhsT=h_codes[:, rows_of(b)].bitcast(E5M2),
+                lhsT=h_codes[b][:].bitcast(E5M2),
                 lhsT_scale=h_scales[:, rows_of(b)],
-                rhs=w2_codes[:].bitcast(E4M3),
+                rhs=w2_codes[0][:].bitcast(E4M3),
                 rhs_scale=w2_scales[:],
                 start=True,
                 stop=True,
@@ -275,8 +307,9 @@ def tile_attend_gsqh_x_ts_kernel(tc, xT, wT, y, wt, ts, offs, out):
                     sums[b][:].rearrange("r (f p) -> r p f", f=PACK)[:, first : first + width, :],
                 )
                 nc.sync.dma_start(out[0, rows_of(b), cols], result[:, cols])
+            release("sums%d" % b)
 
-        turn_w(PACK - 1, 6)
+        turn_w(PACK - 1)
         for b in range(4):
             group_x(b)
         quantize_x(0, 1)
@@ -284,52 +317,73 @@ def tile_attend_gsqh_x_ts_kernel(tc, xT, wT, y, wt, ts, offs, out):
         scores(0)
         scores(1)
         sign_w_vector(PACK - 1)
-        flip(0)
-        weigh(0)
-        quantize_x(2, 2)
-        turn_flipped(0)
-        scores(2)
-        turn_weighted(0)
-        flip(1)
-        weigh(1)
         quantize_w2()
+        quantize_x(2, 2)
+        scores(2)
+        scores(3)
+        weigh_scalar(0)
+        weigh_scalar(1)
+        flip(0)
+        turn_flipped(0)
+        flip(1)
+        turn_flipped(1)
         group_x(4)
         group_x(5)
-        turn_flipped(1)
-        scores(3)
-        turn_weighted(1)
         hinge(0)
         hinge(1)
         flip(2)
         weigh(2)
-        quantize_x(4, 2)
+        turn_weighted(0)
         turn_flipped(2)
-        scores(4)
         flip(3)
         weigh(3)
         turn_flipped(3)
+        quantize_x(4, 2)
+        scores(4)
         scores(5)
+        turn_weighted(1)
+        gradient(0)
+        quantize_h(0)
         group_x(6)
         group_x(7)
         hinge(2)
-        for b in range(BLOCKS):
+        hinge(3)
+        flip(4)
+        weigh(4)
+        turn_flipped(4)
+        flip(5)
+        weigh(5)
+        turn_weighted(2)
+        turn_flipped(5)
+        product(0)
+        gradient(1)
+        quantize_x(6, 2)
+        scores(6)
+        scores(7)
+        quantize_h(1)
+        hinge(4)
+        hinge(5)
+        turn_weighted(3)
+        product(1)
+        gradient(2)
+        flip(6)
+        weigh(6)
+        store(0, nc.scalar.copy)
+        turn_weighted(4)
+        turn_flipped(6)
+        flip(7)
+        weigh(7)
+        turn_flipped(7)
+        store(1, nc.scalar.copy)
+        hinge(6)
+        hinge(7)
+        for b in range(3, BLOCKS):
             gradient(b)
-            if b + 4 < BLOCKS:
-                flip(b + 4)
-            quantize_h(b)
-            if b == 0:
-                quantize_x(6, 2)
-            if b + 4 < BLOCKS:
-                weigh(b + 4)
-                turn_flipped(b + 4)
             if b + 2 < BLOCKS:
                 turn_weighted(b + 2)
-            product(b)
-            if b + 6 < BLOCKS:
-                scores(b + 6)
-            if b + 3 < BLOCKS:
-                hinge(b + 3)
-            if b == BLOCKS - 1:
-                store(b, nc.vector.tensor_copy, 2)
-            else:
-                store(b, nc.scalar.copy)
+            quantize_h(b - 1)
+            product(b - 1)
+            store(b - 1, nc.scalar.copy)
+        quantize_h(BLOCKS - 1)
+        product(BLOCKS - 1)
+        store(BLOCKS - 1, nc.vector.tensor_copy, 2)

@@ -8,6 +8,7 @@ P = 128
 PACK = 4
 RUN = 8
 BANKS = 8
+EARLY = 2
 BLOCKS = R // P
 CHUNK_ROWS = 256
 CHUNK_BLOCKS = CHUNK_ROWS // P
@@ -50,7 +51,6 @@ def tile_attend_gsqh_x_ts_kernel(tc, xT, wT, y, wt, ts, offs, out):
         nc.sync.dma_start(offsets[:], offs)
 
         wt_rows = sbuf([P, P], F32, "wt_rows")
-        nc.sync.dma_start(wt_rows[P - BLOCKS : P, :], wt[0].rearrange("(b p) o -> b (p o)", p=P))
         ts_window = sbuf([P, T], F32, "ts_window")
         nc.sync.dma_start(ts_window[P - 1 : P, :], ts[0:1, :])
         nc.vector.memset(wt_rows[0 : P - BLOCKS, :], 0.0)
@@ -62,6 +62,8 @@ def tile_attend_gsqh_x_ts_kernel(tc, xT, wT, y, wt, ts, offs, out):
             plane = sbuf([P, T], F32, "w_plane%d" % f)
             nc.sync.dma_start(plane[:], w_rows[:, f, :])
             w_planes.append(plane)
+            if f == 0:
+                nc.sync.dma_start(wt_rows[P - BLOCKS : P, :], wt[0].rearrange("(b p) o -> b (p o)", p=P))
 
         x_rows = xT[0].rearrange("(p f) r -> p f r", f=PACK)
         y_rows = y[0].rearrange("(k j p) i -> k p j i", p=P, j=CHUNK_BLOCKS)
@@ -111,6 +113,8 @@ def tile_attend_gsqh_x_ts_kernel(tc, xT, wT, y, wt, ts, offs, out):
         ts_minus = sbuf([P, PACK], F32, "ts_minus")
         ts_slope = sbuf([P, PACK], F32, "ts_slope")
         nc.scalar.activation(ts_sign[:], ts_turned[:, :, P - 1], ACT.Sign)
+        ts_sign_bf16 = sbuf([P, PACK], BF16, "ts_sign_bf16")
+        nc.scalar.activation(ts_sign_bf16[:], ts_turned[:, :, P - 1], ACT.Sign)
         nc.scalar.activation(ts_size[:], ts_turned[:, :, P - 1], ACT.Abs)
         nc.scalar.activation(ts_minus[:], ts_turned[:, :, P - 1], ACT.Copy, scale=-1.0)
         release("ts_turned")
@@ -118,9 +122,9 @@ def tile_attend_gsqh_x_ts_kernel(tc, xT, wT, y, wt, ts, offs, out):
 
         w_by_d = sbuf([P, N, PACK], BF16, "w_by_d")
         w_listed = w_by_d[:].rearrange("p (t g j) f -> p f g t j", t=PACK, j=RUN)
-        w_by_slot = sbuf([P, PACK - 1, P, PACK], BF16, "w_by_slot")
+        w_early = sbuf([P, EARLY, P, PACK], BF16, "w_early")
         w_turned = {}
-        w_last = []
+        w_unsigned = {}
 
         def turn_w(f):
             w_turned[f] = bank([P, PACK, P], BF16, "w_turned%d" % f)
@@ -130,25 +134,31 @@ def tile_attend_gsqh_x_ts_kernel(tc, xT, wT, y, wt, ts, offs, out):
         def sign_w_scalar(f):
             for t in range(PACK):
                 nc.scalar.activation(
-                    w_by_slot[:, f, :, t], w_turned[f][:, t, :], ACT.Copy, scale=ts_sign[:, t : t + 1]
+                    w_early[:, f, :, t], w_turned[f][:, t, :], ACT.Copy, scale=ts_sign[:, t : t + 1]
                 )
             release("w_turned%d" % f)
 
+        def copy_w(f, tag):
+            w_unsigned[f] = sbuf([P, P, PACK], BF16, "w_unsigned%d" % f, tag)
+            nc.scalar.copy(w_unsigned[f][:], w_turned[f][:].rearrange("s t p -> s p t"))
+            release("w_turned%d" % f)
+
         def sign_w_vector(f):
-            w_last.append(sbuf([P, P, PACK], BF16, "w_last", "x_raw0"))
             nc.vector.tensor_tensor(
-                w_last[0][:],
-                ts_sign[:].unsqueeze(1).to_broadcast([P, P, PACK]),
-                w_turned[f][:].rearrange("s t p -> s p t"),
+                w_late[:, f - EARLY],
+                w_unsigned[f][:],
+                ts_sign_bf16[:].unsqueeze(1).to_broadcast([P, P, PACK]),
                 MULT,
             )
-            release("w_turned%d" % f)
 
         for f in range(PACK):
             nc.vector.tensor_copy(w_listed[:, f], w_planes[f][:].indirect(offsets[:]))
             if f < PACK - 1:
                 turn_w(f)
+            if f < EARLY:
                 sign_w_scalar(f)
+        copy_w(EARLY, None)
+        w_late = sbuf([P, PACK - EARLY, P, PACK], BF16, "w_late", "w_plane%d" % (PACK - 1))
 
         w1_codes = sbuf([P, N], U32, "w1_codes")
         w1_scales = sbuf([P, N], U8, "w1_scales")
@@ -160,19 +170,12 @@ def tile_attend_gsqh_x_ts_kernel(tc, xT, wT, y, wt, ts, offs, out):
         w2_codes = []
         w2_scales = sbuf([P, D], U8, "w2_scales")
 
-        def quantize_w2():
-            w2_codes.append(sbuf([P, D], U32, "w2_codes", "x_grouped0"))
-            parts = [
-                (0, 2, w_by_slot[:, 0:2].rearrange("s f p t -> s (f p t)")),
-                (2, 3, w_by_slot[:, 2].rearrange("s p t -> s (p t)")),
-                (3, 4, w_last[0][:].rearrange("s p t -> s (p t)")),
-            ]
-            for first, last, values in parts:
-                nc.vector.quantize_mx(
-                    out=w2_codes[0][:, first * P : last * P].bitcast(E4M3),
-                    scales=w2_scales[:, first * P : last * P],
-                    in_=values,
-                )
+        def quantize_w2(first, values):
+            nc.vector.quantize_mx(
+                out=w2_codes[0][:, first * P : (first + 2) * P].bitcast(E4M3),
+                scales=w2_scales[:, first * P : (first + 2) * P],
+                in_=values[:].rearrange("s f p t -> s (f p t)"),
+            )
 
         x_codes = sbuf([P, R], U32, "x_codes")
         x_scales = sbuf([P, R], U8, "x_scales")
@@ -310,15 +313,20 @@ def tile_attend_gsqh_x_ts_kernel(tc, xT, wT, y, wt, ts, offs, out):
             release("sums%d" % b)
 
         turn_w(PACK - 1)
-        for b in range(4):
+        for b in range(3):
             group_x(b)
+        copy_w(PACK - 1, "x_raw0")
+        group_x(3)
         quantize_x(0, 1)
         quantize_x(1, 1)
         scores(0)
         scores(1)
-        sign_w_vector(PACK - 1)
-        quantize_w2()
+        w2_codes.append(sbuf([P, D], U32, "w2_codes", "x_grouped0"))
+        quantize_w2(0, w_early)
+        sign_w_vector(2)
+        sign_w_vector(3)
         quantize_x(2, 2)
+        quantize_w2(EARLY, w_late)
         scores(2)
         scores(3)
         weigh_scalar(0)

@@ -32,6 +32,7 @@ def tile_attend_gsqh_x_ts_kernel(tc, xT, wT, y, wt, ts, offs, out):
     nc = tc.nc
     with ExitStack() as ctx:
         keep = ctx.enter_context(tc.tile_pool(name="keep", bufs=1))
+        shared = ctx.enter_context(tc.tile_pool(name="shared", bufs=1))
         psum = ctx.enter_context(tc.psum_pool(name="psum", bufs=1))
 
         def sbuf(shape, dtype, name, tag=None):
@@ -59,7 +60,10 @@ def tile_attend_gsqh_x_ts_kernel(tc, xT, wT, y, wt, ts, offs, out):
         w_rows = wT.rearrange("(p f) c -> p f c", f=PACK)
         w_planes = []
         for f in range(PACK):
-            plane = sbuf([P, T], F32, "w_plane%d" % f)
+            if f < PACK - 1:
+                plane = sbuf([P, T], F32, "w_plane%d" % f)
+            else:
+                plane = shared.tile([P, T], F32, name="w_plane_last", offset=0, align_bytes=64)
             nc.sync.dma_start(plane[:], w_rows[:, f, :])
             w_planes.append(plane)
             if f == 0:
@@ -158,7 +162,7 @@ def tile_attend_gsqh_x_ts_kernel(tc, xT, wT, y, wt, ts, offs, out):
             if f < EARLY:
                 sign_w_scalar(f)
         copy_w(EARLY, None)
-        w_late = sbuf([P, PACK - EARLY, P, PACK], BF16, "w_late", "w_plane%d" % (PACK - 1))
+        w_late = shared.tile([P, PACK - EARLY, P, PACK], BF16, name="w_late", offset=0, align_bytes=64)
 
         w1_codes = sbuf([P, N], U32, "w1_codes")
         w1_scales = sbuf([P, N], U8, "w1_scales")
@@ -233,38 +237,68 @@ def tile_attend_gsqh_x_ts_kernel(tc, xT, wT, y, wt, ts, offs, out):
                 nc.tensor.transpose(turned[:, t, :], source[:, t * P : (t + 1) * P], ident_f32[:])
             return turned
 
+        flipped_pairs = {}
+
         def flip(b):
-            flipped[b] = sbuf([P, N], F32, "flipped%d" % b)
-            nc.vector.tensor_tensor(as_dealt(flipped[b][:]), labels(b), as_dealt(raw[b][:]), MULT)
+            k, j = divmod(b, CHUNK_BLOCKS)
+            if j == 0:
+                tag = "x_raw1" if k == 0 else None
+                flipped_pairs[k] = sbuf([P, CHUNK_BLOCKS, N], F32, "flipped_pair%d" % k, tag)
+            flipped[b] = flipped_pairs[k][:, j, :]
+            nc.vector.tensor_tensor(as_dealt(flipped[b]), labels(b), as_dealt(raw[b][:]), MULT)
             release("raw%d" % b)
 
+        PAIRED = (1, 2)
+
         def turn_flipped(b):
-            flipped_turned[b] = turn("flipped_turned%d" % b, flipped[b])
+            if b // CHUNK_BLOCKS not in PAIRED:
+                flipped_turned[b] = turn("flipped_turned%d" % b, flipped[b])
+                return
+            k, j = divmod(b, CHUNK_BLOCKS)
+            if j == 0:
+                flipped_turned[b] = [
+                    bank([P, 2, CHUNK_ROWS], F32, "flipped_turned%d_%d" % (k, half)) for half in range(2)
+                ]
+            for t in range(PACK):
+                nc.tensor.transpose(
+                    flipped_turned[b - j][t // 2][:, t % 2, rows_of(j)],
+                    flipped[b][:, t * P : (t + 1) * P],
+                    ident_f32[:],
+                )
+
+        def relu(target, source, t):
+            nc.scalar.activation(
+                target, source, ACT.Relu, bias=ts_size[:, t : t + 1], scale=ts_slope[:, t : t + 1]
+            )
 
         def hinge(b):
-            slack[b] = sbuf([P, PACK, P], F32, "slack%d" % b)
+            if b // CHUNK_BLOCKS not in PAIRED:
+                slack[b] = sbuf([P, PACK, P], F32, "slack%d" % b)[:]
+                for t in range(PACK):
+                    relu(slack[b][:, t, :], flipped_turned[b][:, t, :], t)
+                release("flipped_turned%d" % b)
+                return
+            k = b // CHUNK_BLOCKS
+            both = sbuf([P, PACK, CHUNK_ROWS], F32, "slack_pair%d" % k)
             for t in range(PACK):
-                nc.scalar.activation(
-                    slack[b][:, t, :],
-                    flipped_turned[b][:, t, :],
-                    ACT.Relu,
-                    bias=ts_size[:, t : t + 1],
-                    scale=ts_slope[:, t : t + 1],
-                )
-            release("flipped_turned%d" % b)
+                relu(both[:, t, :], flipped_turned[b][t // 2][:, t % 2, :], t)
+                if t % 2:
+                    release("flipped_turned%d_%d" % (k, t // 2))
+            for j in range(CHUNK_BLOCKS):
+                slack[b + j] = both[:, :, rows_of(j)]
 
         def weigh_scalar(b):
             weighted[b] = sbuf([P, N], F32, "weighted%d" % b)
             nc.scalar.activation(as_dealt(weighted[b][:]), labels(b), ACT.Copy, scale=wt_minus[:, b : b + 1])
 
-        pair_tags = {1: "x_grouped1", 2: "h_grouped0", 3: "h_grouped1"}
-        pairs = {}
+        runs = {2: (1, "x_grouped1"), 3: (2, "h_grouped0"), 6: (2, "h_grouped1")}
 
         def weigh(b):
-            k, j = divmod(b, CHUNK_BLOCKS)
-            if j == 0:
-                pairs[k] = sbuf([P, CHUNK_BLOCKS, N], F32, "weighted_pair%d" % k, pair_tags[k])
-            weighted[b] = pairs[k][:, j, :]
+            if b in runs:
+                count, tag = runs[b]
+                space = sbuf([P, count, N], F32, "weighted_run%d" % b, tag)
+                for j in range(count):
+                    weighted[b + j] = space[:, j, :]
             nc.gpsimd.tensor_scalar(as_dealt(weighted[b]), labels(b), wt_minus[:, b : b + 1], 0.0, MULT, ADD)
 
         def turn_weighted(b):
@@ -274,7 +308,7 @@ def tile_attend_gsqh_x_ts_kernel(tc, xT, wT, y, wt, ts, offs, out):
             h_grouped[b] = sbuf([P, P, PACK], BF16, "h_grouped%d" % b)
             nc.vector.tensor_tensor(
                 h_grouped[b][:].rearrange("s (c i) t -> s c t i", i=PACK),
-                slack[b][:].rearrange("s t (c i) -> s c t i", i=PACK),
+                slack[b].rearrange("s t (c i) -> s c t i", i=PACK),
                 weighted_turned[b][:].rearrange("s t (c i) -> s c t i", i=PACK),
                 MULT,
             )
@@ -321,7 +355,7 @@ def tile_attend_gsqh_x_ts_kernel(tc, xT, wT, y, wt, ts, offs, out):
         quantize_x(1, 1)
         scores(0)
         scores(1)
-        w2_codes.append(sbuf([P, D], U32, "w2_codes", "x_grouped0"))
+        w2_codes.append(shared.tile([P, D], U32, name="w2_codes", offset=4 * D, align_bytes=64))
         quantize_w2(0, w_early)
         sign_w_vector(2)
         sign_w_vector(3)
@@ -344,7 +378,6 @@ def tile_attend_gsqh_x_ts_kernel(tc, xT, wT, y, wt, ts, offs, out):
         turn_weighted(0)
         turn_flipped(2)
         flip(3)
-        weigh(3)
         turn_flipped(3)
         quantize_x(4, 2)
         scores(4)
@@ -355,12 +388,12 @@ def tile_attend_gsqh_x_ts_kernel(tc, xT, wT, y, wt, ts, offs, out):
         group_x(6)
         group_x(7)
         hinge(2)
-        hinge(3)
+        weigh_scalar(5)
+        weigh(3)
         flip(4)
         weigh(4)
         turn_flipped(4)
         flip(5)
-        weigh(5)
         turn_weighted(2)
         turn_flipped(5)
         product(0)
@@ -370,7 +403,6 @@ def tile_attend_gsqh_x_ts_kernel(tc, xT, wT, y, wt, ts, offs, out):
         scores(7)
         quantize_h(1)
         hinge(4)
-        hinge(5)
         turn_weighted(3)
         product(1)
         gradient(2)

@@ -227,6 +227,19 @@ def tile_attend_gsqh_x_ts_kernel(tc, xT, wT, y, wt, ts, offs, out):
                 stop=True,
             )
 
+        def warm_up(name):
+            unread = bank([P, N], F32, name)
+            nc.tensor.matmul_mx(
+                out=unread[:],
+                lhsT=w1_codes[:, 0:P].bitcast(E4M3),
+                lhsT_scale=w1_scales[:, 0:P],
+                rhs=w1_codes[:].bitcast(E4M3),
+                rhs_scale=w1_scales[:],
+                start=True,
+                stop=True,
+            )
+            release(name)
+
         def labels(b):
             k, j = divmod(b, CHUNK_BLOCKS)
             return dealt(y_raw[k][:, j, :])
@@ -351,6 +364,8 @@ def tile_attend_gsqh_x_ts_kernel(tc, xT, wT, y, wt, ts, offs, out):
             group_x(b)
         copy_w(PACK - 1, "x_raw0")
         group_x(3)
+        warm_up("warm0")
+        warm_up("warm1")
         quantize_x(0, 1)
         quantize_x(1, 1)
         scores(0)

@@ -16,6 +16,20 @@ CHUNK_BLOCKS = CHUNK_ROWS // P
 FLOPS = 2 * 2 * R * N * D
 BYTES = 4 * (D * R + D * T + R * N + R + T + R * D) + 2 * P * (N // 16)
 
+FLIP_TAGS = {2: "h_grouped0", 3: "h_grouped2"}
+GROUP_TAGS = {3: "flipped_pair0"}
+RESULT_TAGS = {}
+PAIRS = (1, 2)
+RUNS = {2: (1, None), 3: (1, "x_grouped2"), 4: (2, "h_grouped1"), 6: (2, "h_grouped3")}
+CODE_TAGS = {}
+BANK_OF = {"wt_turned": 0, "ts_turned": 1, "w_turned0": 2, "w_turned1": 3, "w_turned2": 4, "w_turned3": 5,
+    "raw0": 0, "raw1": 1, "raw2": 6, "raw3": 7, "raw4": 0, "raw5": 1, "raw6": 0, "raw7": 1,
+    "warm0": 1, "warm1": 0, "warm2": 1, "warm3": 1,
+    "flipped_turned0": 2, "flipped_turned1": 3, "flipped_turned1_0": 4, "flipped_turned1_1": 5,
+    "flipped_turned2_0": 4, "flipped_turned2_1": 5, "flipped_turned6": 4, "flipped_turned7": 5,
+    "sums0": 6, "sums1": 7, "sums2": 6, "sums3": 7, "sums4": 0, "sums5": 1, "sums6": 6, "sums7": 4,
+    **{"weighted_turned%d" % b: 2 + b % 2 for b in range(8)}}
+
 F32 = mybir.dt.float32
 BF16 = mybir.dt.bfloat16
 U32 = mybir.dt.uint32
@@ -33,20 +47,14 @@ def tile_attend_gsqh_x_ts_kernel(tc, xT, wT, y, wt, ts, offs, out):
     with ExitStack() as ctx:
         keep = ctx.enter_context(tc.tile_pool(name="keep", bufs=1))
         shared = ctx.enter_context(tc.tile_pool(name="shared", bufs=1))
+        first = ctx.enter_context(tc.tile_pool(name="first", bufs=1))
         psum = ctx.enter_context(tc.psum_pool(name="psum", bufs=1))
 
         def sbuf(shape, dtype, name, tag=None):
             return keep.tile(shape, dtype, name=name, tag=tag or name, align_bytes=64)
 
-        free_banks = list(range(BANKS))
-        bank_of = {}
-
         def bank(shape, dtype, name):
-            bank_of[name] = free_banks.pop(0)
-            return psum.tile(shape, dtype, name=name, tag="bank%d" % bank_of[name])
-
-        def release(name):
-            free_banks.append(bank_of.pop(name))
+            return psum.tile(shape, dtype, name=name, tag="bank%d" % BANK_OF[name])
 
         offsets = keep.tile([P, N // 16], U16, name="offsets")
         nc.sync.dma_start(offsets[:], offs)
@@ -75,7 +83,10 @@ def tile_attend_gsqh_x_ts_kernel(tc, xT, wT, y, wt, ts, offs, out):
         y_raw = {}
 
         def load_x(k):
-            x_raw[k] = sbuf([P, PACK, CHUNK_ROWS], F32, "x_raw%d" % k)
+            if k == 0:
+                x_raw[k] = first.tile([P, PACK, CHUNK_ROWS], F32, name="x_raw0", offset=0, align_bytes=64)
+            else:
+                x_raw[k] = sbuf([P, PACK, CHUNK_ROWS], F32, "x_raw%d" % k)
             nc.sync.dma_start(x_raw[k][:], x_rows[:, :, k * CHUNK_ROWS : (k + 1) * CHUNK_ROWS])
 
         def load_y(k):
@@ -103,7 +114,6 @@ def tile_attend_gsqh_x_ts_kernel(tc, xT, wT, y, wt, ts, offs, out):
         nc.tensor.transpose(wt_turned[:], wt_rows[:], ident_f32[:])
         wt_minus = sbuf([P, BLOCKS], F32, "wt_minus")
         nc.scalar.activation(wt_minus[:], wt_turned[:, P - BLOCKS : P], ACT.Copy, scale=-1.0)
-        release("wt_turned")
 
         ts_listed = sbuf([P, N], F32, "ts_listed")
         nc.vector.tensor_copy(ts_listed[:], ts_window[:].indirect(offsets[:]))
@@ -121,7 +131,6 @@ def tile_attend_gsqh_x_ts_kernel(tc, xT, wT, y, wt, ts, offs, out):
         nc.scalar.activation(ts_sign_bf16[:], ts_turned[:, :, P - 1], ACT.Sign)
         nc.scalar.activation(ts_size[:], ts_turned[:, :, P - 1], ACT.Abs)
         nc.scalar.activation(ts_minus[:], ts_turned[:, :, P - 1], ACT.Copy, scale=-1.0)
-        release("ts_turned")
         nc.gpsimd.tensor_tensor(ts_slope[:], ts_minus[:], ts_size[:], MULT)
 
         w_by_d = sbuf([P, N, PACK], BF16, "w_by_d")
@@ -140,12 +149,10 @@ def tile_attend_gsqh_x_ts_kernel(tc, xT, wT, y, wt, ts, offs, out):
                 nc.scalar.activation(
                     w_early[:, f, :, t], w_turned[f][:, t, :], ACT.Copy, scale=ts_sign[:, t : t + 1]
                 )
-            release("w_turned%d" % f)
 
         def copy_w(f, tag):
             w_unsigned[f] = sbuf([P, P, PACK], BF16, "w_unsigned%d" % f, tag)
             nc.scalar.copy(w_unsigned[f][:], w_turned[f][:].rearrange("s t p -> s p t"))
-            release("w_turned%d" % f)
 
         def sign_w_vector(f):
             nc.vector.tensor_tensor(
@@ -166,11 +173,14 @@ def tile_attend_gsqh_x_ts_kernel(tc, xT, wT, y, wt, ts, offs, out):
 
         w1_codes = sbuf([P, N], U32, "w1_codes")
         w1_scales = sbuf([P, N], U8, "w1_scales")
-        nc.vector.quantize_mx(
-            out=w1_codes[:].bitcast(E4M3),
-            scales=w1_scales[:],
-            in_=w_by_d[:].rearrange("p i f -> p (i f)"),
-        )
+
+        def quantize_w1():
+            nc.vector.quantize_mx(
+                out=w1_codes[:].bitcast(E4M3),
+                scales=w1_scales[:],
+                in_=w_by_d[:].rearrange("p i f -> p (i f)"),
+            )
+
         w2_codes = []
         w2_scales = sbuf([P, D], U8, "w2_scales")
 
@@ -198,13 +208,18 @@ def tile_attend_gsqh_x_ts_kernel(tc, xT, wT, y, wt, ts, offs, out):
         def rows_of(b, count=1):
             return slice(b * P, (b + count) * P)
 
-        def group_x(b):
+        def gpsimd_round(target, source):
+            nc.gpsimd.tensor_scalar(target, source, 1.0, 0.0, MULT, ADD)
+
+        def group_x(b, count=1, copy=nc.scalar.copy):
             k, j = divmod(b, CHUNK_BLOCKS)
-            if j == 0:
-                x_grouped[k] = sbuf([P, CHUNK_ROWS, PACK], BF16, "x_grouped%d" % k)
-            nc.scalar.copy(
-                x_grouped[k][:, rows_of(j), :].rearrange("p (c i) f -> p c f i", i=PACK),
-                x_raw[k][:, :, rows_of(j)].rearrange("p f (c i) -> p c f i", i=PACK),
+            if b == CHUNK_BLOCKS:
+                x_grouped[k] = first.tile([P, CHUNK_ROWS, PACK], BF16, name="x_grouped1", offset=4 * D, align_bytes=64)
+            elif j == 0:
+                x_grouped[k] = sbuf([P, CHUNK_ROWS, PACK], BF16, "x_grouped%d" % k, GROUP_TAGS.get(k))
+            copy(
+                x_grouped[k][:, rows_of(j, count), :].rearrange("p (c i) f -> p c f i", i=PACK),
+                x_raw[k][:, :, rows_of(j, count)].rearrange("p f (c i) -> p c f i", i=PACK),
             )
 
         def quantize_x(b, count):
@@ -227,18 +242,18 @@ def tile_attend_gsqh_x_ts_kernel(tc, xT, wT, y, wt, ts, offs, out):
                 stop=True,
             )
 
-        def warm_up(name):
-            unread = bank([P, N], F32, name)
+        def warm_up(name, width, first):
+            unread = bank([P, width], F32, name)
+            moving, moving_scales = w1_codes, w1_scales
             nc.tensor.matmul_mx(
                 out=unread[:],
-                lhsT=w1_codes[:, 0:P].bitcast(E4M3),
-                lhsT_scale=w1_scales[:, 0:P],
-                rhs=w1_codes[:].bitcast(E4M3),
-                rhs_scale=w1_scales[:],
+                lhsT=w2_codes[0][:, first : first + P].bitcast(E4M3),
+                lhsT_scale=w2_scales[:, first : first + P],
+                rhs=moving[:, 0:width].bitcast(E4M3),
+                rhs_scale=moving_scales[:, 0:width],
                 start=True,
                 stop=True,
             )
-            release(name)
 
         def labels(b):
             k, j = divmod(b, CHUNK_BLOCKS)
@@ -255,13 +270,12 @@ def tile_attend_gsqh_x_ts_kernel(tc, xT, wT, y, wt, ts, offs, out):
         def flip(b):
             k, j = divmod(b, CHUNK_BLOCKS)
             if j == 0:
-                tag = "x_raw1" if k == 0 else None
+                tag = FLIP_TAGS.get(k)
                 flipped_pairs[k] = sbuf([P, CHUNK_BLOCKS, N], F32, "flipped_pair%d" % k, tag)
             flipped[b] = flipped_pairs[k][:, j, :]
             nc.vector.tensor_tensor(as_dealt(flipped[b]), labels(b), as_dealt(raw[b][:]), MULT)
-            release("raw%d" % b)
 
-        PAIRED = (1, 2)
+        PAIRED = PAIRS
 
         def turn_flipped(b):
             if b // CHUNK_BLOCKS not in PAIRED:
@@ -289,14 +303,11 @@ def tile_attend_gsqh_x_ts_kernel(tc, xT, wT, y, wt, ts, offs, out):
                 slack[b] = sbuf([P, PACK, P], F32, "slack%d" % b)[:]
                 for t in range(PACK):
                     relu(slack[b][:, t, :], flipped_turned[b][:, t, :], t)
-                release("flipped_turned%d" % b)
                 return
             k = b // CHUNK_BLOCKS
             both = sbuf([P, PACK, CHUNK_ROWS], F32, "slack_pair%d" % k)
             for t in range(PACK):
                 relu(both[:, t, :], flipped_turned[b][t // 2][:, t % 2, :], t)
-                if t % 2:
-                    release("flipped_turned%d_%d" % (k, t // 2))
             for j in range(CHUNK_BLOCKS):
                 slack[b + j] = both[:, :, rows_of(j)]
 
@@ -304,7 +315,7 @@ def tile_attend_gsqh_x_ts_kernel(tc, xT, wT, y, wt, ts, offs, out):
             weighted[b] = sbuf([P, N], F32, "weighted%d" % b)
             nc.scalar.activation(as_dealt(weighted[b][:]), labels(b), ACT.Copy, scale=wt_minus[:, b : b + 1])
 
-        runs = {2: (1, "x_grouped1"), 3: (2, "h_grouped0"), 6: (2, "h_grouped1")}
+        runs = RUNS
 
         def weigh(b):
             if b in runs:
@@ -325,10 +336,9 @@ def tile_attend_gsqh_x_ts_kernel(tc, xT, wT, y, wt, ts, offs, out):
                 weighted_turned[b][:].rearrange("s t (c i) -> s c t i", i=PACK),
                 MULT,
             )
-            release("weighted_turned%d" % b)
 
         def quantize_h(b):
-            h_codes[b] = sbuf([P, P], U32, "h_codes%d" % b, "y_raw3" if b == 2 else None)
+            h_codes[b] = sbuf([P, P], U32, "h_codes%d" % b, CODE_TAGS.get(b))
             nc.vector.quantize_mx(
                 out=h_codes[b][:].bitcast(E5M2),
                 scales=h_scales[:, rows_of(b)],
@@ -349,7 +359,7 @@ def tile_attend_gsqh_x_ts_kernel(tc, xT, wT, y, wt, ts, offs, out):
 
         def store(b, copy, pieces=1):
             width = P // pieces
-            result = sbuf([P, D], F32, "result%d" % b)
+            result = sbuf([P, D], F32, "result%d" % b, RESULT_TAGS.get(b))
             for first in range(0, P, width):
                 cols = slice(first * PACK, (first + width) * PACK)
                 copy(
@@ -357,25 +367,21 @@ def tile_attend_gsqh_x_ts_kernel(tc, xT, wT, y, wt, ts, offs, out):
                     sums[b][:].rearrange("r (f p) -> r p f", f=PACK)[:, first : first + width, :],
                 )
                 nc.sync.dma_start(out[0, rows_of(b), cols], result[:, cols])
-            release("sums%d" % b)
 
-        turn_w(PACK - 1)
-        for b in range(3):
-            group_x(b)
-        copy_w(PACK - 1, "x_raw0")
-        group_x(3)
-        warm_up("warm0")
-        warm_up("warm1")
+        quantize_w1()
+        sign_w_vector(2)
+        group_x(0)
+        group_x(1)
         quantize_x(0, 1)
         quantize_x(1, 1)
+        turn_w(PACK - 1)
         scores(0)
         scores(1)
-        w2_codes.append(shared.tile([P, D], U32, name="w2_codes", offset=4 * D, align_bytes=64))
+        copy_w(PACK - 1, None)
+        group_x(2, 2, nc.vector.tensor_copy)
+        w2_codes.append(first.tile([P, D], U32, name="w2_codes", offset=0, align_bytes=64))
         quantize_w2(0, w_early)
-        sign_w_vector(2)
-        sign_w_vector(3)
         quantize_x(2, 2)
-        quantize_w2(EARLY, w_late)
         scores(2)
         scores(3)
         weigh_scalar(0)
@@ -384,61 +390,82 @@ def tile_attend_gsqh_x_ts_kernel(tc, xT, wT, y, wt, ts, offs, out):
         turn_flipped(0)
         flip(1)
         turn_flipped(1)
-        group_x(4)
-        group_x(5)
         hinge(0)
         hinge(1)
-        flip(2)
-        weigh(2)
+        sign_w_vector(3)
+        group_x(4, 2, nc.vector.tensor_copy)
+        quantize_w2(EARLY, w_late)
+        warm_up("warm0", N, 0)
+        warm_up("warm1", N, D - P)
+        warm_up("warm2", N, D - P)
         turn_weighted(0)
+        weigh(2)
+        flip(2)
         turn_flipped(2)
+        turn_weighted(1)
         flip(3)
         turn_flipped(3)
         quantize_x(4, 2)
         scores(4)
         scores(5)
-        turn_weighted(1)
-        gradient(0)
-        quantize_h(0)
+        weigh(3)
         group_x(6)
         group_x(7)
         hinge(2)
-        weigh_scalar(5)
-        weigh(3)
-        flip(4)
+        gradient(0)
+        gradient(1)
+        turn_weighted(2)
+        turn_weighted(3)
+        quantize_h(0)
+        quantize_x(6, 2)
+        quantize_h(1)
+        product(0)
+        product(1)
         weigh(4)
+        weigh(5)
+        flip(4)
         turn_flipped(4)
         flip(5)
-        turn_weighted(2)
         turn_flipped(5)
-        product(0)
-        gradient(1)
-        quantize_x(6, 2)
+        store(0, nc.scalar.copy)
+        store(1, nc.scalar.copy)
         scores(6)
         scores(7)
-        quantize_h(1)
         hinge(4)
-        turn_weighted(3)
-        product(1)
         gradient(2)
-        flip(6)
-        weigh(6)
-        store(0, nc.scalar.copy)
+        gradient(3)
         turn_weighted(4)
+        turn_weighted(5)
+        quantize_h(2)
+        quantize_h(3)
+        product(2)
+        product(3)
+        weigh(6)
+        weigh(7)
+        flip(6)
         turn_flipped(6)
         flip(7)
-        weigh(7)
         turn_flipped(7)
-        store(1, nc.scalar.copy)
+        store(2, nc.scalar.copy)
         hinge(6)
         hinge(7)
-        for b in range(3, BLOCKS):
-            gradient(b)
-            if b + 2 < BLOCKS:
-                turn_weighted(b + 2)
-            quantize_h(b - 1)
-            product(b - 1)
-            store(b - 1, nc.scalar.copy)
-        quantize_h(BLOCKS - 1)
-        product(BLOCKS - 1)
-        store(BLOCKS - 1, nc.vector.tensor_copy, 2)
+        warm_up("warm3", N, 0)
+        gradient(4)
+        turn_weighted(6)
+        gradient(5)
+        turn_weighted(7)
+        quantize_h(4)
+        quantize_h(5)
+        product(4)
+        product(5)
+        store(3, nc.vector.tensor_copy)
+        store(4, nc.scalar.copy)
+        store(5, nc.scalar.copy)
+        gradient(6)
+        quantize_h(6)
+        product(6)
+        gradient(7)
+        quantize_h(7)
+        product(7)
+        store(6, nc.scalar.copy)
+        store(7, nc.vector.tensor_copy, 2)

@@ -20,15 +20,17 @@ FLIP_TAGS = {2: "h_grouped0", 3: "h_grouped2"}
 GROUP_TAGS = {3: "flipped_pair0"}
 RESULT_TAGS = {}
 PAIRS = (1, 2)
-RUNS = {2: (1, None), 3: (1, "x_grouped2"), 4: (2, "h_grouped1"), 6: (2, "h_grouped3")}
+RUNS = {1: (1, "w_unsigned2"), 2: (1, "w_late"), 3: (1, "x_grouped2"), 4: (1, "h_grouped1"), 5: (1, "flipped_pair0"), 6: (2, "h_grouped3")}
 CODE_TAGS = {}
 BANK_OF = {"wt_turned": 0, "ts_turned": 1, "w_turned0": 2, "w_turned1": 3, "w_turned2": 4, "w_turned3": 5,
-    "raw0": 0, "raw1": 1, "raw2": 6, "raw3": 7, "raw4": 0, "raw5": 1, "raw6": 0, "raw7": 1,
-    "warm0": 1, "warm1": 0, "warm2": 1, "warm3": 1,
+    "raw0": 0, "raw1": 1, "raw2": 6, "raw3": 7, "raw4": 2, "raw5": 3, "raw6": 2, "raw7": 3,
+    "warm0": 2, "warm1": 3,
     "flipped_turned0": 2, "flipped_turned1": 3, "flipped_turned1_0": 4, "flipped_turned1_1": 5,
     "flipped_turned2_0": 4, "flipped_turned2_1": 5, "flipped_turned6": 4, "flipped_turned7": 5,
-    "sums0": 6, "sums1": 7, "sums2": 6, "sums3": 7, "sums4": 0, "sums5": 1, "sums6": 6, "sums7": 4,
-    **{"weighted_turned%d" % b: 2 + b % 2 for b in range(8)}}
+    "sums0": 6, "sums1": 7, "sums2": 6, "sums3": 7, "sums4": 2, "sums5": 3, "sums6": 6, "sums7": 4,
+    **{"weighted_turned%d" % b: b % 2 for b in range(8)}}
+X_CODE_TAGS = {}
+H_TAGS = {}
 
 F32 = mybir.dt.float32
 BF16 = mybir.dt.bfloat16
@@ -46,7 +48,6 @@ def tile_attend_gsqh_x_ts_kernel(tc, xT, wT, y, wt, ts, offs, out):
     nc = tc.nc
     with ExitStack() as ctx:
         keep = ctx.enter_context(tc.tile_pool(name="keep", bufs=1))
-        shared = ctx.enter_context(tc.tile_pool(name="shared", bufs=1))
         first = ctx.enter_context(tc.tile_pool(name="first", bufs=1))
         psum = ctx.enter_context(tc.psum_pool(name="psum", bufs=1))
 
@@ -68,10 +69,7 @@ def tile_attend_gsqh_x_ts_kernel(tc, xT, wT, y, wt, ts, offs, out):
         w_rows = wT.rearrange("(p f) c -> p f c", f=PACK)
         w_planes = []
         for f in range(PACK):
-            if f < PACK - 1:
-                plane = sbuf([P, T], F32, "w_plane%d" % f)
-            else:
-                plane = shared.tile([P, T], F32, name="w_plane_last", offset=0, align_bytes=64)
+            plane = sbuf([P, T], F32, "w_plane%d" % f)
             nc.sync.dma_start(plane[:], w_rows[:, f, :])
             w_planes.append(plane)
             if f == 0:
@@ -169,7 +167,6 @@ def tile_attend_gsqh_x_ts_kernel(tc, xT, wT, y, wt, ts, offs, out):
             if f < EARLY:
                 sign_w_scalar(f)
         copy_w(EARLY, None)
-        w_late = shared.tile([P, PACK - EARLY, P, PACK], BF16, name="w_late", offset=0, align_bytes=64)
 
         w1_codes = sbuf([P, N], U32, "w1_codes")
         w1_scales = sbuf([P, N], U8, "w1_scales")
@@ -191,7 +188,7 @@ def tile_attend_gsqh_x_ts_kernel(tc, xT, wT, y, wt, ts, offs, out):
                 in_=values[:].rearrange("s f p t -> s (f p t)"),
             )
 
-        x_codes = sbuf([P, R], U32, "x_codes")
+        x_codes = {}
         x_scales = sbuf([P, R], U8, "x_scales")
         h_codes = {}
         h_scales = sbuf([P, R], U8, "h_scales")
@@ -213,9 +210,7 @@ def tile_attend_gsqh_x_ts_kernel(tc, xT, wT, y, wt, ts, offs, out):
 
         def group_x(b, count=1, copy=nc.scalar.copy):
             k, j = divmod(b, CHUNK_BLOCKS)
-            if b == CHUNK_BLOCKS:
-                x_grouped[k] = first.tile([P, CHUNK_ROWS, PACK], BF16, name="x_grouped1", offset=4 * D, align_bytes=64)
-            elif j == 0:
+            if j == 0:
                 x_grouped[k] = sbuf([P, CHUNK_ROWS, PACK], BF16, "x_grouped%d" % k, GROUP_TAGS.get(k))
             copy(
                 x_grouped[k][:, rows_of(j, count), :].rearrange("p (c i) f -> p c f i", i=PACK),
@@ -224,8 +219,10 @@ def tile_attend_gsqh_x_ts_kernel(tc, xT, wT, y, wt, ts, offs, out):
 
         def quantize_x(b, count):
             k, j = divmod(b, CHUNK_BLOCKS)
+            if j == 0:
+                x_codes[k] = sbuf([P, CHUNK_ROWS], U32, "x_codes%d" % k, X_CODE_TAGS.get(k))
             nc.vector.quantize_mx(
-                out=x_codes[:, rows_of(b, count)].bitcast(E4M3),
+                out=x_codes[k][:, rows_of(j, count)].bitcast(E4M3),
                 scales=x_scales[:, rows_of(b, count)],
                 in_=x_grouped[k][:, rows_of(j, count), :].rearrange("p r f -> p (r f)"),
             )
@@ -234,7 +231,7 @@ def tile_attend_gsqh_x_ts_kernel(tc, xT, wT, y, wt, ts, offs, out):
             raw[b] = bank([P, N], F32, "raw%d" % b)
             nc.tensor.matmul_mx(
                 out=raw[b][:],
-                lhsT=x_codes[:, rows_of(b)].bitcast(E4M3),
+                lhsT=x_codes[b // CHUNK_BLOCKS][:, rows_of(b % CHUNK_BLOCKS)].bitcast(E4M3),
                 lhsT_scale=x_scales[:, rows_of(b)],
                 rhs=w1_codes[:].bitcast(E4M3),
                 rhs_scale=w1_scales[:],
@@ -242,13 +239,13 @@ def tile_attend_gsqh_x_ts_kernel(tc, xT, wT, y, wt, ts, offs, out):
                 stop=True,
             )
 
-        def warm_up(name, width, first):
+        def warm_up(name, width):
             unread = bank([P, width], F32, name)
             moving, moving_scales = w1_codes, w1_scales
             nc.tensor.matmul_mx(
                 out=unread[:],
-                lhsT=w2_codes[0][:, first : first + P].bitcast(E4M3),
-                lhsT_scale=w2_scales[:, first : first + P],
+                lhsT=x_codes[0][:, rows_of(1)].bitcast(E4M3),
+                lhsT_scale=x_scales[:, rows_of(1)],
                 rhs=moving[:, 0:width].bitcast(E4M3),
                 rhs_scale=moving_scales[:, 0:width],
                 start=True,
@@ -320,7 +317,10 @@ def tile_attend_gsqh_x_ts_kernel(tc, xT, wT, y, wt, ts, offs, out):
         def weigh(b):
             if b in runs:
                 count, tag = runs[b]
-                space = sbuf([P, count, N], F32, "weighted_run%d" % b, tag)
+                if tag == "w_late":
+                    space = first.tile([P, count, N], F32, name="weighted_run%d" % b, offset=4 * D, align_bytes=64)
+                else:
+                    space = sbuf([P, count, N], F32, "weighted_run%d" % b, tag)
                 for j in range(count):
                     weighted[b + j] = space[:, j, :]
             nc.gpsimd.tensor_scalar(as_dealt(weighted[b]), labels(b), wt_minus[:, b : b + 1], 0.0, MULT, ADD)
@@ -328,12 +328,14 @@ def tile_attend_gsqh_x_ts_kernel(tc, xT, wT, y, wt, ts, offs, out):
         def turn_weighted(b):
             weighted_turned[b] = turn("weighted_turned%d" % b, weighted[b])
 
-        def gradient(b):
-            h_grouped[b] = sbuf([P, P, PACK], BF16, "h_grouped%d" % b)
+        def gradient(b, first=0, count=P):
+            if first == 0:
+                h_grouped[b] = sbuf([P, P, PACK], BF16, "h_grouped%d" % b, H_TAGS.get(b))
+            rows = slice(first, first + count)
             nc.vector.tensor_tensor(
-                h_grouped[b][:].rearrange("s (c i) t -> s c t i", i=PACK),
-                slack[b].rearrange("s t (c i) -> s c t i", i=PACK),
-                weighted_turned[b][:].rearrange("s t (c i) -> s c t i", i=PACK),
+                h_grouped[b][:, rows, :].rearrange("s (c i) t -> s c t i", i=PACK),
+                slack[b][:, :, rows].rearrange("s t (c i) -> s c t i", i=PACK),
+                weighted_turned[b][:, :, rows].rearrange("s t (c i) -> s c t i", i=PACK),
                 MULT,
             )
 
@@ -369,40 +371,40 @@ def tile_attend_gsqh_x_ts_kernel(tc, xT, wT, y, wt, ts, offs, out):
                 nc.sync.dma_start(out[0, rows_of(b), cols], result[:, cols])
 
         quantize_w1()
-        sign_w_vector(2)
-        group_x(0)
-        group_x(1)
+        turn_w(PACK - 1)
+        for b in range(4):
+            group_x(b)
+        copy_w(PACK - 1, "x_raw1")
         quantize_x(0, 1)
         quantize_x(1, 1)
-        turn_w(PACK - 1)
         scores(0)
         scores(1)
-        copy_w(PACK - 1, None)
-        group_x(2, 2, nc.vector.tensor_copy)
+        warm_up("warm0", N)
+        warm_up("warm1", N)
         w2_codes.append(first.tile([P, D], U32, name="w2_codes", offset=0, align_bytes=64))
         quantize_w2(0, w_early)
+        w_late = first.tile([P, PACK - EARLY, P, PACK], BF16, name="w_late", offset=4 * D, align_bytes=64)
+        sign_w_vector(2)
+        weigh_scalar(0)
+        weigh(1)
+        flip(0)
+        turn_flipped(0)
+        turn_weighted(0)
+        flip(1)
+        turn_flipped(1)
         quantize_x(2, 2)
         scores(2)
         scores(3)
-        weigh_scalar(0)
-        weigh_scalar(1)
-        flip(0)
-        turn_flipped(0)
-        flip(1)
-        turn_flipped(1)
+        turn_weighted(1)
+        sign_w_vector(3)
+        quantize_w2(EARLY, w_late)
+        group_x(4)
+        group_x(5)
         hinge(0)
         hinge(1)
-        sign_w_vector(3)
-        group_x(4, 2, nc.vector.tensor_copy)
-        quantize_w2(EARLY, w_late)
-        warm_up("warm0", N, 0)
-        warm_up("warm1", N, D - P)
-        warm_up("warm2", N, D - P)
-        turn_weighted(0)
         weigh(2)
         flip(2)
         turn_flipped(2)
-        turn_weighted(1)
         flip(3)
         turn_flipped(3)
         quantize_x(4, 2)
@@ -417,20 +419,20 @@ def tile_attend_gsqh_x_ts_kernel(tc, xT, wT, y, wt, ts, offs, out):
         turn_weighted(2)
         turn_weighted(3)
         quantize_h(0)
-        quantize_x(6, 2)
         quantize_h(1)
         product(0)
         product(1)
         weigh(4)
-        weigh(5)
         flip(4)
         turn_flipped(4)
         flip(5)
         turn_flipped(5)
         store(0, nc.scalar.copy)
         store(1, nc.scalar.copy)
+        quantize_x(6, 2)
         scores(6)
         scores(7)
+        weigh(5)
         hinge(4)
         gradient(2)
         gradient(3)
@@ -449,23 +451,23 @@ def tile_attend_gsqh_x_ts_kernel(tc, xT, wT, y, wt, ts, offs, out):
         store(2, nc.scalar.copy)
         hinge(6)
         hinge(7)
-        warm_up("warm3", N, 0)
         gradient(4)
         turn_weighted(6)
         gradient(5)
         turn_weighted(7)
         quantize_h(4)
-        quantize_h(5)
         product(4)
-        product(5)
         store(3, nc.vector.tensor_copy)
+        quantize_h(5)
+        product(5)
         store(4, nc.scalar.copy)
         store(5, nc.scalar.copy)
         gradient(6)
+        gradient(7, 0, P // 2)
         quantize_h(6)
         product(6)
-        gradient(7)
+        store(6, nc.scalar.copy)
+        gradient(7, P // 2, P // 2)
         quantize_h(7)
         product(7)
-        store(6, nc.scalar.copy)
         store(7, nc.vector.tensor_copy, 2)

@@ -213,8 +213,8 @@ def tile_attend_gsqh_x_ts_kernel(tc, xT, wT, y, wt, ts, offs, out):
             if j == 0:
                 x_grouped[k] = sbuf([P, CHUNK_ROWS, PACK], BF16, "x_grouped%d" % k, GROUP_TAGS.get(k))
             copy(
-                x_grouped[k][:, rows_of(j, count), :].rearrange("p (c i) f -> p c f i", i=PACK),
-                x_raw[k][:, :, rows_of(j, count)].rearrange("p f (c i) -> p c f i", i=PACK),
+                x_grouped[k][:, rows_of(j, count), :].rearrange("p (c i) f -> p c f i", i=2),
+                x_raw[k][:, :, rows_of(j, count)].rearrange("p f (c i) -> p c f i", i=2),
             )
 
         def quantize_x(b, count):
@@ -333,18 +333,19 @@ def tile_attend_gsqh_x_ts_kernel(tc, xT, wT, y, wt, ts, offs, out):
                 h_grouped[b] = sbuf([P, P, PACK], BF16, "h_grouped%d" % b, H_TAGS.get(b))
             rows = slice(first, first + count)
             nc.vector.tensor_tensor(
-                h_grouped[b][:, rows, :].rearrange("s (c i) t -> s c t i", i=PACK),
-                slack[b][:, :, rows].rearrange("s t (c i) -> s c t i", i=PACK),
-                weighted_turned[b][:, :, rows].rearrange("s t (c i) -> s c t i", i=PACK),
+                h_grouped[b][:, rows, :].rearrange("s (c i) t -> s c t i", i=2),
+                slack[b][:, :, rows].rearrange("s t (c i) -> s c t i", i=2),
+                weighted_turned[b][:, :, rows].rearrange("s t (c i) -> s c t i", i=2),
                 MULT,
             )
 
-        def quantize_h(b):
-            h_codes[b] = sbuf([P, P], U32, "h_codes%d" % b, CODE_TAGS.get(b))
+        def quantize_h(b, first=0, count=P):
+            if first == 0:
+                h_codes[b] = sbuf([P, P], U32, "h_codes%d" % b, CODE_TAGS.get(b))
             nc.vector.quantize_mx(
-                out=h_codes[b][:].bitcast(E5M2),
-                scales=h_scales[:, rows_of(b)],
-                in_=h_grouped[b][:].rearrange("s r t -> s (r t)"),
+                out=h_codes[b][:, first : first + count].bitcast(E5M2),
+                scales=h_scales[:, b * P + first : b * P + first + count],
+                in_=h_grouped[b][:, first : first + count, :].rearrange("s r t -> s (r t)"),
             )
 
         def product(b):
@@ -359,16 +360,25 @@ def tile_attend_gsqh_x_ts_kernel(tc, xT, wT, y, wt, ts, offs, out):
                 stop=True,
             )
 
+        results = {}
+
+        def copy_out(b, copy, first, width):
+            if first == 0:
+                results[b] = sbuf([P, D], F32, "result%d" % b, RESULT_TAGS.get(b))
+            copy(
+                results[b][:, first * PACK : (first + width) * PACK].rearrange("r (p f) -> r p f", f=PACK),
+                sums[b][:].rearrange("r (f p) -> r p f", f=PACK)[:, first : first + width, :],
+            )
+
+        def send(b, first, width):
+            cols = slice(first * PACK, (first + width) * PACK)
+            nc.sync.dma_start(out[0, rows_of(b), cols], results[b][:, cols])
+
         def store(b, copy, pieces=1):
             width = P // pieces
-            result = sbuf([P, D], F32, "result%d" % b, RESULT_TAGS.get(b))
             for first in range(0, P, width):
-                cols = slice(first * PACK, (first + width) * PACK)
-                copy(
-                    result[:, cols].rearrange("r (p f) -> r p f", f=PACK),
-                    sums[b][:].rearrange("r (f p) -> r p f", f=PACK)[:, first : first + width, :],
-                )
-                nc.sync.dma_start(out[0, rows_of(b), cols], result[:, cols])
+                copy_out(b, copy, first, width)
+                send(b, first, width)
 
         quantize_w1()
         turn_w(PACK - 1)
@@ -449,6 +459,7 @@ def tile_attend_gsqh_x_ts_kernel(tc, xT, wT, y, wt, ts, offs, out):
         flip(7)
         turn_flipped(7)
         store(2, nc.scalar.copy)
+        copy_out(3, nc.scalar.copy, 0, P // 2)
         hinge(6)
         hinge(7)
         gradient(4)
@@ -457,7 +468,8 @@ def tile_attend_gsqh_x_ts_kernel(tc, xT, wT, y, wt, ts, offs, out):
         turn_weighted(7)
         quantize_h(4)
         product(4)
-        store(3, nc.vector.tensor_copy)
+        copy_out(3, nc.vector.tensor_copy, P // 2, P // 2)
+        send(3, 0, P)
         quantize_h(5)
         product(5)
         store(4, nc.scalar.copy)
@@ -468,6 +480,7 @@ def tile_attend_gsqh_x_ts_kernel(tc, xT, wT, y, wt, ts, offs, out):
         product(6)
         store(6, nc.scalar.copy)
         gradient(7, P // 2, P // 2)
-        quantize_h(7)
+        quantize_h(7, 0, P // 2)
+        quantize_h(7, P // 2, P // 2)
         product(7)
         store(7, nc.vector.tensor_copy, 2)

@@ -5,32 +5,23 @@ from concourse.masks import make_identity
 
 D, T, N, R = 512, 2048, 512, 1024
 P = 128
+HALF = P // 2
 PACK = 4
 RUN = 8
-BANKS = 8
-EARLY = 2
-BLOCKS = R // P
 CHUNK_ROWS = 256
-CHUNK_BLOCKS = CHUNK_ROWS // P
+PAIR = CHUNK_ROWS // P
+CHUNKS = R // CHUNK_ROWS
+BLOCKS = R // P
+EARLY = 2
+WALK = 2
+
+SCORE_BANKS = (0, 1, 6, 7, 2, 3, 2, 3)
+FLIP_BANKS = ((2, 3), (4, 5), (4, 5), (4, 5))
+WEIGHT_BANKS = (0, 1)
+SUM_BANKS = (6, 7, 6, 7, 2, 3, 6, 4)
 
 FLOPS = 2 * 2 * R * N * D
 BYTES = 4 * (D * R + D * T + R * N + R + T + R * D) + 2 * P * (N // 16)
-
-FLIP_TAGS = {2: "h_grouped0", 3: "h_grouped2"}
-GROUP_TAGS = {3: "flipped_pair0"}
-RESULT_TAGS = {}
-PAIRS = (1, 2)
-RUNS = {1: (1, "w_unsigned2"), 2: (1, "w_late"), 3: (1, "x_grouped2"), 4: (1, "h_grouped1"), 5: (1, "flipped_pair0"), 6: (2, "h_grouped3")}
-CODE_TAGS = {}
-BANK_OF = {"wt_turned": 0, "ts_turned": 1, "w_turned0": 2, "w_turned1": 3, "w_turned2": 4, "w_turned3": 5,
-    "raw0": 0, "raw1": 1, "raw2": 6, "raw3": 7, "raw4": 2, "raw5": 3, "raw6": 2, "raw7": 3,
-    "warm0": 2, "warm1": 3,
-    "flipped_turned0": 2, "flipped_turned1": 3, "flipped_turned1_0": 4, "flipped_turned1_1": 5,
-    "flipped_turned2_0": 4, "flipped_turned2_1": 5, "flipped_turned6": 4, "flipped_turned7": 5,
-    "sums0": 6, "sums1": 7, "sums2": 6, "sums3": 7, "sums4": 2, "sums5": 3, "sums6": 6, "sums7": 4,
-    **{"weighted_turned%d" % b: b % 2 for b in range(8)}}
-X_CODE_TAGS = {}
-H_TAGS = {}
 
 F32 = mybir.dt.float32
 BF16 = mybir.dt.bfloat16
@@ -48,22 +39,25 @@ def tile_attend_gsqh_x_ts_kernel(tc, xT, wT, y, wt, ts, offs, out):
     nc = tc.nc
     with ExitStack() as ctx:
         keep = ctx.enter_context(tc.tile_pool(name="keep", bufs=1))
-        first = ctx.enter_context(tc.tile_pool(name="first", bufs=1))
+        opening = ctx.enter_context(tc.tile_pool(name="opening", bufs=1))
         psum = ctx.enter_context(tc.psum_pool(name="psum", bufs=1))
 
-        def sbuf(shape, dtype, name, tag=None):
-            return keep.tile(shape, dtype, name=name, tag=tag or name, align_bytes=64)
+        def sbuf(shape, dtype, name, reuse=None):
+            return keep.tile(shape, dtype, name=name, tag=reuse or name, align_bytes=64)
 
-        def bank(shape, dtype, name):
-            return psum.tile(shape, dtype, name=name, tag="bank%d" % BANK_OF[name])
+        def on_first_x(shape, dtype, name, half):
+            return opening.tile(shape, dtype, name=name, offset=half * 4 * D, align_bytes=64)
+
+        def bank(index, shape, dtype, name):
+            return psum.tile(shape, dtype, name=name, tag="bank%d" % index)
 
         offsets = keep.tile([P, N // 16], U16, name="offsets")
         nc.sync.dma_start(offsets[:], offs)
 
-        wt_rows = sbuf([P, P], F32, "wt_rows")
+        wt_rows = sbuf([P, CHUNK_ROWS], F32, "wt_rows")
         ts_window = sbuf([P, T], F32, "ts_window")
-        nc.sync.dma_start(ts_window[P - 1 : P, :], ts[0:1, :])
-        nc.vector.memset(wt_rows[0 : P - BLOCKS, :], 0.0)
+        nc.scalar.dma_start(ts_window[P - 1 : P, :], ts[0:1, :])
+        nc.vector.memset(wt_rows[0 : P - CHUNKS, :], 0.0)
         nc.vector.memset(ts_window[0 : P - 1, :], 0.0)
 
         w_rows = wT.rearrange("(p f) c -> p f c", f=PACK)
@@ -73,29 +67,32 @@ def tile_attend_gsqh_x_ts_kernel(tc, xT, wT, y, wt, ts, offs, out):
             nc.sync.dma_start(plane[:], w_rows[:, f, :])
             w_planes.append(plane)
             if f == 0:
-                nc.sync.dma_start(wt_rows[P - BLOCKS : P, :], wt[0].rearrange("(b p) o -> b (p o)", p=P))
+                nc.scalar.dma_start(
+                    wt_rows[P - CHUNKS : P, :], wt[0].rearrange("(k r) o -> k (r o)", r=CHUNK_ROWS)
+                )
 
         x_rows = xT[0].rearrange("(p f) r -> p f r", f=PACK)
-        y_rows = y[0].rearrange("(k j p) i -> k p j i", p=P, j=CHUNK_BLOCKS)
+        y_rows = y[0].rearrange("(k p j) i -> k p j i", p=P, j=PAIR)
+        out_rows = out[0].rearrange("(k p j) d -> k j p d", p=P, j=PAIR)
         x_raw = {}
         y_raw = {}
 
         def load_x(k):
             if k == 0:
-                x_raw[k] = first.tile([P, PACK, CHUNK_ROWS], F32, name="x_raw0", offset=0, align_bytes=64)
+                x_raw[k] = on_first_x([P, PACK, CHUNK_ROWS], F32, "x_raw0", 0)
             else:
                 x_raw[k] = sbuf([P, PACK, CHUNK_ROWS], F32, "x_raw%d" % k)
             nc.sync.dma_start(x_raw[k][:], x_rows[:, :, k * CHUNK_ROWS : (k + 1) * CHUNK_ROWS])
 
         def load_y(k):
-            y_raw[k] = sbuf([P, CHUNK_BLOCKS, N], F32, "y_raw%d" % k)
+            y_raw[k] = sbuf([P, PAIR, N], F32, "y_raw%d" % k)
             nc.sync.dma_start(y_raw[k][:], y_rows[k])
 
         load_x(0)
-        for k in range(1, R // CHUNK_ROWS):
+        for k in range(1, CHUNKS):
             load_x(k)
             load_y(k - 1)
-        load_y(R // CHUNK_ROWS - 1)
+        load_y(CHUNKS - 1)
 
         ident_f32 = sbuf([P, P], F32, "ident_f32")
         make_identity(nc, ident_f32[:])
@@ -108,27 +105,31 @@ def tile_attend_gsqh_x_ts_kernel(tc, xT, wT, y, wt, ts, offs, out):
         def as_dealt(slots):
             return slots.rearrange("p (t g j) -> p t g j", t=PACK, j=RUN)
 
-        wt_turned = bank([P, P], F32, "wt_turned")
-        nc.tensor.transpose(wt_turned[:], wt_rows[:], ident_f32[:])
+        wt_turned = bank(0, [P, PAIR, P], F32, "wt_turned")
+        for j in range(PAIR):
+            nc.tensor.transpose(wt_turned[:, j, :], wt_rows[:, j::PAIR], ident_f32[:])
         wt_minus = sbuf([P, BLOCKS], F32, "wt_minus")
-        nc.scalar.activation(wt_minus[:], wt_turned[:, P - BLOCKS : P], ACT.Copy, scale=-1.0)
+        nc.scalar.activation(
+            wt_minus[:].rearrange("p (k j) -> p j k", j=PAIR), wt_turned[:, :, P - CHUNKS : P], ACT.Copy, scale=-1.0
+        )
 
         ts_listed = sbuf([P, N], F32, "ts_listed")
         nc.vector.tensor_copy(ts_listed[:], ts_window[:].indirect(offsets[:]))
         ts_dealt = sbuf([P, N], F32, "ts_dealt")
         nc.scalar.copy(as_dealt(ts_dealt[:]), dealt(ts_listed[:]))
-        ts_turned = bank([P, PACK, P], F32, "ts_turned")
+        ts_turned = bank(1, [P, PACK, P], F32, "ts_turned")
         for t in range(PACK):
             nc.tensor.transpose(ts_turned[:, t, :], ts_dealt[:, t * P : (t + 1) * P], ident_f32[:])
+        ts_by_place = ts_turned[:, :, P - 1]
         ts_size = sbuf([P, PACK], F32, "ts_size")
         ts_sign = sbuf([P, PACK], F32, "ts_sign")
         ts_minus = sbuf([P, PACK], F32, "ts_minus")
         ts_slope = sbuf([P, PACK], F32, "ts_slope")
-        nc.scalar.activation(ts_sign[:], ts_turned[:, :, P - 1], ACT.Sign)
+        nc.scalar.activation(ts_sign[:], ts_by_place, ACT.Sign)
         ts_sign_bf16 = sbuf([P, PACK], BF16, "ts_sign_bf16")
-        nc.scalar.activation(ts_sign_bf16[:], ts_turned[:, :, P - 1], ACT.Sign)
-        nc.scalar.activation(ts_size[:], ts_turned[:, :, P - 1], ACT.Abs)
-        nc.scalar.activation(ts_minus[:], ts_turned[:, :, P - 1], ACT.Copy, scale=-1.0)
+        nc.scalar.activation(ts_sign_bf16[:], ts_by_place, ACT.Sign)
+        nc.scalar.activation(ts_size[:], ts_by_place, ACT.Abs)
+        nc.scalar.activation(ts_minus[:], ts_by_place, ACT.Copy, scale=-1.0)
         nc.gpsimd.tensor_tensor(ts_slope[:], ts_minus[:], ts_size[:], MULT)
 
         w_by_d = sbuf([P, N, PACK], BF16, "w_by_d")
@@ -138,21 +139,21 @@ def tile_attend_gsqh_x_ts_kernel(tc, xT, wT, y, wt, ts, offs, out):
         w_unsigned = {}
 
         def turn_w(f):
-            w_turned[f] = bank([P, PACK, P], BF16, "w_turned%d" % f)
+            w_turned[f] = bank(2 + f, [P, PACK, P], BF16, "w_turned%d" % f)
             for t in range(PACK):
                 nc.tensor.transpose(w_turned[f][:, t, :], w_by_d[:, t * P : (t + 1) * P, f], ident_bf16[:])
 
-        def sign_w_scalar(f):
+        def sign_early(f):
             for t in range(PACK):
                 nc.scalar.activation(
                     w_early[:, f, :, t], w_turned[f][:, t, :], ACT.Copy, scale=ts_sign[:, t : t + 1]
                 )
 
-        def copy_w(f, tag):
-            w_unsigned[f] = sbuf([P, P, PACK], BF16, "w_unsigned%d" % f, tag)
+        def copy_late(f, reuse=None):
+            w_unsigned[f] = sbuf([P, P, PACK], BF16, "w_unsigned%d" % f, reuse)
             nc.scalar.copy(w_unsigned[f][:], w_turned[f][:].rearrange("s t p -> s p t"))
 
-        def sign_w_vector(f):
+        def sign_late(f):
             nc.vector.tensor_tensor(
                 w_late[:, f - EARLY],
                 w_unsigned[f][:],
@@ -165,34 +166,25 @@ def tile_attend_gsqh_x_ts_kernel(tc, xT, wT, y, wt, ts, offs, out):
             if f < PACK - 1:
                 turn_w(f)
             if f < EARLY:
-                sign_w_scalar(f)
-        copy_w(EARLY, None)
+                sign_early(f)
+        copy_late(EARLY)
 
         w1_codes = sbuf([P, N], U32, "w1_codes")
         w1_scales = sbuf([P, N], U8, "w1_scales")
-
-        def quantize_w1():
-            nc.vector.quantize_mx(
-                out=w1_codes[:].bitcast(E4M3),
-                scales=w1_scales[:],
-                in_=w_by_d[:].rearrange("p i f -> p (i f)"),
-            )
-
-        w2_codes = []
         w2_scales = sbuf([P, D], U8, "w2_scales")
 
-        def quantize_w2(first, values):
+        def quantize_w2(first_plane, planes):
+            columns = slice(first_plane * P, (first_plane + 2) * P)
             nc.vector.quantize_mx(
-                out=w2_codes[0][:, first * P : (first + 2) * P].bitcast(E4M3),
-                scales=w2_scales[:, first * P : (first + 2) * P],
-                in_=values[:].rearrange("s f p t -> s (f p t)"),
+                out=w2_codes[:, columns].bitcast(E4M3),
+                scales=w2_scales[:, columns],
+                in_=planes[:].rearrange("s f p t -> s (f p t)"),
             )
 
-        x_codes = {}
         x_scales = sbuf([P, R], U8, "x_scales")
-        h_codes = {}
         h_scales = sbuf([P, R], U8, "h_scales")
         x_grouped = {}
+        x_codes = {}
         raw = {}
         flipped = {}
         flipped_turned = {}
@@ -200,266 +192,231 @@ def tile_attend_gsqh_x_ts_kernel(tc, xT, wT, y, wt, ts, offs, out):
         weighted_turned = {}
         slack = {}
         h_grouped = {}
+        h_codes = {}
         sums = {}
+        results = {}
 
-        def rows_of(b, count=1):
+        def columns_of(b, count=1):
             return slice(b * P, (b + count) * P)
 
-        def gpsimd_round(target, source):
-            nc.gpsimd.tensor_scalar(target, source, 1.0, 0.0, MULT, ADD)
+        def group_x(k, reuse=None):
+            x_grouped[k] = sbuf([P, CHUNK_ROWS, PACK], BF16, "x_grouped%d" % k, reuse)
+            for j in range(PAIR):
+                nc.scalar.copy(
+                    x_grouped[k][:, columns_of(j), :].rearrange("p (c i) f -> p c f i", i=WALK),
+                    x_raw[k][:].rearrange("p f (c i j) -> p j c f i", i=WALK, j=PAIR)[:, j],
+                )
 
-        def group_x(b, count=1, copy=nc.scalar.copy):
-            k, j = divmod(b, CHUNK_BLOCKS)
-            if j == 0:
-                x_grouped[k] = sbuf([P, CHUNK_ROWS, PACK], BF16, "x_grouped%d" % k, GROUP_TAGS.get(k))
-            copy(
-                x_grouped[k][:, rows_of(j, count), :].rearrange("p (c i) f -> p c f i", i=2),
-                x_raw[k][:, :, rows_of(j, count)].rearrange("p f (c i) -> p c f i", i=2),
-            )
+        def quantize_x(k, calls=1):
+            x_codes[k] = sbuf([P, CHUNK_ROWS], U32, "x_codes%d" % k)
+            count = PAIR // calls
+            for j in range(0, PAIR, count):
+                nc.vector.quantize_mx(
+                    out=x_codes[k][:, columns_of(j, count)].bitcast(E4M3),
+                    scales=x_scales[:, columns_of(PAIR * k + j, count)],
+                    in_=x_grouped[k][:, columns_of(j, count), :].rearrange("p r f -> p (r f)"),
+                )
 
-        def quantize_x(b, count):
-            k, j = divmod(b, CHUNK_BLOCKS)
-            if j == 0:
-                x_codes[k] = sbuf([P, CHUNK_ROWS], U32, "x_codes%d" % k, X_CODE_TAGS.get(k))
-            nc.vector.quantize_mx(
-                out=x_codes[k][:, rows_of(j, count)].bitcast(E4M3),
-                scales=x_scales[:, rows_of(b, count)],
-                in_=x_grouped[k][:, rows_of(j, count), :].rearrange("p r f -> p (r f)"),
-            )
-
-        def scores(b):
-            raw[b] = bank([P, N], F32, "raw%d" % b)
+        def score_pass(target, b):
             nc.tensor.matmul_mx(
-                out=raw[b][:],
-                lhsT=x_codes[b // CHUNK_BLOCKS][:, rows_of(b % CHUNK_BLOCKS)].bitcast(E4M3),
-                lhsT_scale=x_scales[:, rows_of(b)],
+                out=target[:],
+                lhsT=x_codes[b // PAIR][:, columns_of(b % PAIR)].bitcast(E4M3),
+                lhsT_scale=x_scales[:, columns_of(b)],
                 rhs=w1_codes[:].bitcast(E4M3),
                 rhs_scale=w1_scales[:],
                 start=True,
                 stop=True,
             )
 
-        def warm_up(name, width):
-            unread = bank([P, width], F32, name)
-            moving, moving_scales = w1_codes, w1_scales
-            nc.tensor.matmul_mx(
-                out=unread[:],
-                lhsT=x_codes[0][:, rows_of(1)].bitcast(E4M3),
-                lhsT_scale=x_scales[:, rows_of(1)],
-                rhs=moving[:, 0:width].bitcast(E4M3),
-                rhs_scale=moving_scales[:, 0:width],
-                start=True,
-                stop=True,
-            )
+        def scores(k):
+            for b in (PAIR * k, PAIR * k + 1):
+                raw[b] = bank(SCORE_BANKS[b], [P, N], F32, "raw%d" % b)
+                score_pass(raw[b], b)
 
         def labels(b):
-            k, j = divmod(b, CHUNK_BLOCKS)
-            return dealt(y_raw[k][:, j, :])
+            return dealt(y_raw[b // PAIR][:, b % PAIR, :])
 
-        def turn(name, source):
-            turned = bank([P, PACK, P], F32, name)
+        def turn(index, name, source):
+            turned = bank(index, [P, PACK, P], F32, name)
             for t in range(PACK):
                 nc.tensor.transpose(turned[:, t, :], source[:, t * P : (t + 1) * P], ident_f32[:])
             return turned
 
-        flipped_pairs = {}
+        def flip_space(k, reuse=None):
+            space = sbuf([P, PAIR, N], F32, "flipped_pair%d" % k, reuse)
+            for j in range(PAIR):
+                flipped[PAIR * k + j] = space[:, j, :]
 
         def flip(b):
-            k, j = divmod(b, CHUNK_BLOCKS)
-            if j == 0:
-                tag = FLIP_TAGS.get(k)
-                flipped_pairs[k] = sbuf([P, CHUNK_BLOCKS, N], F32, "flipped_pair%d" % k, tag)
-            flipped[b] = flipped_pairs[k][:, j, :]
             nc.vector.tensor_tensor(as_dealt(flipped[b]), labels(b), as_dealt(raw[b][:]), MULT)
-
-        PAIRED = PAIRS
-
-        def turn_flipped(b):
-            if b // CHUNK_BLOCKS not in PAIRED:
-                flipped_turned[b] = turn("flipped_turned%d" % b, flipped[b])
-                return
-            k, j = divmod(b, CHUNK_BLOCKS)
-            if j == 0:
-                flipped_turned[b] = [
-                    bank([P, 2, CHUNK_ROWS], F32, "flipped_turned%d_%d" % (k, half)) for half in range(2)
-                ]
-            for t in range(PACK):
-                nc.tensor.transpose(
-                    flipped_turned[b - j][t // 2][:, t % 2, rows_of(j)],
-                    flipped[b][:, t * P : (t + 1) * P],
-                    ident_f32[:],
-                )
 
         def relu(target, source, t):
             nc.scalar.activation(
                 target, source, ACT.Relu, bias=ts_size[:, t : t + 1], scale=ts_slope[:, t : t + 1]
             )
 
+        def turn_flipped(b):
+            flipped_turned[b] = turn(FLIP_BANKS[b // PAIR][b % PAIR], "flipped_turned%d" % b, flipped[b])
+
         def hinge(b):
-            if b // CHUNK_BLOCKS not in PAIRED:
-                slack[b] = sbuf([P, PACK, P], F32, "slack%d" % b)[:]
+            slack[b] = sbuf([P, PACK, P], F32, "slack%d" % b)[:]
+            for t in range(PACK):
+                relu(slack[b][:, t, :], flipped_turned[b][:, t, :], t)
+
+        def flip_and_turn_pair(k):
+            halves = []
+            for j in range(PAIR):
+                flip(PAIR * k + j)
+                if j == 0:
+                    for half in range(2):
+                        name = "flipped_turned%d_%d" % (k, half)
+                        halves.append(bank(FLIP_BANKS[k][half], [P, 2, CHUNK_ROWS], F32, name))
                 for t in range(PACK):
-                    relu(slack[b][:, t, :], flipped_turned[b][:, t, :], t)
-                return
-            k = b // CHUNK_BLOCKS
+                    nc.tensor.transpose(
+                        halves[t // 2][:, t % 2, columns_of(j)],
+                        flipped[PAIR * k + j][:, t * P : (t + 1) * P],
+                        ident_f32[:],
+                    )
+            return halves
+
+        def hinge_pair(k, halves):
             both = sbuf([P, PACK, CHUNK_ROWS], F32, "slack_pair%d" % k)
             for t in range(PACK):
-                relu(both[:, t, :], flipped_turned[b][t // 2][:, t % 2, :], t)
-            for j in range(CHUNK_BLOCKS):
-                slack[b + j] = both[:, :, rows_of(j)]
+                relu(both[:, t, :], halves[t // 2][:, t % 2, :], t)
+            for j in range(PAIR):
+                slack[PAIR * k + j] = both[:, :, columns_of(j)]
 
-        def weigh_scalar(b):
-            weighted[b] = sbuf([P, N], F32, "weighted%d" % b)
-            nc.scalar.activation(as_dealt(weighted[b][:]), labels(b), ACT.Copy, scale=wt_minus[:, b : b + 1])
+        def weigh(b, space):
+            weighted[b] = space
+            nc.gpsimd.tensor_scalar(as_dealt(space), labels(b), wt_minus[:, b : b + 1], 0.0, MULT, ADD)
 
-        runs = RUNS
-
-        def weigh(b):
-            if b in runs:
-                count, tag = runs[b]
-                if tag == "w_late":
-                    space = first.tile([P, count, N], F32, name="weighted_run%d" % b, offset=4 * D, align_bytes=64)
-                else:
-                    space = sbuf([P, count, N], F32, "weighted_run%d" % b, tag)
-                for j in range(count):
-                    weighted[b + j] = space[:, j, :]
-            nc.gpsimd.tensor_scalar(as_dealt(weighted[b]), labels(b), wt_minus[:, b : b + 1], 0.0, MULT, ADD)
+        def weigh_space(b, reuse, count=1):
+            return sbuf([P, count, N], F32, "weighted_run%d" % b, reuse)
 
         def turn_weighted(b):
-            weighted_turned[b] = turn("weighted_turned%d" % b, weighted[b])
+            weighted_turned[b] = turn(WEIGHT_BANKS[b % PAIR], "weighted_turned%d" % b, weighted[b])
 
         def gradient(b, first=0, count=P):
             if first == 0:
-                h_grouped[b] = sbuf([P, P, PACK], BF16, "h_grouped%d" % b, H_TAGS.get(b))
+                h_grouped[b] = sbuf([P, P, PACK], BF16, "h_grouped%d" % b)
             rows = slice(first, first + count)
             nc.vector.tensor_tensor(
-                h_grouped[b][:, rows, :].rearrange("s (c i) t -> s c t i", i=2),
-                slack[b][:, :, rows].rearrange("s t (c i) -> s c t i", i=2),
-                weighted_turned[b][:, :, rows].rearrange("s t (c i) -> s c t i", i=2),
+                h_grouped[b][:, rows, :].rearrange("s (c i) t -> s c t i", i=WALK),
+                slack[b][:, :, rows].rearrange("s t (c i) -> s c t i", i=WALK),
+                weighted_turned[b][:, :, rows].rearrange("s t (c i) -> s c t i", i=WALK),
                 MULT,
             )
 
-        def quantize_h(b, first=0, count=P):
-            if first == 0:
-                h_codes[b] = sbuf([P, P], U32, "h_codes%d" % b, CODE_TAGS.get(b))
-            nc.vector.quantize_mx(
-                out=h_codes[b][:, first : first + count].bitcast(E5M2),
-                scales=h_scales[:, b * P + first : b * P + first + count],
-                in_=h_grouped[b][:, first : first + count, :].rearrange("s r t -> s (r t)"),
-            )
+        def quantize_h(b, calls=1):
+            h_codes[b] = sbuf([P, P], U32, "h_codes%d" % b)
+            count = P // calls
+            for first in range(0, P, count):
+                nc.vector.quantize_mx(
+                    out=h_codes[b][:, first : first + count].bitcast(E5M2),
+                    scales=h_scales[:, b * P + first : b * P + first + count],
+                    in_=h_grouped[b][:, first : first + count, :].rearrange("s r t -> s (r t)"),
+                )
 
         def product(b):
-            sums[b] = bank([P, D], F32, "sums%d" % b)
+            sums[b] = bank(SUM_BANKS[b], [P, D], F32, "sums%d" % b)
             nc.tensor.matmul_mx(
                 out=sums[b][:],
                 lhsT=h_codes[b][:].bitcast(E5M2),
-                lhsT_scale=h_scales[:, rows_of(b)],
-                rhs=w2_codes[0][:].bitcast(E4M3),
+                lhsT_scale=h_scales[:, columns_of(b)],
+                rhs=w2_codes[:].bitcast(E4M3),
                 rhs_scale=w2_scales[:],
                 start=True,
                 stop=True,
             )
 
-        results = {}
-
-        def copy_out(b, copy, first, width):
+        def copy_out(b, copy, first=0, count=P):
             if first == 0:
-                results[b] = sbuf([P, D], F32, "result%d" % b, RESULT_TAGS.get(b))
+                results[b] = sbuf([P, D], F32, "result%d" % b)
             copy(
-                results[b][:, first * PACK : (first + width) * PACK].rearrange("r (p f) -> r p f", f=PACK),
-                sums[b][:].rearrange("r (f p) -> r p f", f=PACK)[:, first : first + width, :],
+                results[b][:, first * PACK : (first + count) * PACK].rearrange("r (p f) -> r p f", f=PACK),
+                sums[b][:].rearrange("r (f p) -> r p f", f=PACK)[:, first : first + count, :],
             )
 
-        def send(b, first, width):
-            cols = slice(first * PACK, (first + width) * PACK)
-            nc.sync.dma_start(out[0, rows_of(b), cols], results[b][:, cols])
+        def send(b, first=0, count=P):
+            features = slice(first * PACK, (first + count) * PACK)
+            nc.sync.dma_start(out_rows[b // PAIR, b % PAIR][:, features], results[b][:, features])
 
-        def store(b, copy, pieces=1):
-            width = P // pieces
-            for first in range(0, P, width):
-                copy_out(b, copy, first, width)
-                send(b, first, width)
+        def store(b):
+            copy_out(b, nc.scalar.copy)
+            send(b)
 
-        quantize_w1()
+        nc.vector.quantize_mx(
+            out=w1_codes[:].bitcast(E4M3), scales=w1_scales[:], in_=w_by_d[:].rearrange("p i f -> p (i f)")
+        )
         turn_w(PACK - 1)
-        for b in range(4):
-            group_x(b)
-        copy_w(PACK - 1, "x_raw1")
-        quantize_x(0, 1)
-        quantize_x(1, 1)
+        group_x(0)
+        group_x(1)
+        copy_late(PACK - 1, "x_raw1")
+        quantize_x(0, calls=PAIR)
         scores(0)
-        scores(1)
-        warm_up("warm0", N)
-        warm_up("warm1", N)
-        w2_codes.append(first.tile([P, D], U32, name="w2_codes", offset=0, align_bytes=64))
+        for index in FLIP_BANKS[0]:
+            score_pass(bank(index, [P, N], F32, "unread%d" % index), 1)
+        w2_codes = on_first_x([P, D], U32, "w2_codes", 0)
         quantize_w2(0, w_early)
-        w_late = first.tile([P, PACK - EARLY, P, PACK], BF16, name="w_late", offset=4 * D, align_bytes=64)
-        sign_w_vector(2)
-        weigh_scalar(0)
-        weigh(1)
+        w_late = on_first_x([P, PACK - EARLY, P, PACK], BF16, "w_late", 1)
+        sign_late(EARLY)
+        weighted[0] = sbuf([P, N], F32, "weighted0")[:]
+        nc.scalar.activation(as_dealt(weighted[0]), labels(0), ACT.Copy, scale=wt_minus[:, 0:1])
+        weigh(1, weigh_space(1, "w_unsigned%d" % EARLY)[:, 0, :])
+        flip_space(0)
         flip(0)
         turn_flipped(0)
         turn_weighted(0)
         flip(1)
         turn_flipped(1)
-        quantize_x(2, 2)
-        scores(2)
-        scores(3)
+        quantize_x(1)
+        scores(1)
         turn_weighted(1)
-        sign_w_vector(3)
+        sign_late(PACK - 1)
         quantize_w2(EARLY, w_late)
-        group_x(4)
-        group_x(5)
+        group_x(2)
         hinge(0)
         hinge(1)
-        weigh(2)
-        flip(2)
-        turn_flipped(2)
-        flip(3)
-        turn_flipped(3)
-        quantize_x(4, 2)
-        scores(4)
-        scores(5)
-        weigh(3)
-        group_x(6)
-        group_x(7)
-        hinge(2)
-        gradient(0)
-        gradient(1)
-        turn_weighted(2)
-        turn_weighted(3)
-        quantize_h(0)
-        quantize_h(1)
-        product(0)
-        product(1)
-        weigh(4)
-        flip(4)
-        turn_flipped(4)
-        flip(5)
-        turn_flipped(5)
-        store(0, nc.scalar.copy)
-        store(1, nc.scalar.copy)
-        quantize_x(6, 2)
-        scores(6)
-        scores(7)
-        weigh(5)
-        hinge(4)
-        gradient(2)
-        gradient(3)
-        turn_weighted(4)
-        turn_weighted(5)
-        quantize_h(2)
-        quantize_h(3)
-        product(2)
-        product(3)
-        weigh(6)
-        weigh(7)
+
+        for k in (1, 2):
+            a, b = PAIR * k, PAIR * k + 1
+            if k == 1:
+                weigh(a, on_first_x([P, 1, N], F32, "weighted_run%d" % a, 1)[:, 0, :])
+                flip_space(k)
+            else:
+                weigh(a, weigh_space(a, "h_grouped%d" % (b - 4))[:, 0, :])
+                flip_space(k, "h_grouped%d" % (a - 4))
+            halves = flip_and_turn_pair(k)
+            if k == 2:
+                store(a - 4)
+                store(b - 4)
+            quantize_x(k + 1)
+            scores(k + 1)
+            if k == 1:
+                weigh(b, weigh_space(b, "x_grouped%d" % (k + 1))[:, 0, :])
+                group_x(k + 2, "flipped_pair0")
+            else:
+                weigh(b, weigh_space(b, "flipped_pair0")[:, 0, :])
+            hinge_pair(k, halves)
+            gradient(a - 2)
+            gradient(b - 2)
+            turn_weighted(a)
+            turn_weighted(b)
+            quantize_h(a - 2)
+            quantize_h(b - 2)
+            product(a - 2)
+            product(b - 2)
+
+        space = weigh_space(6, "h_grouped3", PAIR)
+        weigh(6, space[:, 0, :])
+        weigh(7, space[:, 1, :])
+        flip_space(3, "h_grouped2")
         flip(6)
         turn_flipped(6)
         flip(7)
         turn_flipped(7)
-        store(2, nc.scalar.copy)
-        copy_out(3, nc.scalar.copy, 0, P // 2)
+        store(2)
+        copy_out(3, nc.scalar.copy, 0, HALF)
         hinge(6)
         hinge(7)
         gradient(4)
@@ -468,19 +425,20 @@ def tile_attend_gsqh_x_ts_kernel(tc, xT, wT, y, wt, ts, offs, out):
         turn_weighted(7)
         quantize_h(4)
         product(4)
-        copy_out(3, nc.vector.tensor_copy, P // 2, P // 2)
-        send(3, 0, P)
+        copy_out(3, nc.vector.tensor_copy, HALF, HALF)
+        send(3)
         quantize_h(5)
         product(5)
-        store(4, nc.scalar.copy)
-        store(5, nc.scalar.copy)
+        store(4)
+        store(5)
         gradient(6)
-        gradient(7, 0, P // 2)
+        gradient(7, 0, HALF)
         quantize_h(6)
         product(6)
-        store(6, nc.scalar.copy)
-        gradient(7, P // 2, P // 2)
-        quantize_h(7, 0, P // 2)
-        quantize_h(7, P // 2, P // 2)
+        store(6)
+        gradient(7, HALF, HALF)
+        quantize_h(7, calls=2)
         product(7)
-        store(7, nc.vector.tensor_copy, 2)
+        for first in (0, HALF):
+            copy_out(7, nc.vector.tensor_copy, first, HALF)
+            send(7, first, HALF)

@@ -13,12 +13,14 @@ PAIR = CHUNK_ROWS // P
 CHUNKS = R // CHUNK_ROWS
 BLOCKS = R // P
 EARLY = 2
-WALK = 2
+X_WALK = 4
+H_WALK = 2
 
-SCORE_BANKS = (0, 1, 6, 7, 2, 3, 2, 3)
-FLIP_BANKS = ((2, 3), (4, 5), (4, 5), (4, 5))
-WEIGHT_BANKS = (0, 1)
-SUM_BANKS = (6, 7, 6, 7, 2, 3, 6, 4)
+SCORE_BANKS = (0, 1, 0, 1, 4, 5, 0, 1)
+FLIP_BANKS = (6, 7, 6, 7, 6, 7, 6, 0)
+WEIGHT_BANKS = (4, 5, 0, 1, 4, 5, 1, 4)
+SUM_BANKS = (2, 3, 2, 3, 5, 7, 6, 0)
+TABLE_BANKS = (6, 7, 2, 3)
 
 FLOPS = 2 * 2 * R * N * D
 BYTES = 4 * (D * R + D * T + R * N + R + T + R * D) + 2 * P * (N // 16)
@@ -40,13 +42,17 @@ def tile_attend_gsqh_x_ts_kernel(tc, xT, wT, y, wt, ts, offs, out):
     with ExitStack() as ctx:
         keep = ctx.enter_context(tc.tile_pool(name="keep", bufs=1))
         opening = ctx.enter_context(tc.tile_pool(name="opening", bufs=1))
+        shared = ctx.enter_context(tc.tile_pool(name="shared", bufs=1))
         psum = ctx.enter_context(tc.psum_pool(name="psum", bufs=1))
 
         def sbuf(shape, dtype, name, reuse=None):
             return keep.tile(shape, dtype, name=name, tag=reuse or name, align_bytes=64)
 
-        def on_first_x(shape, dtype, name, half):
-            return opening.tile(shape, dtype, name=name, offset=half * 4 * D, align_bytes=64)
+        def on_first_x(shape, dtype, name, offset):
+            return opening.tile(shape, dtype, name=name, offset=offset, align_bytes=64)
+
+        def placed(shape, dtype, name, offset):
+            return shared.tile(shape, dtype, name=name, offset=offset, align_bytes=64)
 
         def bank(index, shape, dtype, name):
             return psum.tile(shape, dtype, name=name, tag="bank%d" % index)
@@ -54,10 +60,10 @@ def tile_attend_gsqh_x_ts_kernel(tc, xT, wT, y, wt, ts, offs, out):
         offsets = keep.tile([P, N // 16], U16, name="offsets")
         nc.sync.dma_start(offsets[:], offs)
 
-        wt_rows = sbuf([P, CHUNK_ROWS], F32, "wt_rows")
+        wt_rows = sbuf([P, P], F32, "wt_rows")
         ts_window = sbuf([P, T], F32, "ts_window")
         nc.scalar.dma_start(ts_window[P - 1 : P, :], ts[0:1, :])
-        nc.vector.memset(wt_rows[0 : P - CHUNKS, :], 0.0)
+        nc.vector.memset(wt_rows[0 : P - BLOCKS, :], 0.0)
         nc.vector.memset(ts_window[0 : P - 1, :], 0.0)
 
         w_rows = wT.rearrange("(p f) c -> p f c", f=PACK)
@@ -67,19 +73,17 @@ def tile_attend_gsqh_x_ts_kernel(tc, xT, wT, y, wt, ts, offs, out):
             nc.sync.dma_start(plane[:], w_rows[:, f, :])
             w_planes.append(plane)
             if f == 0:
-                nc.scalar.dma_start(
-                    wt_rows[P - CHUNKS : P, :], wt[0].rearrange("(k r) o -> k (r o)", r=CHUNK_ROWS)
-                )
+                nc.scalar.dma_start(wt_rows[P - BLOCKS : P, :], wt[0].rearrange("(b r) o -> b (r o)", r=P))
 
         x_rows = xT[0].rearrange("(p f) r -> p f r", f=PACK)
-        y_rows = y[0].rearrange("(k p j) i -> k p j i", p=P, j=PAIR)
-        out_rows = out[0].rearrange("(k p j) d -> k j p d", p=P, j=PAIR)
+        y_rows = y[0].rearrange("(k j p) i -> k p j i", p=P, j=PAIR)
+        out_rows = out[0].rearrange("(b p) d -> b p d", p=P)
         x_raw = {}
         y_raw = {}
 
         def load_x(k):
             if k == 0:
-                x_raw[k] = on_first_x([P, PACK, CHUNK_ROWS], F32, "x_raw0", 0)
+                x_raw[k] = on_first_x([P, PACK, CHUNK_ROWS], F32, "x_raw0", 1024)
             else:
                 x_raw[k] = sbuf([P, PACK, CHUNK_ROWS], F32, "x_raw%d" % k)
             nc.sync.dma_start(x_raw[k][:], x_rows[:, :, k * CHUNK_ROWS : (k + 1) * CHUNK_ROWS])
@@ -88,11 +92,9 @@ def tile_attend_gsqh_x_ts_kernel(tc, xT, wT, y, wt, ts, offs, out):
             y_raw[k] = sbuf([P, PAIR, N], F32, "y_raw%d" % k)
             nc.sync.dma_start(y_raw[k][:], y_rows[k])
 
-        load_x(0)
-        for k in range(1, CHUNKS):
+        for k in range(CHUNKS):
             load_x(k)
-            load_y(k - 1)
-        load_y(CHUNKS - 1)
+            load_y(k)
 
         ident_f32 = sbuf([P, P], F32, "ident_f32")
         make_identity(nc, ident_f32[:])
@@ -105,19 +107,16 @@ def tile_attend_gsqh_x_ts_kernel(tc, xT, wT, y, wt, ts, offs, out):
         def as_dealt(slots):
             return slots.rearrange("p (t g j) -> p t g j", t=PACK, j=RUN)
 
-        wt_turned = bank(0, [P, PAIR, P], F32, "wt_turned")
-        for j in range(PAIR):
-            nc.tensor.transpose(wt_turned[:, j, :], wt_rows[:, j::PAIR], ident_f32[:])
+        wt_turned = bank(4, [P, P], F32, "wt_turned")
+        nc.tensor.transpose(wt_turned[:], wt_rows[:], ident_f32[:])
         wt_minus = sbuf([P, BLOCKS], F32, "wt_minus")
-        nc.scalar.activation(
-            wt_minus[:].rearrange("p (k j) -> p j k", j=PAIR), wt_turned[:, :, P - CHUNKS : P], ACT.Copy, scale=-1.0
-        )
+        nc.scalar.activation(wt_minus[:], wt_turned[:, P - BLOCKS : P], ACT.Copy, scale=-1.0)
 
         ts_listed = sbuf([P, N], F32, "ts_listed")
         nc.vector.tensor_copy(ts_listed[:], ts_window[:].indirect(offsets[:]))
         ts_dealt = sbuf([P, N], F32, "ts_dealt")
         nc.scalar.copy(as_dealt(ts_dealt[:]), dealt(ts_listed[:]))
-        ts_turned = bank(1, [P, PACK, P], F32, "ts_turned")
+        ts_turned = bank(5, [P, PACK, P], F32, "ts_turned")
         for t in range(PACK):
             nc.tensor.transpose(ts_turned[:, t, :], ts_dealt[:, t * P : (t + 1) * P], ident_f32[:])
         ts_by_place = ts_turned[:, :, P - 1]
@@ -139,7 +138,7 @@ def tile_attend_gsqh_x_ts_kernel(tc, xT, wT, y, wt, ts, offs, out):
         w_unsigned = {}
 
         def turn_w(f):
-            w_turned[f] = bank(2 + f, [P, PACK, P], BF16, "w_turned%d" % f)
+            w_turned[f] = bank(TABLE_BANKS[f], [P, PACK, P], BF16, "w_turned%d" % f)
             for t in range(PACK):
                 nc.tensor.transpose(w_turned[f][:, t, :], w_by_d[:, t * P : (t + 1) * P, f], ident_bf16[:])
 
@@ -149,9 +148,9 @@ def tile_attend_gsqh_x_ts_kernel(tc, xT, wT, y, wt, ts, offs, out):
                     w_early[:, f, :, t], w_turned[f][:, t, :], ACT.Copy, scale=ts_sign[:, t : t + 1]
                 )
 
-        def copy_late(f, reuse=None):
-            w_unsigned[f] = sbuf([P, P, PACK], BF16, "w_unsigned%d" % f, reuse)
-            nc.scalar.copy(w_unsigned[f][:], w_turned[f][:].rearrange("s t p -> s p t"))
+        def copy_late(f, space):
+            w_unsigned[f] = space
+            nc.scalar.copy(space[:], w_turned[f][:].rearrange("s t p -> s p t"))
 
         def sign_late(f):
             nc.vector.tensor_tensor(
@@ -167,7 +166,7 @@ def tile_attend_gsqh_x_ts_kernel(tc, xT, wT, y, wt, ts, offs, out):
                 turn_w(f)
             if f < EARLY:
                 sign_early(f)
-        copy_late(EARLY)
+        copy_late(EARLY, sbuf([P, P, PACK], BF16, "w_unsigned2"))
 
         w1_codes = sbuf([P, N], U32, "w1_codes")
         w1_scales = sbuf([P, N], U8, "w1_scales")
@@ -199,28 +198,28 @@ def tile_attend_gsqh_x_ts_kernel(tc, xT, wT, y, wt, ts, offs, out):
         def columns_of(b, count=1):
             return slice(b * P, (b + count) * P)
 
-        def group_x(k, reuse=None):
-            x_grouped[k] = sbuf([P, CHUNK_ROWS, PACK], BF16, "x_grouped%d" % k, reuse)
-            for j in range(PAIR):
-                nc.scalar.copy(
-                    x_grouped[k][:, columns_of(j), :].rearrange("p (c i) f -> p c f i", i=WALK),
-                    x_raw[k][:].rearrange("p f (c i j) -> p j c f i", i=WALK, j=PAIR)[:, j],
-                )
+        def group_x(b, reuse=None):
+            x_grouped[b] = sbuf([P, P, PACK], BF16, "x_grouped%d" % b, reuse)
+            nc.scalar.copy(
+                x_grouped[b][:].rearrange("p (c i) f -> p c f i", i=X_WALK),
+                x_raw[b // PAIR][:, :, columns_of(b % PAIR)].rearrange("p f (c i) -> p c f i", i=X_WALK),
+            )
 
-        def quantize_x(k, calls=1):
-            x_codes[k] = sbuf([P, CHUNK_ROWS], U32, "x_codes%d" % k)
-            count = PAIR // calls
-            for j in range(0, PAIR, count):
-                nc.vector.quantize_mx(
-                    out=x_codes[k][:, columns_of(j, count)].bitcast(E4M3),
-                    scales=x_scales[:, columns_of(PAIR * k + j, count)],
-                    in_=x_grouped[k][:, columns_of(j, count), :].rearrange("p r f -> p (r f)"),
-                )
+        def group_x_on_gpsimd(b, space):
+            x_grouped[b] = space
+            nc.gpsimd.tensor_scalar(
+                space[:],
+                x_raw[b // PAIR][:, :, columns_of(b % PAIR)].rearrange("p f r -> p r f"),
+                1.0,
+                0.0,
+                MULT,
+                ADD,
+            )
 
         def score_pass(target, b):
             nc.tensor.matmul_mx(
                 out=target[:],
-                lhsT=x_codes[b // PAIR][:, columns_of(b % PAIR)].bitcast(E4M3),
+                lhsT=x_codes[b][:].bitcast(E4M3),
                 lhsT_scale=x_scales[:, columns_of(b)],
                 rhs=w1_codes[:].bitcast(E4M3),
                 rhs_scale=w1_scales[:],
@@ -228,10 +227,15 @@ def tile_attend_gsqh_x_ts_kernel(tc, xT, wT, y, wt, ts, offs, out):
                 stop=True,
             )
 
-        def scores(k):
-            for b in (PAIR * k, PAIR * k + 1):
-                raw[b] = bank(SCORE_BANKS[b], [P, N], F32, "raw%d" % b)
-                score_pass(raw[b], b)
+        def score(b, reuse=None):
+            x_codes[b] = sbuf([P, P], U32, "x_codes%d" % b, reuse)
+            nc.vector.quantize_mx(
+                out=x_codes[b][:].bitcast(E4M3),
+                scales=x_scales[:, columns_of(b)],
+                in_=x_grouped[b][:].rearrange("p r f -> p (r f)"),
+            )
+            raw[b] = bank(SCORE_BANKS[b], [P, N], F32, "raw%d" % b)
+            score_pass(raw[b], b)
 
         def labels(b):
             return dealt(y_raw[b // PAIR][:, b % PAIR, :])
@@ -242,12 +246,8 @@ def tile_attend_gsqh_x_ts_kernel(tc, xT, wT, y, wt, ts, offs, out):
                 nc.tensor.transpose(turned[:, t, :], source[:, t * P : (t + 1) * P], ident_f32[:])
             return turned
 
-        def flip_space(k, reuse=None):
-            space = sbuf([P, PAIR, N], F32, "flipped_pair%d" % k, reuse)
-            for j in range(PAIR):
-                flipped[PAIR * k + j] = space[:, j, :]
-
-        def flip(b):
+        def flip(b, reuse=None):
+            flipped[b] = sbuf([P, N], F32, "flipped%d" % b, reuse)[:]
             nc.vector.tensor_tensor(as_dealt(flipped[b]), labels(b), as_dealt(raw[b][:]), MULT)
 
         def relu(target, source, t):
@@ -256,10 +256,10 @@ def tile_attend_gsqh_x_ts_kernel(tc, xT, wT, y, wt, ts, offs, out):
             )
 
         def turn_flipped(b):
-            flipped_turned[b] = turn(FLIP_BANKS[b // PAIR][b % PAIR], "flipped_turned%d" % b, flipped[b])
+            flipped_turned[b] = turn(FLIP_BANKS[b], "flipped_turned%d" % b, flipped[b])
 
-        def hinge(b):
-            slack[b] = sbuf([P, PACK, P], F32, "slack%d" % b)[:]
+        def hinge(b, reuse=None):
+            slack[b] = sbuf([P, PACK, P], F32, "slack%d" % b, reuse)[:]
             for t in range(PACK):
                 relu(slack[b][:, t, :], flipped_turned[b][:, t, :], t)
 
@@ -270,7 +270,7 @@ def tile_attend_gsqh_x_ts_kernel(tc, xT, wT, y, wt, ts, offs, out):
                 if j == 0:
                     for half in range(2):
                         name = "flipped_turned%d_%d" % (k, half)
-                        halves.append(bank(FLIP_BANKS[k][half], [P, 2, CHUNK_ROWS], F32, name))
+                        halves.append(bank(FLIP_BANKS[PAIR * k + half], [P, 2, CHUNK_ROWS], F32, name))
                 for t in range(PACK):
                     nc.tensor.transpose(
                         halves[t // 2][:, t % 2, columns_of(j)],
@@ -279,8 +279,8 @@ def tile_attend_gsqh_x_ts_kernel(tc, xT, wT, y, wt, ts, offs, out):
                     )
             return halves
 
-        def hinge_pair(k, halves):
-            both = sbuf([P, PACK, CHUNK_ROWS], F32, "slack_pair%d" % k)
+        def hinge_pair(k, halves, reuse=None):
+            both = sbuf([P, PACK, CHUNK_ROWS], F32, "slack_pair%d" % k, reuse)
             for t in range(PACK):
                 relu(both[:, t, :], halves[t // 2][:, t % 2, :], t)
             for j in range(PAIR):
@@ -290,25 +290,29 @@ def tile_attend_gsqh_x_ts_kernel(tc, xT, wT, y, wt, ts, offs, out):
             weighted[b] = space
             nc.gpsimd.tensor_scalar(as_dealt(space), labels(b), wt_minus[:, b : b + 1], 0.0, MULT, ADD)
 
-        def weigh_space(b, reuse, count=1):
-            return sbuf([P, count, N], F32, "weighted_run%d" % b, reuse)
+        def weigh_pair(k, reuse):
+            space = sbuf([P, PAIR, N], F32, "weighted_pair%d" % k, reuse)
+            for j in range(PAIR):
+                weigh(PAIR * k + j, space[:, j, :])
 
         def turn_weighted(b):
-            weighted_turned[b] = turn(WEIGHT_BANKS[b % PAIR], "weighted_turned%d" % b, weighted[b])
+            weighted_turned[b] = turn(WEIGHT_BANKS[b], "weighted_turned%d" % b, weighted[b])
 
-        def gradient(b, first=0, count=P):
-            if first == 0:
+        def gradient(b, first=0, count=P, space=None):
+            if space is not None:
+                h_grouped[b] = space
+            elif first == 0:
                 h_grouped[b] = sbuf([P, P, PACK], BF16, "h_grouped%d" % b)
             rows = slice(first, first + count)
             nc.vector.tensor_tensor(
-                h_grouped[b][:, rows, :].rearrange("s (c i) t -> s c t i", i=WALK),
-                slack[b][:, :, rows].rearrange("s t (c i) -> s c t i", i=WALK),
-                weighted_turned[b][:, :, rows].rearrange("s t (c i) -> s c t i", i=WALK),
+                h_grouped[b][:, rows, :].rearrange("s (c i) t -> s c t i", i=H_WALK),
+                slack[b][:, :, rows].rearrange("s t (c i) -> s c t i", i=H_WALK),
+                weighted_turned[b][:, :, rows].rearrange("s t (c i) -> s c t i", i=H_WALK),
                 MULT,
             )
 
-        def quantize_h(b, calls=1):
-            h_codes[b] = sbuf([P, P], U32, "h_codes%d" % b)
+        def quantize_h(b, calls=1, reuse=None):
+            h_codes[b] = sbuf([P, P], U32, "h_codes%d" % b, reuse)
             count = P // calls
             for first in range(0, P, count):
                 nc.vector.quantize_mx(
@@ -329,9 +333,9 @@ def tile_attend_gsqh_x_ts_kernel(tc, xT, wT, y, wt, ts, offs, out):
                 stop=True,
             )
 
-        def copy_out(b, copy, first=0, count=P):
+        def copy_out(b, copy, first=0, count=P, reuse=None):
             if first == 0:
-                results[b] = sbuf([P, D], F32, "result%d" % b)
+                results[b] = sbuf([P, D], F32, "result%d" % b, reuse)
             copy(
                 results[b][:, first * PACK : (first + count) * PACK].rearrange("r (p f) -> r p f", f=PACK),
                 sums[b][:].rearrange("r (f p) -> r p f", f=PACK)[:, first : first + count, :],
@@ -339,10 +343,10 @@ def tile_attend_gsqh_x_ts_kernel(tc, xT, wT, y, wt, ts, offs, out):
 
         def send(b, first=0, count=P):
             features = slice(first * PACK, (first + count) * PACK)
-            nc.sync.dma_start(out_rows[b // PAIR, b % PAIR][:, features], results[b][:, features])
+            nc.sync.dma_start(out_rows[b][:, features], results[b][:, features])
 
-        def store(b):
-            copy_out(b, nc.scalar.copy)
+        def store(b, reuse=None):
+            copy_out(b, nc.scalar.copy, reuse=reuse)
             send(b)
 
         nc.vector.quantize_mx(
@@ -351,94 +355,103 @@ def tile_attend_gsqh_x_ts_kernel(tc, xT, wT, y, wt, ts, offs, out):
         turn_w(PACK - 1)
         group_x(0)
         group_x(1)
-        copy_late(PACK - 1, "x_raw1")
-        quantize_x(0, calls=PAIR)
-        scores(0)
-        for index in FLIP_BANKS[0]:
-            score_pass(bank(index, [P, N], F32, "unread%d" % index), 1)
+        score(0)
+        score(1)
+        score_pass(bank(FLIP_BANKS[0], [P, N], F32, "unread0"), 1)
+        copy_late(PACK - 1, on_first_x([P, P, PACK], BF16, "w_unsigned3", 4096))
         w2_codes = on_first_x([P, D], U32, "w2_codes", 0)
         quantize_w2(0, w_early)
-        w_late = on_first_x([P, PACK - EARLY, P, PACK], BF16, "w_late", 1)
+        w_late = on_first_x([P, PACK - EARLY, P, PACK], BF16, "w_late", 2048)
         sign_late(EARLY)
         weighted[0] = sbuf([P, N], F32, "weighted0")[:]
         nc.scalar.activation(as_dealt(weighted[0]), labels(0), ACT.Copy, scale=wt_minus[:, 0:1])
-        weigh(1, weigh_space(1, "w_unsigned%d" % EARLY)[:, 0, :])
-        flip_space(0)
+        weigh(1, sbuf([P, N], F32, "weighted1", "w_unsigned2")[:])
         flip(0)
         turn_flipped(0)
-        turn_weighted(0)
         flip(1)
         turn_flipped(1)
-        quantize_x(1)
-        scores(1)
-        turn_weighted(1)
-        sign_late(PACK - 1)
-        quantize_w2(EARLY, w_late)
         group_x(2)
+        group_x(3)
+        score(2)
+        sign_late(PACK - 1)
+        score(3)
+        quantize_w2(EARLY, w_late)
+        turn_weighted(0)
+        turn_weighted(1)
         hinge(0)
-        hinge(1)
+        hinge(1, "x_raw1")
+        space = on_first_x([P, PAIR, N], F32, "weighted_pair1", 2048)
+        weigh(2, space[:, 0, :])
+        weigh(3, space[:, 1, :])
+        flip(2)
+        turn_flipped(2)
+        turn_weighted(2)
+        flip(3)
+        turn_flipped(3)
+        group_x(4)
+        group_x(5)
+        hinge(2)
+        hinge(3, "x_raw2")
+        gradient(0)
+        score(4)
+        gradient(1)
+        score(5)
+        quantize_h(0)
+        quantize_h(1)
+        product(0)
+        product(1)
 
-        for k in (1, 2):
-            a, b = PAIR * k, PAIR * k + 1
-            if k == 1:
-                weigh(a, on_first_x([P, 1, N], F32, "weighted_run%d" % a, 1)[:, 0, :])
-                flip_space(k)
-            else:
-                weigh(a, weigh_space(a, "h_grouped%d" % (b - 4))[:, 0, :])
-                flip_space(k, "h_grouped%d" % (a - 4))
-            halves = flip_and_turn_pair(k)
-            if k == 2:
-                store(a - 4)
-                store(b - 4)
-            quantize_x(k + 1)
-            scores(k + 1)
-            if k == 1:
-                weigh(b, weigh_space(b, "x_grouped%d" % (k + 1))[:, 0, :])
-                group_x(k + 2, "flipped_pair0")
-            else:
-                weigh(b, weigh_space(b, "flipped_pair0")[:, 0, :])
-            hinge_pair(k, halves)
-            gradient(a - 2)
-            gradient(b - 2)
-            turn_weighted(a)
-            turn_weighted(b)
-            quantize_h(a - 2)
-            quantize_h(b - 2)
-            product(a - 2)
-            product(b - 2)
+        weigh_pair(2, "h_grouped0")
+        turn_weighted(3)
+        flip(4)
+        turn_flipped(4)
+        turn_weighted(4)
+        flip(5)
+        turn_flipped(5)
+        group_x(6)
+        group_x(7)
+        store(0)
+        store(1)
+        hinge(4)
+        hinge(5)
+        gradient(2)
+        score(6)
+        gradient(3)
+        score(7)
+        quantize_h(2)
+        quantize_h(3)
+        product(2)
+        product(3)
 
-        space = weigh_space(6, "h_grouped3", PAIR)
-        weigh(6, space[:, 0, :])
-        weigh(7, space[:, 1, :])
-        flip_space(3, "h_grouped2")
+        weigh_pair(3, "h_grouped2")
+        turn_weighted(5)
         flip(6)
         turn_flipped(6)
         flip(7)
         turn_flipped(7)
         store(2)
-        copy_out(3, nc.scalar.copy, 0, HALF)
         hinge(6)
         hinge(7)
+        store(3)
         gradient(4)
         turn_weighted(6)
         gradient(5)
         turn_weighted(7)
         quantize_h(4)
-        product(4)
-        copy_out(3, nc.vector.tensor_copy, HALF, HALF)
-        send(3)
         quantize_h(5)
+        product(4)
         product(5)
+        gradient(6)
         store(4)
         store(5)
-        gradient(6)
         gradient(7, 0, HALF)
         quantize_h(6)
         product(6)
-        store(6)
         gradient(7, HALF, HALF)
         quantize_h(7, calls=2)
         product(7)
+        copy_out(6, nc.vector.tensor_copy)
+        send(6)
         for first in (0, HALF):
             copy_out(7, nc.vector.tensor_copy, first, HALF)
             send(7, first, HALF)

@@ -366,10 +366,7 @@ def tile_attend_gsqh_x_ts_kernel(tc, xT, wT, y, wt, ts, offs, out):
         weighted[0] = sbuf([P, N], F32, "weighted0")[:]
         nc.scalar.activation(as_dealt(weighted[0]), labels(0), ACT.Copy, scale=wt_minus[:, 0:1])
         weigh(1, sbuf([P, N], F32, "weighted1", "w_unsigned2")[:])
-        flip(0)
-        turn_flipped(0)
-        flip(1)
-        turn_flipped(1)
+        halves = flip_and_turn_pair(0)
         group_x(2)
         group_x(3)
         score(2)
@@ -378,20 +375,15 @@ def tile_attend_gsqh_x_ts_kernel(tc, xT, wT, y, wt, ts, offs, out):
         quantize_w2(EARLY, w_late)
         turn_weighted(0)
         turn_weighted(1)
-        hinge(0)
-        hinge(1, "x_raw1")
+        hinge_pair(0, halves)
         space = on_first_x([P, PAIR, N], F32, "weighted_pair1", 2048)
         weigh(2, space[:, 0, :])
         weigh(3, space[:, 1, :])
-        flip(2)
-        turn_flipped(2)
+        halves = flip_and_turn_pair(1)
         turn_weighted(2)
-        flip(3)
-        turn_flipped(3)
         group_x(4)
         group_x(5)
-        hinge(2)
-        hinge(3, "x_raw2")
+        hinge_pair(1, halves)
         gradient(0)
         score(4)
         gradient(1)
@@ -403,17 +395,13 @@ def tile_attend_gsqh_x_ts_kernel(tc, xT, wT, y, wt, ts, offs, out):
 
         weigh_pair(2, "h_grouped0")
         turn_weighted(3)
-        flip(4)
-        turn_flipped(4)
+        halves = flip_and_turn_pair(2)
         turn_weighted(4)
-        flip(5)
-        turn_flipped(5)
         group_x(6)
         group_x(7)
         store(0)
         store(1)
-        hinge(4)
-        hinge(5)
+        hinge_pair(2, halves)
         gradient(2)
         score(6)
         gradient(3)
@@ -447,11 +435,10 @@ def tile_attend_gsqh_x_ts_kernel(tc, xT, wT, y, wt, ts, offs, out):
         gradient(7, 0, HALF)
         quantize_h(6)
         product(6)
+        store(6)
         gradient(7, HALF, HALF)
         quantize_h(7, calls=2)
         product(7)
-        copy_out(6, nc.vector.tensor_copy)
-        send(6)
         for first in (0, HALF):
             copy_out(7, nc.vector.tensor_copy, first, HALF)
             send(7, first, HALF)

@@ -357,7 +357,6 @@ def tile_attend_gsqh_x_ts_kernel(tc, xT, wT, y, wt, ts, offs, out):
         group_x(1)
         score(0)
         score(1)
-        score_pass(bank(FLIP_BANKS[0], [P, N], F32, "unread0"), 1)
         copy_late(PACK - 1, on_first_x([P, P, PACK], BF16, "w_unsigned3", 4096))
         w2_codes = on_first_x([P, D], U32, "w2_codes", 0)
         quantize_w2(0, w_early)

@@ -20,6 +20,7 @@ SCORE_BANKS = (0, 1, 0, 1, 4, 5, 0, 1)
 FLIP_BANKS = (6, 7, 6, 7, 6, 7, 6, 0)
 WEIGHT_BANKS = (4, 5, 0, 1, 4, 5, 1, 4)
 SUM_BANKS = (2, 3, 2, 3, 5, 7, 6, 0)
+LAST_BANKS = {6: (6, 2), 7: (0, 3)}
 TABLE_BANKS = (6, 7, 2, 3)
 
 FLOPS = 2 * 2 * R * N * D
@@ -133,7 +134,7 @@ def tile_attend_gsqh_x_ts_kernel(tc, xT, wT, y, wt, ts, offs, out):
 
         w_by_d = sbuf([P, N, PACK], BF16, "w_by_d")
         w_listed = w_by_d[:].rearrange("p (t g j) f -> p f g t j", t=PACK, j=RUN)
-        w_early = sbuf([P, EARLY, P, PACK], BF16, "w_early")
+        w_early = sbuf([P, 2, EARLY, HALF, PACK], BF16, "w_early")
         w_turned = {}
         w_unsigned = {}
 
@@ -145,7 +146,10 @@ def tile_attend_gsqh_x_ts_kernel(tc, xT, wT, y, wt, ts, offs, out):
         def sign_early(f):
             for t in range(PACK):
                 nc.scalar.activation(
-                    w_early[:, f, :, t], w_turned[f][:, t, :], ACT.Copy, scale=ts_sign[:, t : t + 1]
+                    w_early[:, :, f, :, t],
+                    w_turned[f][:, t, :].rearrange("s (h q) -> s h q", h=2),
+                    ACT.Copy,
+                    scale=ts_sign[:, t : t + 1],
                 )
 
         def copy_late(f, space):
@@ -154,9 +158,9 @@ def tile_attend_gsqh_x_ts_kernel(tc, xT, wT, y, wt, ts, offs, out):
 
         def sign_late(f):
             nc.vector.tensor_tensor(
-                w_late[:, f - EARLY],
-                w_unsigned[f][:],
-                ts_sign_bf16[:].unsqueeze(1).to_broadcast([P, P, PACK]),
+                w_late[:, :, f - EARLY],
+                w_unsigned[f][:].rearrange("s (h q) t -> s h q t", h=2),
+                ts_sign_bf16[:].unsqueeze(1).unsqueeze(1).to_broadcast([P, 2, HALF, PACK]),
                 MULT,
             )
 
@@ -173,12 +177,13 @@ def tile_attend_gsqh_x_ts_kernel(tc, xT, wT, y, wt, ts, offs, out):
         w2_scales = sbuf([P, D], U8, "w2_scales")
 
         def quantize_w2(first_plane, planes):
-            columns = slice(first_plane * P, (first_plane + 2) * P)
-            nc.vector.quantize_mx(
-                out=w2_codes[:, columns].bitcast(E4M3),
-                scales=w2_scales[:, columns],
-                in_=planes[:].rearrange("s f p t -> s (f p t)"),
-            )
+            for h in range(2):
+                first = h * D // 2 + first_plane * HALF
+                nc.vector.quantize_mx(
+                    out=w2_codes[:, first : first + P].bitcast(E4M3),
+                    scales=w2_scales[:, first : first + P],
+                    in_=planes[:, h].rearrange("s f q t -> s (f q t)"),
+                )
 
         x_scales = sbuf([P, R], U8, "x_scales")
         h_scales = sbuf([P, R], U8, "h_scales")
@@ -333,13 +338,45 @@ def tile_attend_gsqh_x_ts_kernel(tc, xT, wT, y, wt, ts, offs, out):
                 stop=True,
             )
 
+        def half_product(b, h):
+            features = slice(h * D // 2, (h + 1) * D // 2)
+            sums[b, h] = bank(LAST_BANKS[b][h], [P, D // 2], F32, "sums%d_%d" % (b, h))
+            nc.tensor.matmul_mx(
+                out=sums[b, h][:],
+                lhsT=h_codes[b][:].bitcast(E5M2),
+                lhsT_scale=h_scales[:, columns_of(b)],
+                rhs=w2_codes[:, features].bitcast(E4M3),
+                rhs_scale=w2_scales[:, features],
+                start=True,
+                stop=True,
+            )
+
+        def copy_half(b, h, copy):
+            features = slice(h * D // 2, (h + 1) * D // 2)
+            if h == 0:
+                results[b] = sbuf([P, D], F32, "result%d" % b)
+            copy(
+                results[b][:, features].rearrange("r (q f) -> r q f", f=PACK),
+                sums[b, h][:].rearrange("r (f q) -> r q f", f=PACK),
+            )
+
         def copy_out(b, copy, first=0, count=P, reuse=None):
             if first == 0:
                 results[b] = sbuf([P, D], F32, "result%d" % b, reuse)
             copy(
-                results[b][:, first * PACK : (first + count) * PACK].rearrange("r (p f) -> r p f", f=PACK),
-                sums[b][:].rearrange("r (f p) -> r p f", f=PACK)[:, first : first + count, :],
+                results[b][:].rearrange("r (h q f) -> r h q f", h=2, f=PACK),
+                sums[b][:].rearrange("r (h f q) -> r h q f", h=2, f=PACK),
             )
+
+        def store_in_halves(b, copy):
+            for h in range(2):
+                features = slice(h * D // 2, (h + 1) * D // 2)
+                half_result = sbuf([P, D // 2], F32, "result%d_%d" % (b, h))
+                copy(
+                    half_result[:].rearrange("r (q f) -> r q f", f=PACK),
+                    sums[b][:, features].rearrange("r (f q) -> r q f", f=PACK),
+                )
+                nc.sync.dma_start(out_rows[b][:, features], half_result[:])
 
         def send(b, first=0, count=P):
             features = slice(first * PACK, (first + count) * PACK)
@@ -360,7 +397,7 @@ def tile_attend_gsqh_x_ts_kernel(tc, xT, wT, y, wt, ts, offs, out):
         copy_late(PACK - 1, on_first_x([P, P, PACK], BF16, "w_unsigned3", 4096))
         w2_codes = on_first_x([P, D], U32, "w2_codes", 0)
         quantize_w2(0, w_early)
-        w_late = on_first_x([P, PACK - EARLY, P, PACK], BF16, "w_late", 2048)
+        w_late = on_first_x([P, 2, PACK - EARLY, HALF, PACK], BF16, "w_late", 2048)
         sign_late(EARLY)
         weighted[0] = sbuf([P, N], F32, "weighted0")[:]
         nc.scalar.activation(as_dealt(weighted[0]), labels(0), ACT.Copy, scale=wt_minus[:, 0:1])
@@ -433,11 +470,15 @@ def tile_attend_gsqh_x_ts_kernel(tc, xT, wT, y, wt, ts, offs, out):
         store(5)
         gradient(7, 0, HALF)
         quantize_h(6)
-        product(6)
-        store(6)
+        half_product(6, 0)
+        half_product(6, 1)
+        copy_half(6, 0, nc.scalar.copy)
         gradient(7, HALF, HALF)
         quantize_h(7, calls=2)
-        product(7)
-        for first in (0, HALF):
-            copy_out(7, nc.vector.tensor_copy, first, HALF)
-            send(7, first, HALF)
+        half_product(7, 0)
+        half_product(7, 1)
+        copy_half(6, 1, nc.vector.tensor_copy)
+        send(6)
+        copy_half(7, 0, nc.vector.tensor_copy)
+        copy_half(7, 1, nc.scalar.copy)
+        send(7)

@@ -19,9 +19,11 @@ H_WALK = 2
 SCORE_BANKS = (0, 1, 0, 1, 4, 5, 0, 1)
 FLIP_BANKS = (6, 7, 6, 7, 6, 7, 6, 0)
 WEIGHT_BANKS = (4, 5, 0, 1, 4, 5, 1, 4)
-SUM_BANKS = (2, 3, 2, 3, 5, 7, 6, 0)
-LAST_BANKS = {6: (6, 2), 7: (0, 3)}
+SUM_BANKS = (2, 3, 2, 3, 5, 7)
+HALF_SUM_BANKS = {6: (6, 2), 7: (0, 3)}
 TABLE_BANKS = (6, 7, 2, 3)
+
+W2_CODES_AT, FIRST_X_AT, W_LATE_AT, LAST_PLANE_AT = 0, 1024, 2048, 4096
 
 FLOPS = 2 * 2 * R * N * D
 BYTES = 4 * (D * R + D * T + R * N + R + T + R * D) + 2 * P * (N // 16)
@@ -43,7 +45,6 @@ def tile_attend_gsqh_x_ts_kernel(tc, xT, wT, y, wt, ts, offs, out):
     with ExitStack() as ctx:
         keep = ctx.enter_context(tc.tile_pool(name="keep", bufs=1))
         opening = ctx.enter_context(tc.tile_pool(name="opening", bufs=1))
-        shared = ctx.enter_context(tc.tile_pool(name="shared", bufs=1))
         psum = ctx.enter_context(tc.psum_pool(name="psum", bufs=1))
 
         def sbuf(shape, dtype, name, reuse=None):
@@ -51,9 +52,6 @@ def tile_attend_gsqh_x_ts_kernel(tc, xT, wT, y, wt, ts, offs, out):
 
         def on_first_x(shape, dtype, name, offset):
             return opening.tile(shape, dtype, name=name, offset=offset, align_bytes=64)
-
-        def placed(shape, dtype, name, offset):
-            return shared.tile(shape, dtype, name=name, offset=offset, align_bytes=64)
 
         def bank(index, shape, dtype, name):
             return psum.tile(shape, dtype, name=name, tag="bank%d" % index)
@@ -81,21 +79,14 @@ def tile_attend_gsqh_x_ts_kernel(tc, xT, wT, y, wt, ts, offs, out):
         out_rows = out[0].rearrange("(b p) d -> b p d", p=P)
         x_raw = {}
         y_raw = {}
-
-        def load_x(k):
+        for k in range(CHUNKS):
             if k == 0:
-                x_raw[k] = on_first_x([P, PACK, CHUNK_ROWS], F32, "x_raw0", 1024)
+                x_raw[k] = on_first_x([P, PACK, CHUNK_ROWS], F32, "x_raw0", FIRST_X_AT)
             else:
                 x_raw[k] = sbuf([P, PACK, CHUNK_ROWS], F32, "x_raw%d" % k)
             nc.sync.dma_start(x_raw[k][:], x_rows[:, :, k * CHUNK_ROWS : (k + 1) * CHUNK_ROWS])
-
-        def load_y(k):
             y_raw[k] = sbuf([P, PAIR, N], F32, "y_raw%d" % k)
             nc.sync.dma_start(y_raw[k][:], y_rows[k])
-
-        for k in range(CHUNKS):
-            load_x(k)
-            load_y(k)
 
         ident_f32 = sbuf([P, P], F32, "ident_f32")
         make_identity(nc, ident_f32[:])
@@ -200,30 +191,29 @@ def tile_attend_gsqh_x_ts_kernel(tc, xT, wT, y, wt, ts, offs, out):
         sums = {}
         results = {}
 
-        def columns_of(b, count=1):
-            return slice(b * P, (b + count) * P)
+        def columns_of(b):
+            return slice(b * P, (b + 1) * P)
 
-        def group_x(b, reuse=None):
-            x_grouped[b] = sbuf([P, P, PACK], BF16, "x_grouped%d" % b, reuse)
+        def features_of(h):
+            return slice(h * D // 2, (h + 1) * D // 2)
+
+        def group_x(b):
+            x_grouped[b] = sbuf([P, P, PACK], BF16, "x_grouped%d" % b)
             nc.scalar.copy(
                 x_grouped[b][:].rearrange("p (c i) f -> p c f i", i=X_WALK),
                 x_raw[b // PAIR][:, :, columns_of(b % PAIR)].rearrange("p f (c i) -> p c f i", i=X_WALK),
             )
 
-        def group_x_on_gpsimd(b, space):
-            x_grouped[b] = space
-            nc.gpsimd.tensor_scalar(
-                space[:],
-                x_raw[b // PAIR][:, :, columns_of(b % PAIR)].rearrange("p f r -> p r f"),
-                1.0,
-                0.0,
-                MULT,
-                ADD,
+        def score(b):
+            x_codes[b] = sbuf([P, P], U32, "x_codes%d" % b)
+            nc.vector.quantize_mx(
+                out=x_codes[b][:].bitcast(E4M3),
+                scales=x_scales[:, columns_of(b)],
+                in_=x_grouped[b][:].rearrange("p r f -> p (r f)"),
             )
-
-        def score_pass(target, b):
+            raw[b] = bank(SCORE_BANKS[b], [P, N], F32, "raw%d" % b)
             nc.tensor.matmul_mx(
-                out=target[:],
+                out=raw[b][:],
                 lhsT=x_codes[b][:].bitcast(E4M3),
                 lhsT_scale=x_scales[:, columns_of(b)],
                 rhs=w1_codes[:].bitcast(E4M3),
@@ -231,16 +221,6 @@ def tile_attend_gsqh_x_ts_kernel(tc, xT, wT, y, wt, ts, offs, out):
                 start=True,
                 stop=True,
             )
-
-        def score(b, reuse=None):
-            x_codes[b] = sbuf([P, P], U32, "x_codes%d" % b, reuse)
-            nc.vector.quantize_mx(
-                out=x_codes[b][:].bitcast(E4M3),
-                scales=x_scales[:, columns_of(b)],
-                in_=x_grouped[b][:].rearrange("p r f -> p (r f)"),
-            )
-            raw[b] = bank(SCORE_BANKS[b], [P, N], F32, "raw%d" % b)
-            score_pass(raw[b], b)
 
         def labels(b):
             return dealt(y_raw[b // PAIR][:, b % PAIR, :])
@@ -251,8 +231,8 @@ def tile_attend_gsqh_x_ts_kernel(tc, xT, wT, y, wt, ts, offs, out):
                 nc.tensor.transpose(turned[:, t, :], source[:, t * P : (t + 1) * P], ident_f32[:])
             return turned
 
-        def flip(b, reuse=None):
-            flipped[b] = sbuf([P, N], F32, "flipped%d" % b, reuse)[:]
+        def flip(b):
+            flipped[b] = sbuf([P, N], F32, "flipped%d" % b)[:]
             nc.vector.tensor_tensor(as_dealt(flipped[b]), labels(b), as_dealt(raw[b][:]), MULT)
 
         def relu(target, source, t):
@@ -263,8 +243,8 @@ def tile_attend_gsqh_x_ts_kernel(tc, xT, wT, y, wt, ts, offs, out):
         def turn_flipped(b):
             flipped_turned[b] = turn(FLIP_BANKS[b], "flipped_turned%d" % b, flipped[b])
 
-        def hinge(b, reuse=None):
-            slack[b] = sbuf([P, PACK, P], F32, "slack%d" % b, reuse)[:]
+        def hinge(b):
+            slack[b] = sbuf([P, PACK, P], F32, "slack%d" % b)[:]
             for t in range(PACK):
                 relu(slack[b][:, t, :], flipped_turned[b][:, t, :], t)
 
@@ -284,8 +264,8 @@ def tile_attend_gsqh_x_ts_kernel(tc, xT, wT, y, wt, ts, offs, out):
                     )
             return halves
 
-        def hinge_pair(k, halves, reuse=None):
-            both = sbuf([P, PACK, CHUNK_ROWS], F32, "slack_pair%d" % k, reuse)
+        def hinge_pair(k, halves):
+            both = sbuf([P, PACK, CHUNK_ROWS], F32, "slack_pair%d" % k)
             for t in range(PACK):
                 relu(both[:, t, :], halves[t // 2][:, t % 2, :], t)
             for j in range(PAIR):
@@ -295,18 +275,15 @@ def tile_attend_gsqh_x_ts_kernel(tc, xT, wT, y, wt, ts, offs, out):
             weighted[b] = space
             nc.gpsimd.tensor_scalar(as_dealt(space), labels(b), wt_minus[:, b : b + 1], 0.0, MULT, ADD)
 
-        def weigh_pair(k, reuse):
-            space = sbuf([P, PAIR, N], F32, "weighted_pair%d" % k, reuse)
+        def weigh_pair(k, space):
             for j in range(PAIR):
                 weigh(PAIR * k + j, space[:, j, :])
 
         def turn_weighted(b):
             weighted_turned[b] = turn(WEIGHT_BANKS[b], "weighted_turned%d" % b, weighted[b])
 
-        def gradient(b, first=0, count=P, space=None):
-            if space is not None:
-                h_grouped[b] = space
-            elif first == 0:
+        def gradient(b, first=0, count=P):
+            if first == 0:
                 h_grouped[b] = sbuf([P, P, PACK], BF16, "h_grouped%d" % b)
             rows = slice(first, first + count)
             nc.vector.tensor_tensor(
@@ -316,8 +293,8 @@ def tile_attend_gsqh_x_ts_kernel(tc, xT, wT, y, wt, ts, offs, out):
                 MULT,
             )
 
-        def quantize_h(b, calls=1, reuse=None):
-            h_codes[b] = sbuf([P, P], U32, "h_codes%d" % b, reuse)
+        def quantize_h(b, calls=1):
+            h_codes[b] = sbuf([P, P], U32, "h_codes%d" % b)
             count = P // calls
             for first in range(0, P, count):
                 nc.vector.quantize_mx(
@@ -326,23 +303,9 @@ def tile_attend_gsqh_x_ts_kernel(tc, xT, wT, y, wt, ts, offs, out):
                     in_=h_grouped[b][:, first : first + count, :].rearrange("s r t -> s (r t)"),
                 )
 
-        def product(b):
-            sums[b] = bank(SUM_BANKS[b], [P, D], F32, "sums%d" % b)
+        def product_pass(target, b, features):
             nc.tensor.matmul_mx(
-                out=sums[b][:],
-                lhsT=h_codes[b][:].bitcast(E5M2),
-                lhsT_scale=h_scales[:, columns_of(b)],
-                rhs=w2_codes[:].bitcast(E4M3),
-                rhs_scale=w2_scales[:],
-                start=True,
-                stop=True,
-            )
-
-        def half_product(b, h):
-            features = slice(h * D // 2, (h + 1) * D // 2)
-            sums[b, h] = bank(LAST_BANKS[b][h], [P, D // 2], F32, "sums%d_%d" % (b, h))
-            nc.tensor.matmul_mx(
-                out=sums[b, h][:],
+                out=target[:],
                 lhsT=h_codes[b][:].bitcast(E5M2),
                 lhsT_scale=h_scales[:, columns_of(b)],
                 rhs=w2_codes[:, features].bitcast(E4M3),
@@ -351,40 +314,30 @@ def tile_attend_gsqh_x_ts_kernel(tc, xT, wT, y, wt, ts, offs, out):
                 stop=True,
             )
 
-        def copy_half(b, h, copy):
-            features = slice(h * D // 2, (h + 1) * D // 2)
-            if h == 0:
-                results[b] = sbuf([P, D], F32, "result%d" % b)
-            copy(
-                results[b][:, features].rearrange("r (q f) -> r q f", f=PACK),
-                sums[b, h][:].rearrange("r (f q) -> r q f", f=PACK),
-            )
+        def product(b):
+            sums[b] = bank(SUM_BANKS[b], [P, D], F32, "sums%d" % b)
+            product_pass(sums[b], b, slice(0, D))
 
-        def copy_out(b, copy, first=0, count=P, reuse=None):
-            if first == 0:
-                results[b] = sbuf([P, D], F32, "result%d" % b, reuse)
-            copy(
+        def store(b):
+            results[b] = sbuf([P, D], F32, "result%d" % b)
+            nc.scalar.copy(
                 results[b][:].rearrange("r (h q f) -> r h q f", h=2, f=PACK),
                 sums[b][:].rearrange("r (h f q) -> r h q f", h=2, f=PACK),
             )
+            nc.sync.dma_start(out_rows[b], results[b][:])
 
-        def store_in_halves(b, copy):
+        def product_in_halves(b):
             for h in range(2):
-                features = slice(h * D // 2, (h + 1) * D // 2)
-                half_result = sbuf([P, D // 2], F32, "result%d_%d" % (b, h))
-                copy(
-                    half_result[:].rearrange("r (q f) -> r q f", f=PACK),
-                    sums[b][:, features].rearrange("r (f q) -> r q f", f=PACK),
-                )
-                nc.sync.dma_start(out_rows[b][:, features], half_result[:])
+                sums[b, h] = bank(HALF_SUM_BANKS[b][h], [P, D // 2], F32, "sums%d_%d" % (b, h))
+                product_pass(sums[b, h], b, features_of(h))
 
-        def send(b, first=0, count=P):
-            features = slice(first * PACK, (first + count) * PACK)
-            nc.sync.dma_start(out_rows[b][:, features], results[b][:, features])
-
-        def store(b, reuse=None):
-            copy_out(b, nc.scalar.copy, reuse=reuse)
-            send(b)
+        def copy_half(b, h, copy):
+            if h == 0:
+                results[b] = sbuf([P, D], F32, "result%d" % b)
+            copy(
+                results[b][:, features_of(h)].rearrange("r (q f) -> r q f", f=PACK),
+                sums[b, h][:].rearrange("r (f q) -> r q f", f=PACK),
+            )
 
         nc.vector.quantize_mx(
             out=w1_codes[:].bitcast(E4M3), scales=w1_scales[:], in_=w_by_d[:].rearrange("p i f -> p (i f)")
@@ -394,10 +347,10 @@ def tile_attend_gsqh_x_ts_kernel(tc, xT, wT, y, wt, ts, offs, out):
         group_x(1)
         score(0)
         score(1)
-        copy_late(PACK - 1, on_first_x([P, P, PACK], BF16, "w_unsigned3", 4096))
-        w2_codes = on_first_x([P, D], U32, "w2_codes", 0)
+        copy_late(PACK - 1, on_first_x([P, P, PACK], BF16, "w_unsigned3", LAST_PLANE_AT))
+        w2_codes = on_first_x([P, D], U32, "w2_codes", W2_CODES_AT)
         quantize_w2(0, w_early)
-        w_late = on_first_x([P, 2, PACK - EARLY, HALF, PACK], BF16, "w_late", 2048)
+        w_late = on_first_x([P, 2, PACK - EARLY, HALF, PACK], BF16, "w_late", W_LATE_AT)
         sign_late(EARLY)
         weighted[0] = sbuf([P, N], F32, "weighted0")[:]
         nc.scalar.activation(as_dealt(weighted[0]), labels(0), ACT.Copy, scale=wt_minus[:, 0:1])
@@ -412,55 +365,43 @@ def tile_attend_gsqh_x_ts_kernel(tc, xT, wT, y, wt, ts, offs, out):
         turn_weighted(0)
         turn_weighted(1)
         hinge_pair(0, halves)
-        space = on_first_x([P, PAIR, N], F32, "weighted_pair1", 2048)
-        weigh(2, space[:, 0, :])
-        weigh(3, space[:, 1, :])
-        halves = flip_and_turn_pair(1)
-        turn_weighted(2)
-        group_x(4)
-        group_x(5)
-        hinge_pair(1, halves)
-        gradient(0)
-        score(4)
-        gradient(1)
-        score(5)
-        quantize_h(0)
-        quantize_h(1)
-        product(0)
-        product(1)
 
-        weigh_pair(2, "h_grouped0")
-        turn_weighted(3)
-        halves = flip_and_turn_pair(2)
-        turn_weighted(4)
-        group_x(6)
-        group_x(7)
-        store(0)
-        store(1)
-        hinge_pair(2, halves)
-        gradient(2)
-        score(6)
-        gradient(3)
-        score(7)
-        quantize_h(2)
-        quantize_h(3)
-        product(2)
-        product(3)
+        for k in (1, 2):
+            first, second = PAIR * k, PAIR * k + 1
+            if k == 1:
+                weigh_pair(k, on_first_x([P, PAIR, N], F32, "weighted_pair1", W_LATE_AT))
+            else:
+                weigh_pair(k, sbuf([P, PAIR, N], F32, "weighted_pair2", "x_grouped5"))
+                turn_weighted(second - PAIR)
+            halves = flip_and_turn_pair(k)
+            turn_weighted(first)
+            group_x(first + PAIR)
+            group_x(second + PAIR)
+            if k == 2:
+                store(0)
+                store(1)
+            hinge_pair(k, halves)
+            gradient(first - PAIR)
+            score(first + PAIR)
+            gradient(second - PAIR)
+            score(second + PAIR)
+            quantize_h(first - PAIR)
+            quantize_h(second - PAIR)
+            product(first - PAIR)
+            product(second - PAIR)
 
-        weigh_pair(3, "h_grouped2")
+        weigh_pair(3, sbuf([P, PAIR, N], F32, "weighted_pair3", "x_grouped7"))
         turn_weighted(5)
-        flip(6)
-        turn_flipped(6)
-        flip(7)
-        turn_flipped(7)
+        for b in (6, 7):
+            flip(b)
+            turn_flipped(b)
         store(2)
         hinge(6)
         hinge(7)
         store(3)
-        gradient(4)
-        turn_weighted(6)
-        gradient(5)
-        turn_weighted(7)
+        for b in (4, 5):
+            gradient(b)
+            turn_weighted(b + PAIR)
         quantize_h(4)
         quantize_h(5)
         product(4)
@@ -470,15 +411,13 @@ def tile_attend_gsqh_x_ts_kernel(tc, xT, wT, y, wt, ts, offs, out):
         store(5)
         gradient(7, 0, HALF)
         quantize_h(6)
-        half_product(6, 0)
-        half_product(6, 1)
+        product_in_halves(6)
         copy_half(6, 0, nc.scalar.copy)
         gradient(7, HALF, HALF)
         quantize_h(7, calls=2)
-        half_product(7, 0)
-        half_product(7, 1)
+        product_in_halves(7)
         copy_half(6, 1, nc.vector.tensor_copy)
-        send(6)
+        nc.sync.dma_start(out_rows[6], results[6][:])
         copy_half(7, 0, nc.vector.tensor_copy)
         copy_half(7, 1, nc.scalar.copy)
-        send(7)
+        nc.sync.dma_start(out_rows[7], results[7][:])

from contextlib import ExitStack

import concourse.mybir as mybir
from concourse.masks import make_identity

D, T, N, R = 512, 2048, 512, 1024
P = 128
HALF = P // 2
PACK = 4
RUN = 8
CHUNK_ROWS = 256
PAIR = CHUNK_ROWS // P
CHUNKS = R // CHUNK_ROWS
BLOCKS = R // P
EARLY = 2
X_WALK = 4
H_WALK = 2

SCORE_BANKS = (0, 1, 0, 1, 4, 5, 0, 1)
FLIP_BANKS = (6, 7, 6, 7, 6, 7, 6, 0)
WEIGHT_BANKS = (4, 5, 0, 1, 4, 5, 1, 4)
SUM_BANKS = (2, 3, 2, 3, 5, 7)
HALF_SUM_BANKS = {6: (6, 2), 7: (0, 3)}
TABLE_BANKS = (6, 7, 2, 3)

W2_CODES_AT, FIRST_X_AT, W_LATE_AT, LAST_PLANE_AT = 0, 1024, 2048, 4096

FLOPS = 2 * 2 * R * N * D
BYTES = 4 * (D * R + D * T + R * N + R + T + R * D) + 2 * P * (N // 16)

F32 = mybir.dt.float32
BF16 = mybir.dt.bfloat16
U32 = mybir.dt.uint32
U16 = mybir.dt.uint16
U8 = mybir.dt.uint8
E4M3 = mybir.dt.float8_e4m3fn_x4
E5M2 = mybir.dt.float8_e5m2_x4
MULT = mybir.AluOpType.mult
ADD = mybir.AluOpType.add
ACT = mybir.ActivationFunctionType


def tile_attend_gsqh_x_ts_kernel(tc, xT, wT, y, wt, ts, offs, out):
    nc = tc.nc
    with ExitStack() as ctx:
        keep = ctx.enter_context(tc.tile_pool(name="keep", bufs=1))
        opening = ctx.enter_context(tc.tile_pool(name="opening", bufs=1))
        psum = ctx.enter_context(tc.psum_pool(name="psum", bufs=1))

        def sbuf(shape, dtype, name, reuse=None):
            return keep.tile(shape, dtype, name=name, tag=reuse or name, align_bytes=64)

        def on_first_x(shape, dtype, name, offset):
            return opening.tile(shape, dtype, name=name, offset=offset, align_bytes=64)

        def bank(index, shape, dtype, name):
            return psum.tile(shape, dtype, name=name, tag="bank%d" % index)

        offsets = keep.tile([P, N // 16], U16, name="offsets")
        nc.sync.dma_start(offsets[:], offs)

        wt_rows = sbuf([P, P], F32, "wt_rows")
        ts_window = sbuf([P, T], F32, "ts_window")
        nc.scalar.dma_start(ts_window[P - 1 : P, :], ts[0:1, :])
        nc.vector.memset(wt_rows[0 : P - BLOCKS, :], 0.0)
        nc.vector.memset(ts_window[0 : P - 1, :], 0.0)

        w_rows = wT.rearrange("(p f) c -> p f c", f=PACK)
        w_planes = []
        for f in range(PACK):
            plane = sbuf([P, T], F32, "w_plane%d" % f)
            nc.sync.dma_start(plane[:], w_rows[:, f, :])
            w_planes.append(plane)
            if f == 0:
                nc.scalar.dma_start(wt_rows[P - BLOCKS : P, :], wt[0].rearrange("(b r) o -> b (r o)", r=P))

        x_rows = xT[0].rearrange("(p f) r -> p f r", f=PACK)
        y_rows = y[0].rearrange("(k j p) i -> k p j i", p=P, j=PAIR)
        out_rows = out[0].rearrange("(b p) d -> b p d", p=P)
        x_raw = {}
        y_raw = {}
        for k in range(CHUNKS):
            if k == 0:
                x_raw[k] = on_first_x([P, PACK, CHUNK_ROWS], F32, "x_raw0", FIRST_X_AT)
            else:
                x_raw[k] = sbuf([P, PACK, CHUNK_ROWS], F32, "x_raw%d" % k)
            nc.sync.dma_start(x_raw[k][:], x_rows[:, :, k * CHUNK_ROWS : (k + 1) * CHUNK_ROWS])
            y_raw[k] = sbuf([P, PAIR, N], F32, "y_raw%d" % k)
            nc.sync.dma_start(y_raw[k][:], y_rows[k])

        ident_f32 = sbuf([P, P], F32, "ident_f32")
        make_identity(nc, ident_f32[:])
        ident_bf16 = sbuf([P, P], BF16, "ident_bf16")
        make_identity(nc, ident_bf16[:])

        def dealt(slots):
            return slots.rearrange("p (g t j) -> p t g j", t=PACK, j=RUN)

        def as_dealt(slots):
            return slots.rearrange("p (t g j) -> p t g j", t=PACK, j=RUN)

        wt_turned = bank(4, [P, P], F32, "wt_turned")
        nc.tensor.transpose(wt_turned[:], wt_rows[:], ident_f32[:])
        wt_minus = sbuf([P, BLOCKS], F32, "wt_minus")
        nc.scalar.activation(wt_minus[:], wt_turned[:, P - BLOCKS : P], ACT.Copy, scale=-1.0)

        ts_listed = sbuf([P, N], F32, "ts_listed")
        nc.vector.tensor_copy(ts_listed[:], ts_window[:].indirect(offsets[:]))
        ts_dealt = sbuf([P, N], F32, "ts_dealt")
        nc.scalar.copy(as_dealt(ts_dealt[:]), dealt(ts_listed[:]))
        ts_turned = bank(5, [P, PACK, P], F32, "ts_turned")
        for t in range(PACK):
            nc.tensor.transpose(ts_turned[:, t, :], ts_dealt[:, t * P : (t + 1) * P], ident_f32[:])
        ts_by_place = ts_turned[:, :, P - 1]
        ts_size = sbuf([P, PACK], F32, "ts_size")
        ts_sign = sbuf([P, PACK], F32, "ts_sign")
        ts_minus = sbuf([P, PACK], F32, "ts_minus")
        ts_slope = sbuf([P, PACK], F32, "ts_slope")
        nc.scalar.activation(ts_sign[:], ts_by_place, ACT.Sign)
        ts_sign_bf16 = sbuf([P, PACK], BF16, "ts_sign_bf16")
        nc.scalar.activation(ts_sign_bf16[:], ts_by_place, ACT.Sign)
        nc.scalar.activation(ts_size[:], ts_by_place, ACT.Abs)
        nc.scalar.activation(ts_minus[:], ts_by_place, ACT.Copy, scale=-1.0)
        nc.gpsimd.tensor_tensor(ts_slope[:], ts_minus[:], ts_size[:], MULT)

        w_by_d = sbuf([P, N, PACK], BF16, "w_by_d")
        w_listed = w_by_d[:].rearrange("p (t g j) f -> p f g t j", t=PACK, j=RUN)
        w_early = sbuf([P, 2, EARLY, HALF, PACK], BF16, "w_early")
        w_turned = {}
        w_unsigned = {}

        def turn_w(f):
            w_turned[f] = bank(TABLE_BANKS[f], [P, PACK, P], BF16, "w_turned%d" % f)
            for t in range(PACK):
                nc.tensor.transpose(w_turned[f][:, t, :], w_by_d[:, t * P : (t + 1) * P, f], ident_bf16[:])

        def sign_early(f):
            for t in range(PACK):
                nc.scalar.activation(
                    w_early[:, :, f, :, t],
                    w_turned[f][:, t, :].rearrange("s (h q) -> s h q", h=2),
                    ACT.Copy,
                    scale=ts_sign[:, t : t + 1],
                )

        def copy_late(f, space):
            w_unsigned[f] = space
            nc.scalar.copy(space[:], w_turned[f][:].rearrange("s t p -> s p t"))

        def sign_late(f):
            nc.vector.tensor_tensor(
                w_late[:, :, f - EARLY],
                w_unsigned[f][:].rearrange("s (h q) t -> s h q t", h=2),
                ts_sign_bf16[:].unsqueeze(1).unsqueeze(1).to_broadcast([P, 2, HALF, PACK]),
                MULT,
            )

        for f in range(PACK):
            nc.vector.tensor_copy(w_listed[:, f], w_planes[f][:].indirect(offsets[:]))
            if f < PACK - 1:
                turn_w(f)
            if f < EARLY:
                sign_early(f)
        copy_late(EARLY, sbuf([P, P, PACK], BF16, "w_unsigned2"))

        w1_codes = sbuf([P, N], U32, "w1_codes")
        w1_scales = sbuf([P, N], U8, "w1_scales")
        w2_scales = sbuf([P, D], U8, "w2_scales")

        def quantize_w2(first_plane, planes):
            for h in range(2):
                first = h * D // 2 + first_plane * HALF
                nc.vector.quantize_mx(
                    out=w2_codes[:, first : first + P].bitcast(E4M3),
                    scales=w2_scales[:, first : first + P],
                    in_=planes[:, h].rearrange("s f q t -> s (f q t)"),
                )

        x_scales = sbuf([P, R], U8, "x_scales")
        h_scales = sbuf([P, R], U8, "h_scales")
        x_grouped = {}
        x_codes = {}
        raw = {}
        flipped = {}
        flipped_turned = {}
        weighted = {}
        weighted_turned = {}
        slack = {}
        h_grouped = {}
        h_codes = {}
        sums = {}
        results = {}

        def columns_of(b):
            return slice(b * P, (b + 1) * P)

        def features_of(h):
            return slice(h * D // 2, (h + 1) * D // 2)

        def group_x(b):
            x_grouped[b] = sbuf([P, P, PACK], BF16, "x_grouped%d" % b)
            nc.scalar.copy(
                x_grouped[b][:].rearrange("p (c i) f -> p c f i", i=X_WALK),
                x_raw[b // PAIR][:, :, columns_of(b % PAIR)].rearrange("p f (c i) -> p c f i", i=X_WALK),
            )

        def score(b):
            x_codes[b] = sbuf([P, P], U32, "x_codes%d" % b)
            nc.vector.quantize_mx(
                out=x_codes[b][:].bitcast(E4M3),
                scales=x_scales[:, columns_of(b)],
                in_=x_grouped[b][:].rearrange("p r f -> p (r f)"),
            )
            raw[b] = bank(SCORE_BANKS[b], [P, N], F32, "raw%d" % b)
            nc.tensor.matmul_mx(
                out=raw[b][:],
                lhsT=x_codes[b][:].bitcast(E4M3),
                lhsT_scale=x_scales[:, columns_of(b)],
                rhs=w1_codes[:].bitcast(E4M3),
                rhs_scale=w1_scales[:],
                start=True,
                stop=True,
            )

        def labels(b):
            return dealt(y_raw[b // PAIR][:, b % PAIR, :])

        def turn(index, name, source):
            turned = bank(index, [P, PACK, P], F32, name)
            for t in range(PACK):
                nc.tensor.transpose(turned[:, t, :], source[:, t * P : (t + 1) * P], ident_f32[:])
            return turned

        def flip(b):
            flipped[b] = sbuf([P, N], F32, "flipped%d" % b)[:]
            nc.vector.tensor_tensor(as_dealt(flipped[b]), labels(b), as_dealt(raw[b][:]), MULT)

        def relu(target, source, t):
            nc.scalar.activation(
                target, source, ACT.Relu, bias=ts_size[:, t : t + 1], scale=ts_slope[:, t : t + 1]
            )

        def turn_flipped(b):
            flipped_turned[b] = turn(FLIP_BANKS[b], "flipped_turned%d" % b, flipped[b])

        def hinge(b):
            slack[b] = sbuf([P, PACK, P], F32, "slack%d" % b)[:]
            for t in range(PACK):
                relu(slack[b][:, t, :], flipped_turned[b][:, t, :], t)

        def flip_and_turn_pair(k):
            halves = []
            for j in range(PAIR):
                flip(PAIR * k + j)
                if j == 0:
                    for half in range(2):
                        name = "flipped_turned%d_%d" % (k, half)
                        halves.append(bank(FLIP_BANKS[PAIR * k + half], [P, 2, CHUNK_ROWS], F32, name))
                for t in range(PACK):
                    nc.tensor.transpose(
                        halves[t // 2][:, t % 2, columns_of(j)],
                        flipped[PAIR * k + j][:, t * P : (t + 1) * P],
                        ident_f32[:],
                    )
            return halves

        def hinge_pair(k, halves):
            both = sbuf([P, PACK, CHUNK_ROWS], F32, "slack_pair%d" % k)
            for t in range(PACK):
                relu(both[:, t, :], halves[t // 2][:, t % 2, :], t)
            for j in range(PAIR):
                slack[PAIR * k + j] = both[:, :, columns_of(j)]

        def weigh(b, space):
            weighted[b] = space
            nc.gpsimd.tensor_scalar(as_dealt(space), labels(b), wt_minus[:, b : b + 1], 0.0, MULT, ADD)

        def weigh_pair(k, space):
            for j in range(PAIR):
                weigh(PAIR * k + j, space[:, j, :])

        def turn_weighted(b):
            weighted_turned[b] = turn(WEIGHT_BANKS[b], "weighted_turned%d" % b, weighted[b])

        def gradient(b, first=0, count=P):
            if first == 0:
                h_grouped[b] = sbuf([P, P, PACK], BF16, "h_grouped%d" % b)
            rows = slice(first, first + count)
            nc.vector.tensor_tensor(
                h_grouped[b][:, rows, :].rearrange("s (c i) t -> s c t i", i=H_WALK),
                slack[b][:, :, rows].rearrange("s t (c i) -> s c t i", i=H_WALK),
                weighted_turned[b][:, :, rows].rearrange("s t (c i) -> s c t i", i=H_WALK),
                MULT,
            )

        def quantize_h(b, calls=1):
            h_codes[b] = sbuf([P, P], U32, "h_codes%d" % b)
            count = P // calls
            for first in range(0, P, count):
                nc.vector.quantize_mx(
                    out=h_codes[b][:, first : first + count].bitcast(E5M2),
                    scales=h_scales[:, b * P + first : b * P + first + count],
                    in_=h_grouped[b][:, first : first + count, :].rearrange("s r t -> s (r t)"),
                )

        def product_pass(target, b, features):
            nc.tensor.matmul_mx(
                out=target[:],
                lhsT=h_codes[b][:].bitcast(E5M2),
                lhsT_scale=h_scales[:, columns_of(b)],
                rhs=w2_codes[:, features].bitcast(E4M3),
                rhs_scale=w2_scales[:, features],
                start=True,
                stop=True,
            )

        def product(b):
            sums[b] = bank(SUM_BANKS[b], [P, D], F32, "sums%d" % b)
            product_pass(sums[b], b, slice(0, D))

        def store(b):
            results[b] = sbuf([P, D], F32, "result%d" % b)
            nc.scalar.copy(
                results[b][:].rearrange("r (h q f) -> r h q f", h=2, f=PACK),
                sums[b][:].rearrange("r (h f q) -> r h q f", h=2, f=PACK),
            )
            nc.sync.dma_start(out_rows[b], results[b][:])

        def product_in_halves(b):
            for h in range(2):
                sums[b, h] = bank(HALF_SUM_BANKS[b][h], [P, D // 2], F32, "sums%d_%d" % (b, h))
                product_pass(sums[b, h], b, features_of(h))

        def copy_half(b, h, copy):
            if h == 0:
                results[b] = sbuf([P, D], F32, "result%d" % b)
            copy(
                results[b][:, features_of(h)].rearrange("r (q f) -> r q f", f=PACK),
                sums[b, h][:].rearrange("r (f q) -> r q f", f=PACK),
            )

        nc.vector.quantize_mx(
            out=w1_codes[:].bitcast(E4M3), scales=w1_scales[:], in_=w_by_d[:].rearrange("p i f -> p (i f)")
        )
        turn_w(PACK - 1)
        group_x(0)
        group_x(1)
        score(0)
        score(1)
        copy_late(PACK - 1, on_first_x([P, P, PACK], BF16, "w_unsigned3", LAST_PLANE_AT))
        w2_codes = on_first_x([P, D], U32, "w2_codes", W2_CODES_AT)
        quantize_w2(0, w_early)
        w_late = on_first_x([P, 2, PACK - EARLY, HALF, PACK], BF16, "w_late", W_LATE_AT)
        sign_late(EARLY)
        weighted[0] = sbuf([P, N], F32, "weighted0")[:]
        nc.scalar.activation(as_dealt(weighted[0]), labels(0), ACT.Copy, scale=wt_minus[:, 0:1])
        weigh(1, sbuf([P, N], F32, "weighted1", "w_unsigned2")[:])
        halves = flip_and_turn_pair(0)
        group_x(2)
        group_x(3)
        score(2)
        sign_late(PACK - 1)
        score(3)
        quantize_w2(EARLY, w_late)
        turn_weighted(0)
        turn_weighted(1)
        hinge_pair(0, halves)

        for k in (1, 2):
            first, second = PAIR * k, PAIR * k + 1
            if k == 1:
                weigh_pair(k, on_first_x([P, PAIR, N], F32, "weighted_pair1", W_LATE_AT))
            else:
                weigh_pair(k, sbuf([P, PAIR, N], F32, "weighted_pair2", "x_grouped5"))
                turn_weighted(second - PAIR)
            halves = flip_and_turn_pair(k)
            turn_weighted(first)
            group_x(first + PAIR)
            group_x(second + PAIR)
            if k == 2:
                store(0)
                store(1)
            hinge_pair(k, halves)
            gradient(first - PAIR)
            score(first + PAIR)
            gradient(second - PAIR)
            score(second + PAIR)
            quantize_h(first - PAIR)
            quantize_h(second - PAIR)
            product(first - PAIR)
            product(second - PAIR)

        weigh_pair(3, sbuf([P, PAIR, N], F32, "weighted_pair3", "x_grouped7"))
        turn_weighted(5)
        for b in (6, 7):
            flip(b)
            turn_flipped(b)
        store(2)
        hinge(6)
        hinge(7)
        store(3)
        for b in (4, 5):
            gradient(b)
            turn_weighted(b + PAIR)
        quantize_h(4)
        quantize_h(5)
        product(4)
        product(5)
        gradient(6)
        store(4)
        store(5)
        gradient(7, 0, HALF)
        quantize_h(6)
        product_in_halves(6)
        copy_half(6, 0, nc.scalar.copy)
        gradient(7, HALF, HALF)
        quantize_h(7, calls=2)
        product_in_halves(7)
        copy_half(6, 1, nc.vector.tensor_copy)
        nc.sync.dma_start(out_rows[6], results[6][:])
        copy_half(7, 0, nc.vector.tensor_copy)
        copy_half(7, 1, nc.scalar.copy)
        nc.sync.dma_start(out_rows[7], results[7][:])
